import numpy as np, ml_dtypes
CORES = [10,34,74,98]
N = 4
import mx_ref
BF = ml_dtypes.bfloat16
def entries(a):
    return np.ascontiguousarray(a.T).reshape(-1)
def table(e):
    return np.ascontiguousarray(np.reshape(e, (-1, 16)).T).astype(np.int32)
def pick(q, e):
    c = np.concatenate([q[0].reshape(128, -1, 4), np.zeros((128, 1, 4), np.uint8)], axis=1); s = np.concatenate([q[1], np.ones((16, 1), np.uint8)], axis=1)
    return (np.ascontiguousarray(c[:, e].reshape(128, -1)), np.ascontiguousarray(s[:, e]))
def join(*qs):
    return (np.concatenate([q[0] for q in qs], axis=1), np.concatenate([q[1] for q in qs], axis=1))
def put(q, e, v):
    c, s = q[0].reshape(128, -1, 4).copy(), q[1].copy(); c[:, e] = v[0].reshape(128, -1, 4); s[:, e] = v[1]
    return (c.reshape(128, -1), s)
def pk(c, s):
    return (np.ascontiguousarray(c), mx_ref.live(s))
def emit(q):
    return q[0], q[1]
def decode(q):
    o = []
    for b in range(4):
        e = np.zeros((128, 128, 4), np.float32); e[np.arange(128), np.arange(128), b] = 1
        o.append(mx_ref.matmul(mx_ref.quantize(e.reshape(128, 512).astype(BF)), q))
    return np.stack(o, axis=2).reshape(128, -1)
def f(rng, *shape):
    return mx_ref.flush((rng.standard_normal(shape, dtype=np.float32) * np.exp2(rng.integers(-2, 3, shape[:-1] + (1,)))).astype(BF))
def wide(rng, *shape, cols=0):
    v = rng.standard_normal(shape, dtype=np.float32) * np.exp2(rng.integers(-12, 13, shape)).astype(np.float32)
    if cols: v *= np.repeat(np.exp2(rng.integers(-cols, cols + 1, shape[:-2] + (1, shape[-1] // 4))) * (rng.random(shape[:-2] + (1, shape[-1] // 4)) > 0.0625), 4, axis=-1).astype(np.float32)
    return mx_ref.flush(v.astype(BF))
M, K, J, R = 256, 80, 3, 3
def unpack(q):
    c = q[0].reshape(16, 8, -1, 4).astype(int)
    s = np.broadcast_to(q[1].astype(int)[:, None, :, None], c.shape)
    k = np.unique(q[1]).astype(int)
    k = np.concatenate([k, np.ones(4 + k.size % 2, int)])
    here = np.zeros((256, 256), np.uint8)
    here[s, c] = c
    z = np.zeros((128, k.size, 4), np.uint8)
    z[:64] = here[k].reshape(-1, 64, 4).transpose(1, 0, 2)
    v = decode((z.reshape(128, -1), np.repeat(k[None], 16, axis=0).astype(np.uint8)))
    held = np.zeros((256, 256), np.float32)
    held[k] = v.reshape(128, -1, 4)[:64].transpose(1, 0, 2).reshape(-1, 256)
    return held[s, c].reshape(128, -1)
def big(v):
    v = np.array(v)
    v[np.abs(v.astype(np.float32)) < np.float32(2.0 ** -16)] = 0
    return v
def bf(v):
    return np.asarray(v, np.float32).astype(BF)
def parts(t):
    return t.reshape(N, 128, -1, 4)
def store(e):
    return np.stack([table(v.T) for v in e.reshape(N, M, J)])
def setup_inputs(rng):
    return {"x": big(f(rng, N, 128, 4 * M)), "u": np.array(f(rng, N, 128, 512)), "w": np.array(f(rng, N, 128, 512)), "nb": store(rng.integers(0, N * M, (N * M, J)))}
def setup_inputs_chain(rng):
    d, n = setup_inputs(rng), N * M
    at = rng.permutation(n)
    e = at[rng.integers(0, np.arange(1, n + 1)[:, None], (n, J))]
    j = np.arange(n - 1)
    e[j, rng.integers(0, J, n - 1)] = at[j + 1]
    nb, h = np.zeros((n, J), int), np.zeros(n, int)
    nb[at], h[at] = e, np.arange(n)
    x, u = parts(d["x"]), parts(d["u"])
    x[:, :16] = 0
    u[:, :, :R] = 0
    for k in range(12):
        x[:, 4 * (k // 4), :, k % 4] = bf((h >> k & 1).reshape(N, M))
        u[:, 4 * (k // 4), :R, k % 4] = 2.0 ** k
    return {"x": x.reshape(N, 128, -1), "u": u.reshape(N, 128, -1), "w": d["w"], "nb": store(nb)}
def setup_inputs_deep(rng):
    d, n = setup_inputs(rng), N * M
    at = np.sort(rng.permutation(n).reshape(-1, 4), axis=1)
    nb, low = np.zeros((n, J), int), np.zeros(n)
    for k in range(4): nb[at[:, k]] = at[:, [min(k + i, 3) for i in (1, 2, 3)]]
    low[at[1::2]] = 11
    x, u = parts(d["x"]), parts(d["u"])
    u[:, :, :R] = 0
    for t, k in enumerate(rng.permutation(R)):
        v = np.zeros(n)
        v[at] = [(4, 4, 4, 7), (4, 7, 4, 6), (7, 7, 5, 5)][k]
        x[:, 40 * t:40 * t + 40] = bf((v - low).reshape(N, 1, M, 1) * 2.0 ** 27)
        u[:, 40 * t:40 * t + 40, t] = 2.0 ** 30
    return {"x": x.reshape(N, 128, -1), "u": u.reshape(N, 128, -1), "w": d["w"], "nb": store(rng.permuted(nb, axis=1))}
def setup_inputs_peaks(rng):
    d, n = setup_inputs(rng), N * M
    who = rng.permutation(N)
    peaks = [M * who[t] + rng.permutation(M)[:K] for t in range(R)]
    lone = np.zeros(n, bool)
    lone[np.concatenate(peaks)] = True
    lone[M * who[R]:M * who[R] + M] = True
    m = np.flatnonzero(~lone)
    nb = np.repeat(np.arange(n)[:, None], J, axis=1)
    x, u = parts(d["x"]), parts(d["u"])
    u[:, :, :R] = mx_ref.flush(bf(u[:, :, :R].astype(np.float32) * np.float32(2.0 ** -6)))
    for t in range(R):
        nb[m, t] = rng.permutation(np.concatenate([peaks[t], peaks[t], rng.choice(peaks[t], m.size - 2 * K)]))
        level = rng.integers(1, 4, n)
        level[peaks[t]] = 7
        x[:, 32 * t:32 * t + 16] = 0
        u[:, 32 * t:32 * t + 16, :R] = 0
        x[:, 32 * t, :, 0] = bf(level.reshape(N, M))
        u[:, 32 * t, t, 0] = 1024
    return {"x": x.reshape(N, 128, -1), "u": u.reshape(N, 128, -1), "w": d["w"], "nb": store(rng.permuted(nb, axis=1))}
def setup_inputs_spread(rng):
    return {**setup_inputs(rng), "x": big(wide(rng, N, 128, 4 * M, cols=6))}
def setup_inputs_ties(rng):
    d = setup_inputs(rng)
    x, u = parts(d["x"]), parts(d["u"])
    x[:, :16] = 0
    x[:, 0, :, 0] = 4
    u[:, :, :R] = 0
    u[:, 0, :R, 0] = -2.0 ** 30
    for t in range(R):
        p = 32 * t + 32
        x[:, p:p + 16] = 0
        x[:, p, :, 0] = bf(rng.integers(4, 8, (N, M)))
        u[:, p, t, 0] = 1024
    return {"x": x.reshape(N, 128, -1), "u": u.reshape(N, 128, -1), "w": d["w"], "nb": d["nb"]}
def check_inputs(d):
    b = []
    for k in ("x", "u", "w"):
        v = np.abs(d[k].astype(np.float32))
        if not (np.isfinite(v).all() and ((v == 0) | (v >= 2.0 ** -30) & (v <= 2.0 ** 30)).all()): b.append("a value of " + k)
    if d["nb"].min() < 0 or d["nb"].max() >= N * M: b.append("nb")
    return b
def reference(x, u, w, nb):
    node = np.arange(N * M)
    near = np.concatenate([entries(nb[r]).reshape(J, M).T for r in range(N)])
    near = np.sort(np.concatenate([node[:, None], near], axis=1), axis=1)
    state = join(*[mx_ref.quantize(np.ascontiguousarray(x[r])) for r in range(N)])
    own = node.reshape(N, M)
    pieces = [np.concatenate([own[r], np.full(-M % 128, -1)]).reshape(-1, 128) for r in range(N)]
    qu = [mx_ref.quantize(np.ascontiguousarray(u[r][:, :16])) for r in range(N)]
    y, rt = np.zeros((N, 128, M), np.float32), np.zeros((N, 1, R * M), np.float32)
    oc, osc = np.zeros((N, 128, 4 * M), np.uint8), np.zeros((N, 16, M), np.uint8)
    for t in range(R):
        h = np.concatenate([np.concatenate([mx_ref.matmul(pick(state, e), qu[r])[:, t] for e in pieces[r]])[:M] for r in range(N)]) + np.float32(0)
        root = near[node, np.argmax(h[near], axis=1)]
        while (root[root] != root).any(): root = root[root]
        size = np.bincount(root, minlength=N * M)
        chosen = np.argsort(-size, kind="stable")[:K]
        m = np.flatnonzero(np.isin(root, chosen) & (root != node))
        if m.size:
            v = unpack(state).reshape(128, N * M, 4)
            v = (v[:, m] + v[:, root[m]]) * np.float32(0.5)
            v = np.concatenate([v, np.zeros((128, -m.size % 4, 4), np.float32)], axis=1)
            new = mx_ref.quantize(np.ascontiguousarray(v.reshape(128, -1).astype(BF)))
            state = put(state, m, pick(new, np.arange(m.size)))
        rt[:, 0, t * M:t * M + M] = root.reshape(N, M)
    for r in range(N):
        y[r] = mx_ref.matmul(mx_ref.quantize(np.ascontiguousarray(w[r])), pick(state, own[r]))
        oc[r], osc[r] = emit(pick(state, own[r]))
    return {"y": y, "oc": oc, "osc": osc, "rt": rt}

@@ -1,0 +1,568 @@
+import numpy as np
+from concourse.bass import DstId, RemoteDMATransfer
+from concourse.mybir import dt, AluOpType, AxisListType, ActivationFunctionType
+
+ALU = AluOpType
+AF = ActivationFunctionType
+N, M, K, J, R = 4, 256, 80, 3, 3
+NM = N * M
+SMAX = NM // K + 1
+NTH = SMAX - 1
+NTS = 5
+NTV = NTH - NTS
+BIGR = NM + K
+WINV = BIGR + M
+CUT1, CUT2 = 64, 544
+C8, U8, F32, B16, I32, U16 = "float8_e4m3fn_x4", "uint8", "float32", "bfloat16", "int32", "uint16"
+
+SCRATCH = {
+    "xt": ("sbuf", [128, 4 * M], B16), "ut": ("sbuf", [128, 512], B16), "wt": ("sbuf", [128, 512], B16),
+    "qu": ("sbuf", [128, 128], C8), "su": ("sbuf", [128, 128], U8),
+    "qw": ("sbuf", [128, 128], C8), "sw": ("sbuf", [128, 128], U8),
+    "qr": ("sbuf", [128, 384], C8), "sr": ("sbuf", [128, 384], U8),
+    "one": ("sbuf", [128, 2048], B16), "et": ("sbuf", [128, 2048], B16),
+    "qe": ("sbuf", [128, 512], C8), "se": ("sbuf", [128, 512], U8),
+    "hp": ("psum", [128, 512], F32), "yp": ("psum", [128, 512], F32), "bl": ("psum", [128, 2048], F32),
+    "d0": ("sbuf", [128, NM], F32), "idf": ("sbuf", [128, NM + 16], F32), "io2": ("sbuf", [128, M], F32),
+    "wn": ("sbuf", [128, NM + 16], F32),
+    "xe": ("sbuf", [128, NM], F32), "fh": ("sbuf", [128, NM], F32), "fs": ("sbuf", [128, NM], F32),
+    "fa": ("sbuf", [128, NM], F32), "fb": ("sbuf", [128, NM], F32), "fc": ("sbuf", [128, NM], F32),
+    "la": ("sbuf", [128, 64], U16), "lb": ("sbuf", [128, 64], U16), "lc": ("sbuf", [128, 64], U16),
+    "l0": ("sbuf", [128, 64], U16), "l1": ("sbuf", [128, 64], U16), "l2": ("sbuf", [128, 64], U16),
+    "sc": ("sbuf", [128, NM], F32), "ra": ("sbuf", [128, 1536], F32), "rb": ("sbuf", [128, 1536], F32),
+    "trs": ("sbuf", [128, NM], F32), "eqa": ("sbuf", [128, NM], B16), "eqb": ("sbuf", [128, NM], B16),
+    "ht": ("sbuf", [128, M], F32), "inv": ("sbuf", [128, WINV], F32),
+    "iw": ("sbuf", [128, 64], I32), "iu": ("sbuf", [128, 24], I32), "id16": ("sbuf", [128, 16], I32),
+    "r12": ("sbuf", [128, 32 * NTV], B16), "cm": ("sbuf", [128, 32 * NTV], B16), "cms": ("sbuf", [128, 32 * NTV], B16),
+    "nb8": ("sbuf", [128, 48], I32), "nbl": ("sbuf", [128, 64], U16), "nbw": ("sbuf", [128, 64], U16), "lnb": ("sbuf", [128, 96], U16),
+    "sz8": ("sbuf", [128, 8], F32), "rot": ("sbuf", [128, 32], F32), "acc": ("sbuf", [128, 8], F32), "ypd": ("sbuf", [128, 32], F32),
+    "szs": ("sbuf", [128, 32], F32), "hb": ("sbuf", [128, 4 * M], B16), "ys": ("sbuf", [128, M], F32),
+}
+SMALL = {
+    "zf": (F32, {"d16": 16, "d17": 16, "cf": 32, "ri": 32, "mlt": 32, "rest": 32, "alp": 32, "one32": 32, "cn": 128, "sn": 16, "ki": 16, "s80": 8,
+                 "nbf": 24, "nbg": 24, "nbh": 16, "nba": 64, "nbb": 64, "nbd": 64, "m1": 32, "m2": 32, "mm": 32, "eq4": 128, "b4": 128,
+                 "b2": 64, "b1": 32, "nx": 32, "tn": 32, "tw": 32, "nxs": 32, "hd": 32, "hv": 64, "ytr": 32, "col": 8, "a1": 32, "cs": 32,
+                 "f2": 32, "g1": 32, "gt": 32, "eq2": 32, "eqf": 32, "gg": 32, "inc": 32, "a2": 32, "a2t": 32, "ie": 32, "t1": 32, "t3": 32,
+                 "nr": 32, "slot": 32, "slw": 32, "sx": 32, "sxs": 32, "rho": 64, "j2f": 8}),
+    "zi": (I32, {"ip": 16, "aci": 4, "i6": 6, "si": 32, "tie": 32, "gc2": 32, "rhi": 16}),
+    "zu": (U16, {"cexp": 64, "crep": 64, "cu": 24, "rotl": 2, "lro": 16, "sll": 16, "j1": 6, "j2": 6, "pl": 16, "kl": 16}),
+}
+AT = {}
+for _b, (_d, _parts) in SMALL.items():
+    _o = 0
+    for _n, _w in _parts.items():
+        AT[_n] = (_b, _o, _w)
+        _o += -(-_w // 16) * 16
+    SCRATCH[_b] = ("sbuf", [128, _o], _d)
+for _t in range(R):
+    SCRATCH["xh%d" % _t] = ("sbuf", [128, 32], F32)
+    for _n in ("a", "b"):
+        SCRATCH["q%s%d" % (_n, _t)] = ("sbuf", [128, 2 * K], C8)
+        SCRATCH["s%s%d" % (_n, _t)] = ("sbuf", [128, 2 * K], U8)
+    SCRATCH["qp%d" % _t] = ("sbuf", [128, M], C8)
+    SCRATCH["sp%d" % _t] = ("sbuf", [128, M], U8)
+for _t in range(R + 1):
+    SCRATCH["qc%d" % _t] = ("sbuf", [128, 2 * M if _t < R else M], C8)
+    SCRATCH["scp%d" % _t] = ("sbuf", [128, 2 * M if _t < R else M], U8)
+
+SEMAPHORES = (["ev", "es", "et", "eg", "loc", "nbr"] + ["h%d" % t for t in range(R)]
+              + ["%s%d" % (k, t) for t in range(R) for k in ("ac", "as", "bc", "bs")]
+              + ["dx", "du", "dw", "dnb", "dswap", "drot", "drt", "dout"])
+
+
+def rank_program(g, core, T, topo):
+    rank = T.rank_of(core)
+    if rank is None:
+        return
+    queue = {"v": g.vector, "s": g.scalar, "t": g.tensor, "g": g, "y": g.sync}
+    esem = {"v": "ev", "s": "es", "t": "et", "g": "eg"}
+    cnt, known, clock, hist = {}, {k: {} for k in queue}, {}, {}
+
+    def V(name, a=0, b=None, step=1, p0=0, p1=128):
+        buf, off, w = AT[name] if name in AT else (name, 0, SCRATCH[name][1][1])
+        return (buf, off + a, off + (w if b is None else b), step, p0, p1)
+
+    def A(r):
+        return T[r[0]][r[4]:r[5], r[1]:r[2]] if r[3] == 1 else T[r[0]][r[4]:r[5], r[1]:r[2]:r[3]]
+
+    def meets(a, b):
+        if a[1] >= b[2] or b[1] >= a[2] or a[4] >= b[5] or b[4] >= a[5]:
+            return False
+        return not (a[3] == b[3] and a[3] > 1 and (a[1] - b[1]) % a[3])
+
+    def grown(r):
+        return (r[0], r[1] // 512 * 512, -(-r[2] // 512) * 512, 1, 0, 128)
+
+    def split(reads, writes):
+        ps = [r for r in list(reads) + list(writes) if SCRATCH[r[0]][0] == "psum"]
+        return ([r for r in reads if SCRATCH[r[0]][0] != "psum"],
+                [r for r in writes if SCRATCH[r[0]][0] != "psum"] + [grown(r) for r in ps])
+
+    def use(qn, reads, writes):
+        reads, writes = split(reads, writes)
+        need = {}
+        for r, w in [(r, False) for r in reads] + [(r, True) for r in writes]:
+            for e, ew, sem, val in hist.get(r[0], []):
+                if (w or ew) and meets(r, e) and known[qn].get(sem, 0) < val:
+                    need[sem] = max(need.get(sem, 0), val)
+        for sem in sorted(need):
+            if any(o != sem and clock[(o, need[o])].get(sem, 0) >= need[sem] for o in need):
+                continue
+            queue[qn].wait_ge(T.sem[sem], need[sem])
+        for sem in need:
+            for s2, v2 in clock[(sem, need[sem])].items():
+                known[qn][s2] = max(known[qn].get(s2, 0), v2)
+            known[qn][sem] = max(known[qn].get(sem, 0), need[sem])
+
+    def mark(sem, val, reads, writes):
+        reads, writes = split(reads, writes)
+        for r in writes:
+            hist[r[0]] = [h for h in hist.get(r[0], []) if not (r[3] == 1 and r[1] <= h[0][1] and h[0][2] <= r[2] and r[4] <= h[0][4] and h[0][5] <= r[5])]
+        for r, w in [(r, False) for r in reads] + [(r, True) for r in writes]:
+            hist.setdefault(r[0], []).append((r, w, sem, val))
+
+    def done(qn, inst, sem, n, reads, writes):
+        cnt[sem] = cnt.get(sem, 0) + n
+        inst.then_inc(T.sem[sem], n)
+        clock[(sem, cnt[sem])] = dict(known[qn])
+        mark(sem, cnt[sem], reads, writes)
+
+    def emit(qn, fn, outs, ins):
+        use(qn, ins, outs)
+        done(qn, fn(), esem[qn], 1, ins, outs)
+
+    def dmas(sem, items):
+        tot = cnt.get(sem, 0) + 16 * len(items)
+        merged = {}
+        for qn, out, in_, outs, ins in items:
+            use(qn, ins, outs)
+            queue[qn].dma_start(out, in_).then_inc(T.sem[sem], 16)
+            for s, v in known[qn].items():
+                merged[s] = max(merged.get(s, 0), v)
+        cnt[sem] = tot
+        clock[(sem, tot)] = merged
+        for qn, out, in_, outs, ins in items:
+            mark(sem, tot, ins, outs)
+
+    def arrives(sem, n, writes):
+        cnt[sem] = cnt.get(sem, 0) + n
+        clock[(sem, cnt[sem])] = {}
+        mark(sem, cnt[sem], [], writes)
+
+    def ind(win, off):
+        return A(win).indirect(A(off))
+
+    def cp(out, in_, off=None):
+        emit("v", lambda: g.vector.tensor_copy(A(out), A(in_) if off is None else ind(in_, off)), [out], [in_] + ([off] if off else []))
+
+    def ts(out, in0, s1, op0, s2=None, op1=None):
+        cols = [s for s in (s1, s2) if isinstance(s, tuple)]
+        val = lambda s: A(s) if isinstance(s, tuple) else s
+        if op1 is None:
+            fn = lambda: g.vector.tensor_scalar(A(out), A(in0), val(s1), None, op0)
+        else:
+            fn = lambda: g.vector.tensor_scalar(A(out), A(in0), val(s1), val(s2), op0, op1)
+        emit("v", fn, [out], [in0] + cols)
+
+    def tt(out, a, b, op):
+        emit("v", lambda: g.vector.tensor_tensor(A(out), A(a), A(b), op), [out], [a, b])
+
+    def red(out, in_, op):
+        emit("v", lambda: g.vector.tensor_reduce(A(out), A(in_), AxisListType.X, op), [out], [in_])
+
+    def scan(out, d0, d1, op0, op1):
+        emit("v", lambda: g.vector.tensor_tensor_scan(A(out), A(d0), A(d1), 0.0, op0, op1), [out], [d0, d1])
+
+    def tr(out, in_):
+        emit("v", lambda: g.vector.transpose(A(out), A(in_)), [out], [in_])
+
+    def fill(out, c):
+        emit("v", lambda: g.vector.memset(A(out), c), [out], [])
+
+    def act(out, in_, func=AF.Copy, off=None, accum=None, **kw):
+        src = lambda: A(in_) if off is None else ind(in_, off)
+        def fn():
+            if accum is None:
+                return g.scalar.activation(A(out), src(), func, **kw)
+            return g.scalar.activation(A(out), src(), func, accum_out=A(accum), **kw)
+        emit("s", fn, [out] + ([accum] if accum else []), [in_] + ([off] if off else []))
+
+    def iota(out, pattern, base, cm):
+        if SCRATCH[out[0]][2] == I32:
+            fn = lambda: g.iota(A(out), pattern, base, cm)
+        else:
+            fn = lambda: g.iota(A(out), pattern, base, cm, allow_small_or_imprecise_dtypes=True)
+        emit("g", fn, [out], [])
+
+    def select(out, in_, pattern, cmp, fillv, base, cm):
+        emit("g", lambda: g.affine_select(A(out), A(in_), pattern, cmp, fillv, base, cm), [out], [in_])
+
+    def quant(q, s, in_):
+        emit("v", lambda: g.vector.quantize_mx(A(q), A(s), A(in_)), [q, s], [in_])
+
+    def mm(out, lq, ls, rq, rs, start, stop):
+        emit("t", lambda: g.tensor.matmul_mx(A(out), A(lq), A(ls), A(rq), A(rs), start, stop), [out], [lq, ls, rq, rs])
+
+    def pick(qo, so, qi, si, off):
+        emit("v", lambda: g.vector.tensor_copy(A(qo).bitcast(dt.uint32), A(qi).bitcast(dt.uint32).indirect(A(off))), [qo], [qi, off])
+        act(so, si, off=off)
+
+    others = [d for d in range(N) if d != rank]
+    groups = 2
+
+    def spread(src, sem):
+        use("g", [src], [])
+        tx = []
+        for i, d in enumerate(others):
+            dst = T.cores[d]
+            rid, pid = topo.addr(dst)[:2]
+            mask = sum(1 << e for e in topo.engines(core, dst)[groups * i:groups * i + groups])
+            tx.append(RemoteDMATransfer(dst_ids=[DstId(rid=rid, pnc=pid)], dma_engine_mask=mask, remote_sem=T.sem[sem], src=A(src), dst=A(src)))
+        g.remote_dma_fused(tx, local_sem=T.sem.loc)
+        cnt["loc"] = cnt.get("loc", 0) + groups * len(others)
+
+    near = [d for d in others if topo.same_plane(topo.chip(core), topo.chip(T.cores[d]))][0]
+    pair = sorted([rank, near])
+    pair2 = [d for d in range(N) if d not in pair]
+    far = pair2[pair.index(rank)]
+
+    def swap(q, s, d, semc, sems):
+        dst = T.cores[d]
+        rid, pid = topo.addr(dst)[:2]
+        mask, n = topo.mask(core, dst), len(topo.engines(core, dst))
+        use("g", [V(q, 0, K)], [])
+        g.remote_dma(A(V(q, K, 2 * K)).bitcast(dt.uint8), A(V(q, 0, K)).bitcast(dt.uint8), T.sem[semc], T.sem.loc, pid, rid, mask)
+        use("g", [V(s, 0, K)], [])
+        g.remote_dma(A(V(s, K, 2 * K)), A(V(s, 0, K)), T.sem[sems], T.sem.loc, pid, rid, mask)
+        cnt["loc"] = cnt.get("loc", 0) + 2 * n
+        arrives(semc, n, [V(q, K, 2 * K)])
+        arrives(sems, n, [V(s, K, 2 * K)])
+
+    def widen(x, c0, c1, on, scale=1.0, bias=0.0):
+        out, win, off = V("xe", 32 * c0, 32 * c1), V(x, c0, c1), V("cexp", 0, 2 * (c1 - c0))
+        if on == "v":
+            cp(out, win, off)
+        elif scale == 1.0 and bias == 0.0:
+            act(out, win, off=off)
+        else:
+            act(out, win, AF.Identity, off=off, scale=scale, bias=bias)
+
+    def turn(f, c0, c1):
+        tr(V(f, 32 * c0, 32 * c1), V("xe", 32 * c0, 32 * c1))
+
+    CF = lambda k: V("cf", k, k + 1)
+    OFFC, OFFM, HCOL, UCOL, SCOL, LCOL, BCOL, BETA = [CF(k) for k in (0, 1, 4, 5, 6, 7, 8, 3)]
+
+    def lift(f, a, b):
+        scan(V("sc", a, b), V("d0", 0, b - a), V(f, a, b), ALU.add, ALU.max)
+
+    def listed(out, a, b, extra=None):
+        if extra is None:
+            ts(out, V("sc", a + 15, b, 16), OFFC, ALU.add)
+        else:
+            ts(out, V("sc", a + 15, b, 16), OFFC, ALU.add, float(extra), ALU.add)
+
+    def halves(x, xs, a, n, out):
+        tt(V("hd", 0, n), V(xs, a, a + n), V(x, a, a + n), ALU.subtract)
+        ts(V("hd", 0, n), V("hd", 0, n), HCOL, ALU.mult)
+        tt(V("hv", 0, 2 * n, 2), V(x, a, a + n), V("hd", 0, n), ALU.add)
+        tt(V("hv", 1, 2 * n, 2), V(xs, a, a + n), V("hd", 0, n), ALU.subtract)
+        cp(out, V("hv", 0, 2 * n))
+
+    dmas("dx", [("y", A(V("xt")), T.x[:], [V("xt")], [])])
+    dmas("du", [("s", A(V("ut")), T.u[:], [V("ut")], [])])
+    dmas("dnb", [("ys"[k % 2], A(V("nb8", p0=16 * k, p1=16 * k + 16)), T.nb[:], [V("nb8", p0=16 * k, p1=16 * k + 16)], []) for k in range(8)])
+    IP = lambda k: V("ip", k, k + 1)
+    iota(IP(0), [[0, 1]], 0, 1)
+    iota(V("iu"), [[1, 3], [0, 8]], 0, 0)
+    iota(V("iw"), [[1, 32], [0, 2]], 0, 0)
+    iota(V("id16"), [[1, 16]], 128, -1)
+    iota(V("ri"), [[1, 32]], 0, 0)
+    cp(V("cu"), V("iu"))
+    ts(IP(4), IP(0), 4, ALU.logical_shift_right, 1, ALU.bitwise_and)
+    ts(IP(5), IP(0), 6, ALU.logical_shift_right)
+    ts(IP(1), IP(0), 15, ALU.bitwise_and)
+    ts(IP(2), IP(0), 31, ALU.bitwise_and)
+    ts(IP(3), IP(0), 5, ALU.logical_shift_right)
+    cp(V("cf", 4, 6), V("ip", 4, 6))
+    cp(V("cf", 6, 9), V("ip", 1, 4))
+    cp(V("cexp"), V("iw"))
+    quant(V("qu"), V("su"), V("ut"))
+    pick(V("qr"), V("sr"), V("qu"), V("su"), V("cu"))
+    quant(V("qc0", 0, M), V("scp0", 0, M), V("xt"))
+
+    def heights(t):
+        mm(V("hp", 0, M), V("qr", 128 * t, 128 * t + 128), V("sr", 128 * t, 128 * t + 128), V("qc%d" % t, 0, M), V("scp%d" % t, 0, M), True, True)
+        tr(V("ht"), V("hp", 0, M))
+        own = V("xh%d" % t, 8 * rank, 8 * rank + 8)
+        cp(own, V("ht", 0, M, 32))
+        spread(own, "h%d" % t)
+        arrives("h%d" % t, groups * len(others), [V("xh%d" % t, 8 * d, 8 * d + 8) for d in others])
+
+    for e in (0, 1):
+        tt(V("nbg", e, 24, 2), V("nb8", 2 + e, 48, 4), V("nb8", e, 48, 4), ALU.subtract)
+    fill(V("nbh", 12, 16), 0.0)
+    ts(V("nbg"), V("nbg"), HCOL, ALU.mult)
+    for e in (0, 1):
+        tt(V("nbf", e, 24, 2), V("nbg", e, 24, 2), V("nb8", e, 48, 4), ALU.add)
+    tt(V("nbg", 0, 12), V("nbf", 12, 24), V("nbf", 0, 12), ALU.subtract)
+    ts(V("nbg", 0, 12), V("nbg", 0, 12), UCOL, ALU.mult)
+    tt(V("nbh", 0, 12), V("nbg", 0, 12), V("nbf", 0, 12), ALU.add)
+    cp(V("nbl", 16 * rank, 16 * rank + 16), V("nbh"))
+    spread(V("nbl", 16 * rank, 16 * rank + 16), "nbr")
+    arrives("nbr", groups * len(others), [V("nbl", 16 * d, 16 * d + 16) for d in others])
+    heights(0)
+    dmas("dw", [("y", A(V("wt")), T.w[:], [V("wt")], [])])
+
+    iota(V("idf"), [[1, NM + 16]], 0, 0)
+    iota(V("sn"), [[16, 16]], M * rank, 0)
+    iota(V("ki"), [[16, 16]], 0, 0)
+    iota(V("s80"), [[16, 8]], 0, 0)
+    iota(V("io2"), [[1, M]], NM, 0)
+    widen("xh0", 8 * rank, 8 * rank + 8, "v")
+    turn("fh", 8 * rank, 8 * rank + 8)
+    ts(OFFC, SCOL, 15.0, ALU.is_lt, -2048.0, ALU.mult)
+    ts(V("id16"), V("id16"), 15, ALU.bitwise_and)
+    ts(V("iw"), V("iw"), 0.0, ALU.mult)
+    ts(OFFM, OFFC, float(-NM), ALU.add)
+    ts(V("d16"), V("id16"), 0.0, ALU.is_equal, -2048.0, ALU.mult)
+    ts(V("d17"), V("id16"), 1.0, ALU.is_equal, 2048.0, ALU.mult)
+    ts(V("crep"), V("iw"), SCOL, ALU.add)
+    tt(V("d16"), V("d16"), V("d17"), ALU.add)
+    fill(V("one32"), 1.0)
+    ts(V("d16", 0, 1), V("d16", 0, 1), -4096.0, ALU.add)
+    act(V("d0"), V("d16"), off=V("crep"))
+    act(V("wn"), V("idf"), scale=0.0)
+    fill(V("one"), 1.0)
+    select(V("et"), V("one"), [[-1, 4], [1, 512]], ALU.is_equal, 0.0, 0, -4)
+    for b in range(4):
+        blk = V("wn", p0=32 * b, p1=32 * b + 32)
+        select(blk, blk, [[1, NM + 16]], ALU.not_equal, 1.0, -(8 * b + 8), -32)
+        select(blk, blk, [[1, NM + 16]], ALU.not_equal, 2048.0, -(8 * b + 9), -32)
+    ts(V("mlt"), V("ri"), LCOL, ALU.is_gt)
+    ts(IP(6), IP(2), 7, ALU.bitwise_and)
+    ts(CF(10), LCOL, -1.0, ALU.mult, float(NM), ALU.add)
+    ts(CF(11), LCOL, 32.0, ALU.mult)
+    ts(CF(9), IP(6), 32.0, ALU.mult, float(BIGR), ALU.add)
+    ts(V("cn", 96, 128), V("ri"), -32.0, ALU.mult, CF(10), ALU.add)
+    ts(CF(12), BCOL, 8.0, ALU.mult, CF(11), ALU.add)
+    ts(V("rest"), V("ri"), CF(9), ALU.add)
+    for k in (6, 7):
+        ts(CF(10 + k), CF(12), float(k), ALU.add)
+    ts(BETA, LCOL, float(NTS), ALU.is_lt, NM / 2.0, ALU.mult)
+    ts(V("alp"), V("one32"), BETA, ALU.mult, -1.0 / NM, ALU.mult)
+    ts(V("alp"), V("alp"), 1.0, ALU.add)
+    ts(IP(7), IP(1), 3, ALU.logical_shift_right)
+    ts(IP(8), IP(1), 7, ALU.bitwise_and)
+    tt(IP(9), IP(3), IP(7), ALU.subtract)
+    cp(CF(20), IP(8))
+    ts(IP(10), IP(9), 4.0, ALU.add)
+    ts(IP(11), IP(9), 2.0, ALU.add)
+    ts(V("ip", 12, 14), V("ip", 10, 12), 3, ALU.bitwise_and)
+    ts(V("sn"), V("sn"), SCOL, ALU.add)
+    ts(V("rotl"), V("ip", 12, 14), 8.0, ALU.mult, CF(20), ALU.add)
+    ts(V("ki"), V("ki"), SCOL, ALU.add)
+    ts(V("s80"), V("s80"), SCOL, ALU.add)
+    fill(V("ypd"), 0.0)
+    fill(V("r12"), 1.0)
+    fill(V("r12", 0, 32 * NTV, 32), 0.0)
+
+    dmas("dswap", [("y", A(V("nbw", p0=0, p1=64)), A(V("nbl", p0=64, p1=128)), [V("nbw", p0=0, p1=64)], [V("nbl", p0=64, p1=128)]),
+                   ("s", A(V("nbw", p0=64, p1=128)), A(V("nbl", p0=0, p1=64)), [V("nbw", p0=64, p1=128)], [V("nbl", p0=0, p1=64)])])
+    cp(V("nba"), V("nbl"))
+    cp(V("nbb"), V("nbw"))
+    tt(V("nbd"), V("nbb"), V("nba"), ALU.subtract)
+    ts(V("nbd"), V("nbd"), UCOL, ALU.mult)
+    tt(V("nba"), V("nba"), V("nbd"), ALU.add)
+    tt(V("nbb"), V("nbb"), V("nbd"), ALU.subtract)
+    for to, src, a, n in ((0, "nba", 0, 8), (32, "nba", 8, 4), (36, "nbb", 0, 4), (64, "nbb", 4, 8)):
+        for d in range(N):
+            cp(V("lnb", to + 8 * d, to + 8 * d + n), V(src, 16 * d + a, 16 * d + a + n))
+
+    def around(win):
+        cuts = ((384, 960), (960, 1536))
+        for a, b in cuts:
+            act(V("ra", a, b), win, off=V("lnb", a // 16, b // 16))
+        cp(V("ra", 0, 384), win, V("lnb", 0, 24))
+        for a, b in ((0, 384),) + cuts:
+            tr(V("rb", a, b), V("ra", a, b))
+
+    around(V("idf", 0, NM))
+    ts(V("cn", 0, 96), V("rb", 0, 1536, 16), -1.0, ALU.mult, float(NM), ALU.add)
+
+    b1, b2 = CUT1, CUT2
+    win3 = ["fa", "fb", "fc"]
+    lst3 = ["la", "lb", "lc"]
+    lo = M * rank
+    COL = lambda k: V("col", k, k + 1)
+    for t in range(R):
+        xh, qc, sp = "xh%d" % t, "qc%d" % t, "scp%d" % t
+        if t:
+            heights(t)
+            widen(xh, 8 * rank, 8 * rank + 8, "v")
+            turn("fh", 8 * rank, 8 * rank + 8)
+        widen(xh, 8 * others[1], 8 * others[1] + 8, "s")
+        widen(xh, 8 * others[2], 8 * others[2] + 8, "s")
+        widen(xh, 8 * others[0], 8 * others[0] + 8, "v")
+        for d in others:
+            turn("fh", 8 * d, 8 * d + 8)
+        around(V("fh"))
+        nbh = [V("rb", 512 * k, 512 * k + 512, 16) for k in range(J)] + [V(xh)]
+        tt(V("m1"), nbh[0], nbh[1], ALU.max)
+        tt(V("m2"), nbh[2], nbh[3], ALU.max)
+        tt(V("mm"), V("m1"), V("m2"), ALU.max)
+        for k in range(J + 1):
+            tt(V("eq4", 32 * k, 32 * k + 32), nbh[k], V("mm"), ALU.is_equal)
+        tt(V("b4"), V("eq4"), V("cn"), ALU.mult)
+        tt(V("b2"), V("b4", 0, 64), V("b4", 64, 128), ALU.max)
+        tt(V("b1"), V("b2", 0, 32), V("b2", 32, 64), ALU.max)
+        widen("b1", 0, 16, "s", -1.0, float(NM))
+        widen("b1", 16, 32, "s", -1.0, float(NM))
+        ts(V("nx"), V("b1"), -1.0, ALU.mult, float(NM), ALU.add)
+        tr(V("tn"), V("nx"))
+        cp(V("tw", 0, 16), V("tn", 16, 32))
+        cp(V("tw", 16, 32), V("tn", 0, 16))
+        tr(V("nxs"), V("tw"))
+        halves("nx", "nxs", 0, 32, V("la"))
+        turn("fa", 0, 16)
+        turn("fa", 16, 32)
+        for k in range(10):
+            fi, fo, li, lw = win3[k % 3], win3[(k + 1) % 3], lst3[k % 3], lst3[(k + 1) % 3]
+            act(V(fo, b1, b2), V(fi), off=V(li, b1 // 16, b2 // 16))
+            act(V(fo, b2, NM), V(fi), off=V(li, b2 // 16, 64))
+            cp(V(fo, 0, b1), V(fi), V(li, 0, b1 // 16))
+            for a, b in ((0, b2), (b2, NM)):
+                lift(fo, a, b)
+                if k < 9:
+                    listed(V(lw, a // 16, b // 16), a, b)
+                else:
+                    listed(V("l0", a // 16, b // 16), a, b, 8)
+                    act(V("trs", 0, b - a), V("wn"), off=V("l0", a // 16, b // 16), accum=V("acc", 3 * (a > 0), 3 * (a > 0) + 1))
+        ff = win3[10 % 3]
+        for j in (1, 2):
+            listed(V("l%d" % j), 0, NM, 8 - 2 * j)
+            act(V("trs"), V("wn"), off=V("l%d" % j), accum=V("acc", j, j + 1))
+        row = V(ff, lo, lo + M, 1, 0, 1)
+        dmas("drt", [("y", T.rt[0:1, M * t:M * t + M], A(row), [], [row])])
+        for k, e in ((6, "eqa"), (7, "eqb")):
+            ts(V(e), V(ff), CF(10 + k), ALU.is_equal)
+            red(V("sz8", k, k + 1), V(e), ALU.add)
+        tt(V("acc", 0, 1), V("acc", 0, 1), V("acc", 3, 4), ALU.add)
+        cp(V("aci", 0, 3), V("acc", 0, 3))
+        ts(V("i6", 0, 6, 2), V("aci", 0, 3), 2047, ALU.bitwise_and)
+        ts(V("i6", 1, 6, 2), V("aci", 0, 3), 11, ALU.logical_shift_right)
+        cp(V("sz8", 0, 6), V("i6"))
+        moves = []
+        for i in (1, 2, 3):
+            c = 32 * i
+            for qn, d0, d1, s0, s1 in (("y", c, 128, 0, 128 - c), ("s", 0, c, 128 - c, 128)):
+                o, s = V("rot", 8 * i, 8 * i + 8, 1, d0, d1), V("sz8", 0, 8, 1, s0, s1)
+                moves.append((qn, A(o), A(s), [o], [s]))
+        dmas("drot", moves)
+        cp(V("rot", 0, 8), V("sz8"))
+        listed(V("rho", 0, 16), lo, lo + M)
+        listed(V("lro"), lo, lo + M)
+        cp(V("rhi"), V("rho", 0, 16))
+        tt(V("rho", 16, 32), V("rho", 0, 16), V("sn"), ALU.not_equal)
+        ts(V("rhi"), V("rhi"), 8, ALU.logical_shift_right)
+        ts(V("rho", 32, 48), V("rhi"), float(pair2[0]), ALU.is_equal, float(K), ALU.mult)
+        ts(V("rho", 48, 64), V("rhi"), float(pair2[1]), ALU.is_equal, float(K), ALU.mult)
+        tt(V("rho", 32, 48), V("rho", 32, 48), V("rho", 48, 64), ALU.add)
+        fill(V("inv", 0, 96), 0.0)
+        if not t:
+            quant(V("qe"), V("se"), V("et"))
+            quant(V("qw"), V("sw"), V("wt"))
+        for b in range(4):
+            mm(V("bl", 512 * b, 512 * b + M), V("qe", 128 * b, 128 * b + 128), V("se", 128 * b, 128 * b + 128), V(qc, 0, M), V(sp, 0, M), True, False)
+        for j in range(NTS):
+            act(V("trs", 32 * j, 32 * j + 32), V("rot"), AF.Sign, bias=-1.5 - j, accum=V("ypd", j, j + 1))
+        act(V("szs"), V("rot"), AF.Identity, off=V("rotl"), scale=2048.0, bias=-2048.0)
+        for j in range(NTV):
+            ts(V("cm", 32 * j, 32 * j + 32), V("rot"), float(NTS + j + 2), ALU.is_ge)
+        scan(V("cms"), V("r12"), V("cm"), ALU.mult, ALU.add)
+        cp(V("ypd", NTS, NTH), V("cms", 31, 32 * NTV, 32))
+        tr(V("ytr"), V("ypd"))
+        red(COL(0), V("ytr"), ALU.add)
+        ts(V("a1"), V("alp"), COL(0), ALU.mult, BETA, ALU.add)
+        tr(V("cs"), V("a1"))
+        ts(V("f2"), V("cs"), float(K), ALU.is_ge, 2048.0, ALU.mult)
+        red(COL(1), V("f2"), ALU.add)
+        tt(V("g1"), V("cs"), V("f2"), ALU.subtract)
+        ts(V("eq2"), V("szs"), COL(1), ALU.is_equal, 2048.0, ALU.mult)
+        ts(V("gt"), V("szs"), COL(1), ALU.is_gt)
+        red(COL(2), V("g1"), ALU.max)
+        tt(V("gg"), V("gt"), V("eq2"), ALU.add)
+        ts(V("eqf"), V("eq2"), 1.0 / 2048.0, ALU.mult)
+        scan(V("inc"), V("one32"), V("gg"), ALU.mult, ALU.add)
+        tt(V("nr"), V("gt"), V("eqf"), ALU.add)
+        ts(V("a2"), V("mlt"), V("inc", 31, 32), ALU.mult)
+        tt(V("ie"), V("inc"), V("gg"), ALU.subtract)
+        tr(V("a2t"), V("a2"))
+        ts(V("nr"), V("nr"), -1.0, ALU.mult, 1.0, ALU.add)
+        red(COL(3), V("a2t"), ALU.add)
+        tt(V("nr"), V("nr"), V("rest"), ALU.mult)
+        ts(V("si"), V("ie"), COL(3), ALU.add)
+        ts(V("tie"), V("si"), 11, ALU.logical_shift_right)
+        ts(V("gc2"), V("si"), 2047, ALU.bitwise_and)
+        ts(V("t3"), V("tie"), COL(2), ALU.add)
+        tt(V("t1"), V("gc2"), V("gt"), ALU.mult)
+        tt(V("t3"), V("t3"), V("eqf"), ALU.mult)
+        tt(V("t1"), V("t1"), V("nr"), ALU.add)
+        tt(V("slot"), V("t1"), V("t3"), ALU.add)
+        tt(V("slw", 0, 16), V("t1", 16, 32), V("t3", 16, 32), ALU.add)
+        tt(V("slw", 16, 32), V("t1", 0, 16), V("t3", 0, 16), ALU.add)
+        tr(V("sx"), V("slot"))
+        tr(V("sxs"), V("slw"))
+        widen("sx", 0, 16, "s")
+        halves("sx", "sxs", 8 * rank, 8, V("sll"))
+        emit("v", lambda: g.vector.tensor_copy(ind(V("inv"), V("sll")), A(V("io2"))), [V("inv")], [V("io2"), V("sll")])
+        lift("inv", 0, K)
+        k5 = V("sc", 15, K, 16)
+        ts(V("j1", 0, 5), k5, OFFM, ALU.add, 0.0, ALU.max)
+        qa, sa, qb, sb = "qa%d" % t, "sa%d" % t, "qb%d" % t, "sb%d" % t
+        pick(V(qa, 0, K), V(sa, 0, K), V(qc, 0, M), V(sp, 0, M), V("j1", 0, 5))
+        widen("sx", 16, 32, "s")
+        swap(qa, sa, near, "ac%d" % t, "as%d" % t)
+        ts(V("j2f", 0, 5), k5, OFFC, ALU.add, float(NM), ALU.is_lt)
+        turn("fs", 0, 16)
+        ts(V("j2f", 0, 5), V("j2f", 0, 5), float(K), ALU.mult)
+        tt(V("j2f", 0, 5), V("j2f", 0, 5), V("s80", 0, 5), ALU.add)
+        turn("fs", 16, 32)
+        cp(V("j2", 0, 5), V("j2f", 0, 5))
+        cp(V("ht"), V("fs"), V("lro"))
+        scan(V("sc", 0, M), V("d0", 0, M), V("ht"), ALU.add, ALU.max)
+        so = V("rho", 0, 16)
+        listed(so, 0, M)
+        ts(V("rho", 48, 64), so, float(K), ALU.is_lt)
+        tt(V("rho", 16, 32), V("rho", 16, 32), V("rho", 48, 64), ALU.mult)
+        tt(so, so, V("rho", 16, 32), ALU.mult)
+        tt(V("rho", 32, 48), V("rho", 32, 48), so, ALU.add)
+        cp(V("pl"), V("rho", 32, 48))
+        ts(V("rho", 16, 32), V("rho", 16, 32), float(M), ALU.mult)
+        tt(V("rho", 16, 32), V("rho", 16, 32), V("ki"), ALU.add)
+        cp(V("kl"), V("rho", 16, 32))
+        pick(V(qb, 0, K), V(sb, 0, K), V(qa), V(sa), V("j2", 0, 5))
+        swap(qb, sb, far, "bc%d" % t, "bs%d" % t)
+        pick(V("qp%d" % t), V("sp%d" % t), V(qb), V(sb), V("pl"))
+        for b in range(4):
+            mm(V("bl", 512 * b, 512 * b + M), V("qe", 128 * b, 128 * b + 128), V("se", 128 * b, 128 * b + 128), V("qp%d" % t), V("sp%d" % t), False, True)
+        for b in range(4):
+            src, out = V("bl", 512 * b, 512 * b + M), V("hb", b, 4 * M, 4)
+            if b % 2:
+                act(out, src, scale=0.5)
+            else:
+                ts(out, src, 0.5, ALU.mult)
+        quant(V(qc, M, 2 * M), V(sp, M, 2 * M), V("hb"))
+        pick(V("qc%d" % (t + 1), 0, M), V("scp%d" % (t + 1), 0, M), V(qc), V(sp), V("kl"))
+
+    qc, sp = V("qc%d" % R), V("scp%d" % R)
+    mm(V("yp", 0, M), V("qw"), V("sw"), qc, sp, True, True)
+    outs = [("y", T.oc[:], A(qc).bitcast(dt.uint8), [], [qc])]
+    for k in range(4):
+        o = V("scp%d" % R, 0, M, 1, 32 * k, 32 * k + 4)
+        outs.append(("y", T.osc[4 * k:4 * k + 4, 0:M], A(o), [], [o]))
+    cp(V("ys"), V("yp", 0, M))
+    outs.append(("s", T.y[:], A(V("ys")), [], [V("ys")]))
+    dmas("dout", outs)
+    for sem in sorted(cnt):
+        g.sync.wait_ge(T.sem[sem], cnt[sem])

@@ -8,11 +8,11 @@ N, M, K, J, R = 4, 256, 80, 3, 3
 NM = N * M
 SMAX = NM // K + 1
 NTH = SMAX - 1
-NTS = 5
-NTV = NTH - NTS
+NTS = 7
+LOW = 4.0 * NM
 BIGR = NM + K
-WINV = BIGR + M
-CUT1, CUT2 = 64, 544
+WINV = BIGR + M + K
+CUT1, CUT2 = 480, 928
 C8, U8, F32, B16, I32, U16 = "float8_e4m3fn_x4", "uint8", "float32", "bfloat16", "int32", "uint16"
 
 SCRATCH = {
@@ -20,7 +20,7 @@ SCRATCH = {
     "qu": ("sbuf", [128, 128], C8), "su": ("sbuf", [128, 128], U8),
     "qw": ("sbuf", [128, 128], C8), "sw": ("sbuf", [128, 128], U8),
     "qr": ("sbuf", [128, 384], C8), "sr": ("sbuf", [128, 384], U8),
-    "one": ("sbuf", [128, 2048], B16), "et": ("sbuf", [128, 2048], B16),
+    "one": ("sbuf", [128, 512], B16), "et": ("sbuf", [128, 2048], B16),
     "qe": ("sbuf", [128, 512], C8), "se": ("sbuf", [128, 512], U8),
     "hp": ("psum", [128, 512], F32), "yp": ("psum", [128, 512], F32), "bl": ("psum", [128, 2048], F32),
     "d0": ("sbuf", [128, NM], F32), "idf": ("sbuf", [128, NM + 16], F32), "io2": ("sbuf", [128, M], F32),
@@ -31,20 +31,20 @@ SCRATCH = {
     "l0": ("sbuf", [128, 64], U16), "l1": ("sbuf", [128, 64], U16), "l2": ("sbuf", [128, 64], U16),
     "sc": ("sbuf", [128, NM], F32), "ra": ("sbuf", [128, 1536], F32), "rb": ("sbuf", [128, 1536], F32),
     "trs": ("sbuf", [128, NM], F32), "eqa": ("sbuf", [128, NM], B16), "eqb": ("sbuf", [128, NM], B16),
-    "ht": ("sbuf", [128, M], F32), "inv": ("sbuf", [128, WINV], F32),
+    "ht": ("sbuf", [128, M], F32), "ho": ("sbuf", [128, M], F32), "rs": ("sbuf", [128, M], F32), "inv": ("sbuf", [128, WINV], F32),
     "iw": ("sbuf", [128, 64], I32), "iu": ("sbuf", [128, 24], I32), "id16": ("sbuf", [128, 16], I32),
-    "r12": ("sbuf", [128, 32 * NTV], B16), "cm": ("sbuf", [128, 32 * NTV], B16), "cms": ("sbuf", [128, 32 * NTV], B16),
-    "nb8": ("sbuf", [128, 48], I32), "nbl": ("sbuf", [128, 64], U16), "nbw": ("sbuf", [128, 64], U16), "lnb": ("sbuf", [128, 96], U16),
+    "cm": ("sbuf", [128, 32 * NTH], F32),
+    "nbe": ("sbuf", [128, 48], I32), "nbl": ("sbuf", [128, 64], U16), "nbw": ("sbuf", [128, 64], U16), "lnb": ("sbuf", [128, 96], U16),
     "sz8": ("sbuf", [128, 8], F32), "rot": ("sbuf", [128, 32], F32), "acc": ("sbuf", [128, 8], F32), "ypd": ("sbuf", [128, 32], F32),
     "szs": ("sbuf", [128, 32], F32), "hb": ("sbuf", [128, 4 * M], B16), "ys": ("sbuf", [128, M], F32),
 }
 SMALL = {
     "zf": (F32, {"d16": 16, "d17": 16, "cf": 32, "ri": 32, "mlt": 32, "rest": 32, "alp": 32, "one32": 32, "cn": 128, "sn": 16, "ki": 16, "s80": 8,
-                 "nbf": 24, "nbg": 24, "nbh": 16, "nba": 64, "nbb": 64, "nbd": 64, "m1": 32, "m2": 32, "mm": 32, "eq4": 128, "b4": 128,
-                 "b2": 64, "b1": 32, "nx": 32, "tn": 32, "tw": 32, "nxs": 32, "hd": 32, "hv": 64, "ytr": 32, "col": 8, "a1": 32, "cs": 32,
-                 "f2": 32, "g1": 32, "gt": 32, "eq2": 32, "eqf": 32, "gg": 32, "inc": 32, "a2": 32, "a2t": 32, "ie": 32, "t1": 32, "t3": 32,
-                 "nr": 32, "slot": 32, "slw": 32, "sx": 32, "sxs": 32, "rho": 64, "j2f": 8}),
-    "zi": (I32, {"ip": 16, "aci": 4, "i6": 6, "si": 32, "tie": 32, "gc2": 32, "rhi": 16}),
+                 "m1": 32, "mm": 32, "eq4": 128, "b4": 128, "b2": 64, "b1": 32, "nx": 32, "tn": 32, "zz": 64, "zt": 64,
+                 "ytr": 32, "col": 8, "a1": 32, "cs": 32, "f2": 32, "g1": 32, "ge": 64, "inc": 64, "ie": 64, "a2": 64, "a2t": 64,
+                 "ne": 32, "je": 32, "nr": 32, "e4": 32, "jg": 32, "ug": 32, "ue": 32, "slot": 32, "sx": 32,
+                 "rho": 64, "j2f": 8, "mx": 8, "mx1": 8, "xo": 8, "xm": 8}),
+    "zi": (I32, {"ip": 16, "aci": 4, "rhi": 16}),
     "zu": (U16, {"cexp": 64, "crep": 64, "cu": 24, "rotl": 2, "lro": 16, "sll": 16, "j1": 6, "j2": 6, "pl": 16, "kl": 16}),
 }
 AT = {}
@@ -129,6 +129,9 @@ def rank_program(g, core, T, topo):
 
     def emit(qn, fn, outs, ins):
         use(qn, ins, outs)
+        if qn == "g" and known["g"].get("eg", 0) < cnt.get("eg", 0):
+            g.wait_ge(T.sem.eg, cnt["eg"])
+            known["g"]["eg"] = cnt["eg"]
         done(qn, fn(), esem[qn], 1, ins, outs)
 
     def dmas(sem, items):
@@ -251,7 +254,7 @@ def rank_program(g, core, T, topo):
         tr(V(f, 32 * c0, 32 * c1), V("xe", 32 * c0, 32 * c1))
 
     CF = lambda k: V("cf", k, k + 1)
-    OFFC, OFFM, HCOL, UCOL, SCOL, LCOL, BCOL, BETA = [CF(k) for k in (0, 1, 4, 5, 6, 7, 8, 3)]
+    OFFC, OFFM, SCOL, LCOL, BCOL, BETA, HCOL = [CF(k) for k in (0, 1, 6, 7, 8, 3, 4)]
 
     def lift(f, a, b):
         scan(V("sc", a, b), V("d0", 0, b - a), V(f, a, b), ALU.add, ALU.max)
@@ -262,65 +265,74 @@ def rank_program(g, core, T, topo):
         else:
             ts(out, V("sc", a + 15, b, 16), OFFC, ALU.add, float(extra), ALU.add)
 
-    def halves(x, xs, a, n, out):
-        tt(V("hd", 0, n), V(xs, a, a + n), V(x, a, a + n), ALU.subtract)
-        ts(V("hd", 0, n), V("hd", 0, n), HCOL, ALU.mult)
-        tt(V("hv", 0, 2 * n, 2), V(x, a, a + n), V("hd", 0, n), ALU.add)
-        tt(V("hv", 1, 2 * n, 2), V(xs, a, a + n), V("hd", 0, n), ALU.subtract)
-        cp(out, V("hv", 0, 2 * n))
-
+    loads = []
+    for k in range(8):
+        o = V("nbe", 0, 48 - 2 * (k % 2), 1, 16 * k, 16 * k + 16)
+        loads.append(("ys"[k % 2], A(o), T.nb[:, 2 * (k % 2):48], [o], []))
+    dmas("dnb", loads)
     dmas("dx", [("y", A(V("xt")), T.x[:], [V("xt")], [])])
     dmas("du", [("s", A(V("ut")), T.u[:], [V("ut")], [])])
-    dmas("dnb", [("ys"[k % 2], A(V("nb8", p0=16 * k, p1=16 * k + 16)), T.nb[:], [V("nb8", p0=16 * k, p1=16 * k + 16)], []) for k in range(8)])
     IP = lambda k: V("ip", k, k + 1)
-    iota(IP(0), [[0, 1]], 0, 1)
     iota(V("iu"), [[1, 3], [0, 8]], 0, 0)
+    iota(IP(0), [[0, 1]], 0, 1)
     iota(V("iw"), [[1, 32], [0, 2]], 0, 0)
-    iota(V("id16"), [[1, 16]], 128, -1)
-    iota(V("ri"), [[1, 32]], 0, 0)
     cp(V("cu"), V("iu"))
     ts(IP(4), IP(0), 4, ALU.logical_shift_right, 1, ALU.bitwise_and)
-    ts(IP(5), IP(0), 6, ALU.logical_shift_right)
     ts(IP(1), IP(0), 15, ALU.bitwise_and)
     ts(IP(2), IP(0), 31, ALU.bitwise_and)
     ts(IP(3), IP(0), 5, ALU.logical_shift_right)
-    cp(V("cf", 4, 6), V("ip", 4, 6))
-    cp(V("cf", 6, 9), V("ip", 1, 4))
     cp(V("cexp"), V("iw"))
+    cp(CF(4), IP(4))
+    cp(V("cf", 6, 9), V("ip", 1, 4))
+    o = 16 * rank
+    for e in (0, 1):
+        cp(V("nbl", o + e, o + 12, 2, 0, 64), V("nbe", e, 24, 4, 0, 64))
+        cp(V("nbl", o + e, o + 12, 2, 64, 128), V("nbe", 24 + e, 48, 4, 64, 128))
+    cp(V("nbl", o + 12, o + 16), V("nbe", 0, 4))
+    spread(V("nbl", o, o + 16), "nbr")
+    arrives("nbr", groups * len(others), [V("nbl", 16 * d, 16 * d + 16) for d in others])
     quant(V("qu"), V("su"), V("ut"))
     pick(V("qr"), V("sr"), V("qu"), V("su"), V("cu"))
     quant(V("qc0", 0, M), V("scp0", 0, M), V("xt"))
 
-    def heights(t):
-        mm(V("hp", 0, M), V("qr", 128 * t, 128 * t + 128), V("sr", 128 * t, 128 * t + 128), V("qc%d" % t, 0, M), V("scp%d" % t, 0, M), True, True)
-        tr(V("ht"), V("hp", 0, M))
-        own = V("xh%d" % t, 8 * rank, 8 * rank + 8)
-        cp(own, V("ht", 0, M, 32))
-        spread(own, "h%d" % t)
+    def height(out, t, q, s, a):
+        mm(V(out, 0, M), V("qr", 128 * t, 128 * t + 128), V("sr", 128 * t, 128 * t + 128), V(q, a, a + M), V(s, a, a + M), True, True)
+
+    def share(t):
+        spread(V("xh%d" % t, 8 * rank, 8 * rank + 8), "h%d" % t)
         arrives("h%d" % t, groups * len(others), [V("xh%d" % t, 8 * d, 8 * d + 8) for d in others])
 
-    for e in (0, 1):
-        tt(V("nbg", e, 24, 2), V("nb8", 2 + e, 48, 4), V("nb8", e, 48, 4), ALU.subtract)
-    fill(V("nbh", 12, 16), 0.0)
-    ts(V("nbg"), V("nbg"), HCOL, ALU.mult)
-    for e in (0, 1):
-        tt(V("nbf", e, 24, 2), V("nbg", e, 24, 2), V("nb8", e, 48, 4), ALU.add)
-    tt(V("nbg", 0, 12), V("nbf", 12, 24), V("nbf", 0, 12), ALU.subtract)
-    ts(V("nbg", 0, 12), V("nbg", 0, 12), UCOL, ALU.mult)
-    tt(V("nbh", 0, 12), V("nbg", 0, 12), V("nbf", 0, 12), ALU.add)
-    cp(V("nbl", 16 * rank, 16 * rank + 16), V("nbh"))
-    spread(V("nbl", 16 * rank, 16 * rank + 16), "nbr")
-    arrives("nbr", groups * len(others), [V("nbl", 16 * d, 16 * d + 16) for d in others])
-    heights(0)
+    def own_f(t):
+        widen("xh%d" % t, 8 * rank, 8 * rank + 8, "v")
+        turn("fh", 8 * rank, 8 * rank + 8)
+
+    def others_f(t):
+        xh = "xh%d" % t
+        widen(xh, 8 * others[1], 8 * others[1] + 8, "s")
+        widen(xh, 8 * others[2], 8 * others[2] + 8, "s")
+        widen(xh, 8 * others[0], 8 * others[0] + 8, "v")
+        for d in others:
+            turn("fh", 8 * d, 8 * d + 8)
+
+    height("hp", 0, "qc0", "scp0", 0)
+    tr(V("ht"), V("hp", 0, M))
+    cp(V("xh0", 8 * rank, 8 * rank + 8), V("ht", 0, M, 32))
+    share(0)
     dmas("dw", [("y", A(V("wt")), T.w[:], [V("wt")], [])])
 
+    iota(V("ri"), [[1, 32]], 0, 0)
+    iota(V("id16"), [[1, 16]], 128, -1)
     iota(V("idf"), [[1, NM + 16]], 0, 0)
     iota(V("sn"), [[16, 16]], M * rank, 0)
     iota(V("ki"), [[16, 16]], 0, 0)
     iota(V("s80"), [[16, 8]], 0, 0)
     iota(V("io2"), [[1, M]], NM, 0)
-    widen("xh0", 8 * rank, 8 * rank + 8, "v")
-    turn("fh", 8 * rank, 8 * rank + 8)
+    own_f(0)
+    for k in range(J):
+        for e in (0, 1):
+            a = 32 * k + 8 * rank
+            cp(V("lnb", a + e, a + 8, 2), V("nbe", 16 * k + e, 16 * k + 16, 4))
+    fill(V("one"), 1.0)
     ts(OFFC, SCOL, 15.0, ALU.is_lt, -2048.0, ALU.mult)
     ts(V("id16"), V("id16"), 15, ALU.bitwise_and)
     ts(V("iw"), V("iw"), 0.0, ALU.mult)
@@ -331,127 +343,133 @@ def rank_program(g, core, T, topo):
     tt(V("d16"), V("d16"), V("d17"), ALU.add)
     fill(V("one32"), 1.0)
     ts(V("d16", 0, 1), V("d16", 0, 1), -4096.0, ALU.add)
-    act(V("d0"), V("d16"), off=V("crep"))
     act(V("wn"), V("idf"), scale=0.0)
-    fill(V("one"), 1.0)
-    select(V("et"), V("one"), [[-1, 4], [1, 512]], ALU.is_equal, 0.0, 0, -4)
     for b in range(4):
         blk = V("wn", p0=32 * b, p1=32 * b + 32)
         select(blk, blk, [[1, NM + 16]], ALU.not_equal, 1.0, -(8 * b + 8), -32)
         select(blk, blk, [[1, NM + 16]], ALU.not_equal, 2048.0, -(8 * b + 9), -32)
-    ts(V("mlt"), V("ri"), LCOL, ALU.is_gt)
-    ts(IP(6), IP(2), 7, ALU.bitwise_and)
-    ts(CF(10), LCOL, -1.0, ALU.mult, float(NM), ALU.add)
+    for b in range(4):
+        select(V("et", 512 * b, 512 * b + 512), V("one"), [[1, 512]], ALU.is_equal, 0.0, -b, -4)
     ts(CF(11), LCOL, 32.0, ALU.mult)
-    ts(CF(9), IP(6), 32.0, ALU.mult, float(BIGR), ALU.add)
-    ts(V("cn", 96, 128), V("ri"), -32.0, ALU.mult, CF(10), ALU.add)
+    ts(CF(10), LCOL, -1.0, ALU.mult, float(NM), ALU.add)
+    ts(V("mlt"), V("ri"), LCOL, ALU.is_gt)
     ts(CF(12), BCOL, 8.0, ALU.mult, CF(11), ALU.add)
-    ts(V("rest"), V("ri"), CF(9), ALU.add)
+    ts(V("cn", 96, 128), V("ri"), -32.0, ALU.mult, CF(10), ALU.add)
     for k in (6, 7):
         ts(CF(10 + k), CF(12), float(k), ALU.add)
-    ts(BETA, LCOL, float(NTS), ALU.is_lt, NM / 2.0, ALU.mult)
-    ts(V("alp"), V("one32"), BETA, ALU.mult, -1.0 / NM, ALU.mult)
-    ts(V("alp"), V("alp"), 1.0, ALU.add)
-    ts(IP(7), IP(1), 3, ALU.logical_shift_right)
-    ts(IP(8), IP(1), 7, ALU.bitwise_and)
-    tt(IP(9), IP(3), IP(7), ALU.subtract)
-    cp(CF(20), IP(8))
-    ts(IP(10), IP(9), 4.0, ALU.add)
-    ts(IP(11), IP(9), 2.0, ALU.add)
-    ts(V("ip", 12, 14), V("ip", 10, 12), 3, ALU.bitwise_and)
-    ts(V("sn"), V("sn"), SCOL, ALU.add)
-    ts(V("rotl"), V("ip", 12, 14), 8.0, ALU.mult, CF(20), ALU.add)
-    ts(V("ki"), V("ki"), SCOL, ALU.add)
-    ts(V("s80"), V("s80"), SCOL, ALU.add)
-    fill(V("ypd"), 0.0)
-    fill(V("r12"), 1.0)
-    fill(V("r12", 0, 32 * NTV, 32), 0.0)
 
     dmas("dswap", [("y", A(V("nbw", p0=0, p1=64)), A(V("nbl", p0=64, p1=128)), [V("nbw", p0=0, p1=64)], [V("nbl", p0=64, p1=128)]),
-                   ("s", A(V("nbw", p0=64, p1=128)), A(V("nbl", p0=0, p1=64)), [V("nbw", p0=64, p1=128)], [V("nbl", p0=0, p1=64)])])
-    cp(V("nba"), V("nbl"))
-    cp(V("nbb"), V("nbw"))
-    tt(V("nbd"), V("nbb"), V("nba"), ALU.subtract)
-    ts(V("nbd"), V("nbd"), UCOL, ALU.mult)
-    tt(V("nba"), V("nba"), V("nbd"), ALU.add)
-    tt(V("nbb"), V("nbb"), V("nbd"), ALU.subtract)
-    for to, src, a, n in ((0, "nba", 0, 8), (32, "nba", 8, 4), (36, "nbb", 0, 4), (64, "nbb", 4, 8)):
-        for d in range(N):
-            cp(V("lnb", to + 8 * d, to + 8 * d + n), V(src, 16 * d + a, 16 * d + a + n))
+                   ("y", A(V("nbw", p0=64, p1=128)), A(V("nbl", p0=0, p1=64)), [V("nbw", p0=64, p1=128)], [V("nbl", p0=0, p1=64)])])
+    first, second = ((0, 0, 8), (32, 8, 4)), ((36, 0, 4), (64, 4, 8))
 
-    def around(win):
-        cuts = ((384, 960), (960, 1536))
+    def lists(src, a, b):
+        for d in others:
+            for p, parts in ((a, first), (b, second)):
+                for to, at, n in parts:
+                    cp(V("lnb", to + 8 * d, to + 8 * d + n, 1, p, p + 64), V(src, 16 * d + at, 16 * d + at + n, 1, p, p + 64))
+
+    lists("nbl", 0, 64)
+    others_f(0)
+    lists("nbw", 64, 0)
+
+    def around(win, mid=None):
+        cuts = ((384, 1024), (1024, 1536))
         for a, b in cuts:
             act(V("ra", a, b), win, off=V("lnb", a // 16, b // 16))
         cp(V("ra", 0, 384), win, V("lnb", 0, 24))
-        for a, b in ((0, 384),) + cuts:
-            tr(V("rb", a, b), V("ra", a, b))
+        tr(V("rb", 0, 384), V("ra", 0, 384))
+        tr(V("rb", 384, 1024), V("ra", 384, 1024))
+        if mid:
+            mid()
+        tr(V("rb", 1024, 1536), V("ra", 1024, 1536))
 
     around(V("idf", 0, NM))
     ts(V("cn", 0, 96), V("rb", 0, 1536, 16), -1.0, ALU.mult, float(NM), ALU.add)
+
+    def late():
+        ts(BETA, LCOL, float(NTS), ALU.is_lt, NM / 2.0, ALU.mult)
+        ts(IP(6), IP(2), 7, ALU.bitwise_and)
+        ts(IP(7), IP(1), 3, ALU.logical_shift_right)
+        ts(IP(8), IP(1), 7, ALU.bitwise_and)
+        ts(V("alp"), V("one32"), BETA, ALU.mult, -1.0 / NM, ALU.mult)
+        ts(CF(9), IP(6), 32.0, ALU.mult, float(BIGR), ALU.add)
+        tt(IP(9), IP(3), IP(7), ALU.subtract)
+        cp(CF(20), IP(8))
+        ts(V("alp"), V("alp"), 1.0, ALU.add)
+        ts(V("rest"), V("ri"), CF(9), ALU.add)
+        ts(IP(10), IP(9), 4.0, ALU.add)
+        ts(IP(11), IP(9), 2.0, ALU.add)
+        ts(V("sn"), V("sn"), SCOL, ALU.add)
+        ts(V("ip", 12, 14), V("ip", 10, 12), 3, ALU.bitwise_and)
+        ts(V("ki"), V("ki"), SCOL, ALU.add)
+        ts(V("rotl"), V("ip", 12, 14), 8.0, ALU.mult, CF(20), ALU.add)
+        ts(V("s80"), V("s80"), SCOL, ALU.add)
+        fill(V("ypd"), 0.0)
 
     b1, b2 = CUT1, CUT2
     win3 = ["fa", "fb", "fc"]
     lst3 = ["la", "lb", "lc"]
     lo = M * rank
     COL = lambda k: V("col", k, k + 1)
+    ACC = lambda k: V("acc", k, k + 1)
     for t in range(R):
         xh, qc, sp = "xh%d" % t, "qc%d" % t, "scp%d" % t
         if t:
-            heights(t)
-            widen(xh, 8 * rank, 8 * rank + 8, "v")
-            turn("fh", 8 * rank, 8 * rank + 8)
-        widen(xh, 8 * others[1], 8 * others[1] + 8, "s")
-        widen(xh, 8 * others[2], 8 * others[2] + 8, "s")
-        widen(xh, 8 * others[0], 8 * others[0] + 8, "v")
-        for d in others:
-            turn("fh", 8 * d, 8 * d + 8)
-        around(V("fh"))
+            own_f(t)
+            others_f(t)
         nbh = [V("rb", 512 * k, 512 * k + 512, 16) for k in range(J)] + [V(xh)]
-        tt(V("m1"), nbh[0], nbh[1], ALU.max)
-        tt(V("m2"), nbh[2], nbh[3], ALU.max)
-        tt(V("mm"), V("m1"), V("m2"), ALU.max)
+
+        def mid():
+            tt(V("m1"), nbh[0], nbh[1], ALU.max)
+            tt(V("m1"), V("m1"), nbh[3], ALU.max)
+
+        around(V("fh"), mid)
+        if not t:
+            act(V("d0"), V("d16"), off=V("crep"))
+        tt(V("mm"), V("m1"), nbh[2], ALU.max)
         for k in range(J + 1):
             tt(V("eq4", 32 * k, 32 * k + 32), nbh[k], V("mm"), ALU.is_equal)
         tt(V("b4"), V("eq4"), V("cn"), ALU.mult)
         tt(V("b2"), V("b4", 0, 64), V("b4", 64, 128), ALU.max)
         tt(V("b1"), V("b2", 0, 32), V("b2", 32, 64), ALU.max)
-        widen("b1", 0, 16, "s", -1.0, float(NM))
-        widen("b1", 16, 32, "s", -1.0, float(NM))
+        for a, b in ((0, 16), (16, 24), (24, 32)):
+            widen("b1", a, b, "s", -1.0, float(NM))
         ts(V("nx"), V("b1"), -1.0, ALU.mult, float(NM), ALU.add)
         tr(V("tn"), V("nx"))
-        cp(V("tw", 0, 16), V("tn", 16, 32))
-        cp(V("tw", 16, 32), V("tn", 0, 16))
-        tr(V("nxs"), V("tw"))
-        halves("nx", "nxs", 0, 32, V("la"))
-        turn("fa", 0, 16)
-        turn("fa", 16, 32)
+        for a in (0, 16, 32, 48):
+            cp(V("zz", a, a + 16), V("tn", a // 32 * 16, a // 32 * 16 + 16))
+        tr(V("zt"), V("zz"))
+        for e in (0, 1):
+            cp(V("la", e, 64, 2), V("zt", 32 * e, 32 * e + 32))
+        for a, b in ((0, 16), (16, 24), (24, 32)):
+            turn("fa", a, b)
         for k in range(10):
             fi, fo, li, lw = win3[k % 3], win3[(k + 1) % 3], lst3[k % 3], lst3[(k + 1) % 3]
+            act(V(fo, 0, b1), V(fi), off=V(li, 0, b1 // 16))
             act(V(fo, b1, b2), V(fi), off=V(li, b1 // 16, b2 // 16))
-            act(V(fo, b2, NM), V(fi), off=V(li, b2 // 16, 64))
-            cp(V(fo, 0, b1), V(fi), V(li, 0, b1 // 16))
-            for a, b in ((0, b2), (b2, NM)):
+            cp(V(fo, b2, NM), V(fi), V(li, b2 // 16, 64))
+            for a, b in ((0, b1), (b1, NM)):
                 lift(fo, a, b)
                 if k < 9:
                     listed(V(lw, a // 16, b // 16), a, b)
                 else:
                     listed(V("l0", a // 16, b // 16), a, b, 8)
-                    act(V("trs", 0, b - a), V("wn"), off=V("l0", a // 16, b // 16), accum=V("acc", 3 * (a > 0), 3 * (a > 0) + 1))
+                    act(V("trs", 0, b - a), V("wn"), off=V("l0", a // 16, b // 16), accum=ACC(3 * (a > 0)))
         ff = win3[10 % 3]
         for j in (1, 2):
             listed(V("l%d" % j), 0, NM, 8 - 2 * j)
-            act(V("trs"), V("wn"), off=V("l%d" % j), accum=V("acc", j, j + 1))
+            act(V("trs"), V("wn"), off=V("l%d" % j), accum=ACC(j))
         row = V(ff, lo, lo + M, 1, 0, 1)
         dmas("drt", [("y", T.rt[0:1, M * t:M * t + M], A(row), [], [row])])
-        for k, e in ((6, "eqa"), (7, "eqb")):
-            ts(V(e), V(ff), CF(10 + k), ALU.is_equal)
-            red(V("sz8", k, k + 1), V(e), ALU.add)
-        tt(V("acc", 0, 1), V("acc", 0, 1), V("acc", 3, 4), ALU.add)
-        cp(V("aci", 0, 3), V("acc", 0, 3))
-        ts(V("i6", 0, 6, 2), V("aci", 0, 3), 2047, ALU.bitwise_and)
-        ts(V("i6", 1, 6, 2), V("aci", 0, 3), 11, ALU.logical_shift_right)
-        cp(V("sz8", 0, 6), V("i6"))
+        ts(V("eqa"), V(ff), CF(16), ALU.is_equal)
+        ts(V("eqb"), V(ff), CF(17), ALU.is_equal)
+        red(V("sz8", 6, 7), V("eqa"), ALU.add)
+        tt(ACC(0), ACC(0), ACC(3), ALU.add)
+        red(V("sz8", 7, 8), V("eqb"), ALU.add)
+        ts(V("aci", 0, 3), V("acc", 0, 3), 1.0 / 2048.0, ALU.mult, -0.499, ALU.add)
+        for j in range(3):
+            ts(V("sz8", 2 * j, 2 * j + 1), V("aci", j, j + 1), -2048.0, ALU.mult, ACC(j), ALU.add)
+        cp(V("sz8", 1, 6, 2), V("aci", 0, 3))
         moves = []
         for i in (1, 2, 3):
             c = 32 * i
@@ -460,62 +478,63 @@ def rank_program(g, core, T, topo):
                 moves.append((qn, A(o), A(s), [o], [s]))
         dmas("drot", moves)
         cp(V("rot", 0, 8), V("sz8"))
+        if not t:
+            late()
         listed(V("rho", 0, 16), lo, lo + M)
         listed(V("lro"), lo, lo + M)
         cp(V("rhi"), V("rho", 0, 16))
         tt(V("rho", 16, 32), V("rho", 0, 16), V("sn"), ALU.not_equal)
         ts(V("rhi"), V("rhi"), 8, ALU.logical_shift_right)
+        fill(V("inv", 0, 96), 0.0)
         ts(V("rho", 32, 48), V("rhi"), float(pair2[0]), ALU.is_equal, float(K), ALU.mult)
         ts(V("rho", 48, 64), V("rhi"), float(pair2[1]), ALU.is_equal, float(K), ALU.mult)
         tt(V("rho", 32, 48), V("rho", 32, 48), V("rho", 48, 64), ALU.add)
-        fill(V("inv", 0, 96), 0.0)
-        if not t:
-            quant(V("qe"), V("se"), V("et"))
-            quant(V("qw"), V("sw"), V("wt"))
-        for b in range(4):
-            mm(V("bl", 512 * b, 512 * b + M), V("qe", 128 * b, 128 * b + 128), V("se", 128 * b, 128 * b + 128), V(qc, 0, M), V(sp, 0, M), True, False)
         for j in range(NTS):
             act(V("trs", 32 * j, 32 * j + 32), V("rot"), AF.Sign, bias=-1.5 - j, accum=V("ypd", j, j + 1))
-        act(V("szs"), V("rot"), AF.Identity, off=V("rotl"), scale=2048.0, bias=-2048.0)
-        for j in range(NTV):
-            ts(V("cm", 32 * j, 32 * j + 32), V("rot"), float(NTS + j + 2), ALU.is_ge)
-        scan(V("cms"), V("r12"), V("cm"), ALU.mult, ALU.add)
-        cp(V("ypd", NTS, NTH), V("cms", 31, 32 * NTV, 32))
+        act(V("szs"), V("rot"), AF.Identity, off=V("rotl"), scale=2.0, bias=-34.0)
+        for j in range(NTS, NTH):
+            ts(V("cm", 32 * j, 32 * j + 32), V("rot"), float(j + 2), ALU.is_ge)
+        for j in range(NTS, NTH):
+            red(V("ypd", j, j + 1), V("cm", 32 * j, 32 * j + 32), ALU.add)
         tr(V("ytr"), V("ypd"))
         red(COL(0), V("ytr"), ALU.add)
         ts(V("a1"), V("alp"), COL(0), ALU.mult, BETA, ALU.add)
         tr(V("cs"), V("a1"))
+        act(V("trs", 0, 32), V("cs"), AF.Sign, bias=0.5 - K, accum=ACC(4))
         ts(V("f2"), V("cs"), float(K), ALU.is_ge, 2048.0, ALU.mult)
-        red(COL(1), V("f2"), ALU.add)
         tt(V("g1"), V("cs"), V("f2"), ALU.subtract)
-        ts(V("eq2"), V("szs"), COL(1), ALU.is_equal, 2048.0, ALU.mult)
-        ts(V("gt"), V("szs"), COL(1), ALU.is_gt)
+        gt, eq = V("ge", 0, 32), V("ge", 32, 64)
+        ts(gt, V("szs"), ACC(4), ALU.is_gt)
+        ts(eq, V("szs"), ACC(4), ALU.is_equal)
         red(COL(2), V("g1"), ALU.max)
-        tt(V("gg"), V("gt"), V("eq2"), ALU.add)
-        ts(V("eqf"), V("eq2"), 1.0 / 2048.0, ALU.mult)
-        scan(V("inc"), V("one32"), V("gg"), ALU.mult, ALU.add)
-        tt(V("nr"), V("gt"), V("eqf"), ALU.add)
-        ts(V("a2"), V("mlt"), V("inc", 31, 32), ALU.mult)
-        tt(V("ie"), V("inc"), V("gg"), ALU.subtract)
-        tr(V("a2t"), V("a2"))
+        scan(V("inc", 0, 32), V("one32"), gt, ALU.mult, ALU.add)
+        scan(V("inc", 32, 64), V("one32"), eq, ALU.mult, ALU.add)
+        tt(V("nr"), gt, eq, ALU.add)
+        ts(V("a2", 0, 32), V("mlt"), V("inc", 31, 32), ALU.mult)
+        ts(V("a2", 32, 64), V("mlt"), V("inc", 63, 64), ALU.mult)
         ts(V("nr"), V("nr"), -1.0, ALU.mult, 1.0, ALU.add)
-        red(COL(3), V("a2t"), ALU.add)
+        tr(V("a2t"), V("a2"))
+        tt(V("ie"), V("inc"), V("ge"), ALU.subtract)
+        ts(V("e4"), eq, -LOW, ALU.mult)
+        red(COL(3), V("a2t", 0, 32), ALU.add)
+        red(COL(5), V("a2t", 32, 64), ALU.add)
         tt(V("nr"), V("nr"), V("rest"), ALU.mult)
-        ts(V("si"), V("ie"), COL(3), ALU.add)
-        ts(V("tie"), V("si"), 11, ALU.logical_shift_right)
-        ts(V("gc2"), V("si"), 2047, ALU.bitwise_and)
-        ts(V("t3"), V("tie"), COL(2), ALU.add)
-        tt(V("t1"), V("gc2"), V("gt"), ALU.mult)
-        tt(V("t3"), V("t3"), V("eqf"), ALU.mult)
-        tt(V("t1"), V("t1"), V("nr"), ALU.add)
-        tt(V("slot"), V("t1"), V("t3"), ALU.add)
-        tt(V("slw", 0, 16), V("t1", 16, 32), V("t3", 16, 32), ALU.add)
-        tt(V("slw", 16, 32), V("t1", 0, 16), V("t3", 0, 16), ALU.add)
+        ts(V("ne"), eq, LOW, ALU.mult, -LOW, ALU.add)
+        tt(V("e4"), V("e4"), V("ie", 0, 32), ALU.add)
+        tt(V("je"), V("ne"), V("ie", 32, 64), ALU.add)
+        tt(V("jg"), V("e4"), V("nr"), ALU.add)
+        ts(V("ue"), V("je"), COL(5), ALU.add, COL(2), ALU.add)
+        ts(V("ug"), V("jg"), COL(3), ALU.add)
+        for a in (0, 16, 32, 48):
+            h = a // 32 * 16
+            tt(V("zz", a, a + 16), V("ug", h, h + 16), V("ue", h, h + 16), ALU.max)
+        tr(V("zt"), V("zz"))
+        tt(V("slot"), V("ug"), V("ue"), ALU.max)
+        for e in (0, 1):
+            cp(V("sll", e, 16, 2), V("zt", 32 * e + 8 * rank, 32 * e + 8 * rank + 8))
         tr(V("sx"), V("slot"))
-        tr(V("sxs"), V("slw"))
-        widen("sx", 0, 16, "s")
-        halves("sx", "sxs", 8 * rank, 8, V("sll"))
         emit("v", lambda: g.vector.tensor_copy(ind(V("inv"), V("sll")), A(V("io2"))), [V("inv")], [V("io2"), V("sll")])
+        widen("sx", 0, 16, "s")
         lift("inv", 0, K)
         k5 = V("sc", 15, K, 16)
         ts(V("j1", 0, 5), k5, OFFM, ALU.add, 0.0, ALU.max)
@@ -529,20 +548,35 @@ def rank_program(g, core, T, topo):
         tt(V("j2f", 0, 5), V("j2f", 0, 5), V("s80", 0, 5), ALU.add)
         turn("fs", 16, 32)
         cp(V("j2", 0, 5), V("j2f", 0, 5))
-        cp(V("ht"), V("fs"), V("lro"))
-        scan(V("sc", 0, M), V("d0", 0, M), V("ht"), ALU.add, ALU.max)
-        so = V("rho", 0, 16)
+        cp(V("rs"), V("fs"), V("lro"))
+        scan(V("sc", 0, M), V("d0", 0, M), V("rs"), ALU.add, ALU.max)
+        so, me = V("rho", 0, 16), V("rho", 16, 32)
         listed(so, 0, M)
         ts(V("rho", 48, 64), so, float(K), ALU.is_lt)
-        tt(V("rho", 16, 32), V("rho", 16, 32), V("rho", 48, 64), ALU.mult)
-        tt(so, so, V("rho", 16, 32), ALU.mult)
+        tt(me, me, V("rho", 48, 64), ALU.mult)
+        tt(so, so, me, ALU.mult)
         tt(V("rho", 32, 48), V("rho", 32, 48), so, ALU.add)
         cp(V("pl"), V("rho", 32, 48))
-        ts(V("rho", 16, 32), V("rho", 16, 32), float(M), ALU.mult)
-        tt(V("rho", 16, 32), V("rho", 16, 32), V("ki"), ALU.add)
-        cp(V("kl"), V("rho", 16, 32))
         pick(V(qb, 0, K), V(sb, 0, K), V(qa), V(sa), V("j2", 0, 5))
         swap(qb, sb, far, "bc%d" % t, "bs%d" % t)
+        ts(V("rho", 48, 64), me, float(M), ALU.mult)
+        tt(V("rho", 48, 64), V("rho", 48, 64), V("ki"), ALU.add)
+        cp(V("kl"), V("rho", 48, 64))
+        if not t:
+            quant(V("qe"), V("se"), V("et"))
+            quant(V("qw"), V("sw"), V("wt"))
+        if t + 1 < R:
+            height("yp", t + 1, qc, sp, 0)
+        for b in range(4):
+            mm(V("bl", 512 * b, 512 * b + M), V("qe", 128 * b, 128 * b + 128), V("se", 128 * b, 128 * b + 128), V(qc, 0, M), V(sp, 0, M), True, False)
+        if t + 1 < R:
+            tr(V("ho"), V("yp", 0, M))
+            m0, m1 = V("rho", 16, 32, 2), V("rho", 17, 32, 2)
+            tt(V("mx"), m1, m0, ALU.subtract)
+            ts(V("mx"), V("mx"), HCOL, ALU.mult)
+            tt(V("mx"), V("mx"), m0, ALU.add)
+            ts(V("mx1"), V("mx"), -1.0, ALU.mult, 1.0, ALU.add)
+            tt(V("xo"), V("ho", 0, M, 32), V("mx1"), ALU.mult)
         pick(V("qp%d" % t), V("sp%d" % t), V(qb), V(sb), V("pl"))
         for b in range(4):
             mm(V("bl", 512 * b, 512 * b + M), V("qe", 128 * b, 128 * b + 128), V("se", 128 * b, 128 * b + 128), V("qp%d" % t), V("sp%d" % t), False, True)
@@ -553,6 +587,12 @@ def rank_program(g, core, T, topo):
             else:
                 ts(out, src, 0.5, ALU.mult)
         quant(V(qc, M, 2 * M), V(sp, M, 2 * M), V("hb"))
+        if t + 1 < R:
+            height("hp", t + 1, qc, sp, M)
+            tr(V("ht"), V("hp", 0, M))
+            tt(V("xm"), V("ht", 0, M, 32), V("mx"), ALU.mult)
+            tt(V("xh%d" % (t + 1), 8 * rank, 8 * rank + 8), V("xm"), V("xo"), ALU.add)
+            share(t + 1)
         pick(V("qc%d" % (t + 1), 0, M), V("scp%d" % (t + 1), 0, M), V(qc), V(sp), V("kl"))
 
     qc, sp = V("qc%d" % R), V("scp%d" % R)

@@ -6,13 +6,15 @@ ALU = AluOpType
 AF = ActivationFunctionType
 N, M, K, J, R = 4, 256, 80, 3, 3
 NM = N * M
+H = M // 2
 SMAX = NM // K + 1
 NTH = SMAX - 1
-NTS = 7
-LOW = 4.0 * NM
+NTS = 8
+BIG = 4.0 * NM
 BIGR = NM + K
 WINV = BIGR + M + K
-CUT1, CUT2 = 480, 928
+CUT1, CUT2 = 160, 640
+CUT3 = 672
 C8, U8, F32, B16, I32, U16 = "float8_e4m3fn_x4", "uint8", "float32", "bfloat16", "int32", "uint16"
 
 SCRATCH = {
@@ -22,15 +24,16 @@ SCRATCH = {
     "qr": ("sbuf", [128, 384], C8), "sr": ("sbuf", [128, 384], U8),
     "one": ("sbuf", [128, 512], B16), "et": ("sbuf", [128, 2048], B16),
     "qe": ("sbuf", [128, 512], C8), "se": ("sbuf", [128, 512], U8),
-    "hp": ("psum", [128, 512], F32), "yp": ("psum", [128, 512], F32), "bl": ("psum", [128, 2048], F32),
-    "d0": ("sbuf", [128, NM], F32), "idf": ("sbuf", [128, NM + 16], F32), "io2": ("sbuf", [128, M], F32),
+    "bl": ("psum", [128, 4096], F32),
+    "d0": ("sbuf", [128, NM], F32), "idf": ("sbuf", [128, NM], F32), "io2": ("sbuf", [128, M], F32),
     "wn": ("sbuf", [128, NM + 16], F32),
     "xe": ("sbuf", [128, NM], F32), "fh": ("sbuf", [128, NM], F32), "fs": ("sbuf", [128, NM], F32),
     "fa": ("sbuf", [128, NM], F32), "fb": ("sbuf", [128, NM], F32), "fc": ("sbuf", [128, NM], F32),
     "la": ("sbuf", [128, 64], U16), "lb": ("sbuf", [128, 64], U16), "lc": ("sbuf", [128, 64], U16),
-    "l0": ("sbuf", [128, 64], U16), "l1": ("sbuf", [128, 64], U16), "l2": ("sbuf", [128, 64], U16),
+    "l0": ("sbuf", [128, 64], U16), "l1": ("sbuf", [128, 64], U16), "l2": ("sbuf", [128, 64], U16), "l3": ("sbuf", [128, 64], U16),
     "sc": ("sbuf", [128, NM], F32), "ra": ("sbuf", [128, 1536], F32), "rb": ("sbuf", [128, 1536], F32),
-    "trs": ("sbuf", [128, NM], F32), "eqa": ("sbuf", [128, NM], B16), "eqb": ("sbuf", [128, NM], B16),
+    "rc": ("sbuf", [128, 1536], F32), "rd": ("sbuf", [128, 1536], F32),
+    "trs": ("sbuf", [128, NM], F32), "dvs": ("sbuf", [128, NM], F32), "dvt": ("sbuf", [128, NM - CUT3], F32),
     "ht": ("sbuf", [128, M], F32), "ho": ("sbuf", [128, M], F32), "rs": ("sbuf", [128, M], F32), "inv": ("sbuf", [128, WINV], F32),
     "iw": ("sbuf", [128, 64], I32), "iu": ("sbuf", [128, 24], I32), "id16": ("sbuf", [128, 16], I32),
     "cm": ("sbuf", [128, 32 * NTH], F32),
@@ -39,13 +42,13 @@ SCRATCH = {
     "szs": ("sbuf", [128, 32], F32), "hb": ("sbuf", [128, 4 * M], B16), "ys": ("sbuf", [128, M], F32),
 }
 SMALL = {
-    "zf": (F32, {"d16": 16, "d17": 16, "cf": 32, "ri": 32, "mlt": 32, "rest": 32, "alp": 32, "one32": 32, "cn": 128, "sn": 16, "ki": 16, "s80": 8,
-                 "m1": 32, "mm": 32, "eq4": 128, "b4": 128, "b2": 64, "b1": 32, "nx": 32, "tn": 32, "zz": 64, "zt": 64,
-                 "ytr": 32, "col": 8, "a1": 32, "cs": 32, "f2": 32, "g1": 32, "ge": 64, "inc": 64, "ie": 64, "a2": 64, "a2t": 64,
-                 "ne": 32, "je": 32, "nr": 32, "e4": 32, "jg": 32, "ug": 32, "ue": 32, "slot": 32, "sx": 32,
+    "zf": (F32, {"d16": 16, "d17": 16, "cf": 32, "ri": 32, "mlt": 32, "rest": 32, "rest2": 64, "alp": 32, "one32": 32, "cn": 128, "sn": 16, "ki": 16, "s80": 8,
+                 "m1": 32, "mm": 32, "eq4": 128, "b4": 128, "b2": 64, "b1": 32, "tn": 32, "zz": 64, "zt": 64, "thr": 8, "t2": 8,
+                 "ytr": 32, "col": 8, "a1": 32, "cs": 32, "f2": 32, "g1": 32, "ge": 64, "inc": 64, "hh": 64, "je": 64, "a2": 64, "a2t": 64,
+                 "ug": 32, "ue": 32, "um": 32, "slot": 32, "sx": 32,
                  "rho": 64, "j2f": 8, "mx": 8, "mx1": 8, "xo": 8, "xm": 8}),
     "zi": (I32, {"ip": 16, "aci": 4, "rhi": 16}),
-    "zu": (U16, {"cexp": 64, "crep": 64, "cu": 24, "rotl": 2, "lro": 16, "sll": 16, "j1": 6, "j2": 6, "pl": 16, "kl": 16}),
+    "zu": (U16, {"cexp": 64, "crep": 64, "cu": 24, "twice": 4, "rotl": 2, "lro": 16, "sll": 16, "j1": 6, "j2": 6, "pl": 16, "kl": 16}),
 }
 AT = {}
 for _b, (_d, _parts) in SMALL.items():
@@ -158,17 +161,18 @@ def rank_program(g, core, T, topo):
     def cp(out, in_, off=None):
         emit("v", lambda: g.vector.tensor_copy(A(out), A(in_) if off is None else ind(in_, off)), [out], [in_] + ([off] if off else []))
 
-    def ts(out, in0, s1, op0, s2=None, op1=None):
+    def ts(out, in0, s1, op0, s2=None, op1=None, off=None):
         cols = [s for s in (s1, s2) if isinstance(s, tuple)]
         val = lambda s: A(s) if isinstance(s, tuple) else s
+        src = lambda: A(in0) if off is None else ind(in0, off)
         if op1 is None:
-            fn = lambda: g.vector.tensor_scalar(A(out), A(in0), val(s1), None, op0)
+            fn = lambda: g.vector.tensor_scalar(A(out), src(), val(s1), None, op0)
         else:
-            fn = lambda: g.vector.tensor_scalar(A(out), A(in0), val(s1), val(s2), op0, op1)
-        emit("v", fn, [out], [in0] + cols)
+            fn = lambda: g.vector.tensor_scalar(A(out), src(), val(s1), val(s2), op0, op1)
+        emit("v", fn, [out], [in0] + cols + ([off] if off else []))
 
-    def tt(out, a, b, op):
-        emit("v", lambda: g.vector.tensor_tensor(A(out), A(a), A(b), op), [out], [a, b])
+    def tt(out, a, b, op, off=None):
+        emit("v", lambda: g.vector.tensor_tensor(A(out), A(a) if off is None else ind(a, off), A(b), op), [out], [a, b] + ([off] if off else []))
 
     def red(out, in_, op):
         emit("v", lambda: g.vector.tensor_reduce(A(out), A(in_), AxisListType.X, op), [out], [in_])
@@ -211,18 +215,17 @@ def rank_program(g, core, T, topo):
         act(so, si, off=off)
 
     others = [d for d in range(N) if d != rank]
-    groups = 2
+    mask3 = 0xFFFF
+    for d in others:
+        mask3 &= topo.mask(core, T.cores[d])
+    groups = bin(mask3).count("1")
 
     def spread(src, sem):
         use("g", [src], [])
-        tx = []
-        for i, d in enumerate(others):
-            dst = T.cores[d]
-            rid, pid = topo.addr(dst)[:2]
-            mask = sum(1 << e for e in topo.engines(core, dst)[groups * i:groups * i + groups])
-            tx.append(RemoteDMATransfer(dst_ids=[DstId(rid=rid, pnc=pid)], dma_engine_mask=mask, remote_sem=T.sem[sem], src=A(src), dst=A(src)))
-        g.remote_dma_fused(tx, local_sem=T.sem.loc)
-        cnt["loc"] = cnt.get("loc", 0) + groups * len(others)
+        ids = [DstId(rid=topo.addr(T.cores[d])[0], pnc=topo.addr(T.cores[d])[1]) for d in others]
+        g.remote_dma_fused([RemoteDMATransfer(dst_ids=ids, dma_engine_mask=mask3, remote_sem=T.sem[sem], srcs=[A(src)], dsts=[A(src) for d in others])],
+                           local_sem=T.sem.loc)
+        cnt["loc"] = cnt.get("loc", 0) + groups
 
     near = [d for d in others if topo.same_plane(topo.chip(core), topo.chip(T.cores[d]))][0]
     pair = sorted([rank, near])
@@ -241,14 +244,12 @@ def rank_program(g, core, T, topo):
         arrives(semc, n, [V(q, K, 2 * K)])
         arrives(sems, n, [V(s, K, 2 * K)])
 
-    def widen(x, c0, c1, on, scale=1.0, bias=0.0):
+    def widen(x, c0, c1, on):
         out, win, off = V("xe", 32 * c0, 32 * c1), V(x, c0, c1), V("cexp", 0, 2 * (c1 - c0))
         if on == "v":
             cp(out, win, off)
-        elif scale == 1.0 and bias == 0.0:
-            act(out, win, off=off)
         else:
-            act(out, win, AF.Identity, off=off, scale=scale, bias=bias)
+            act(out, win, off=off)
 
     def turn(f, c0, c1):
         tr(V(f, 32 * c0, 32 * c1), V("xe", 32 * c0, 32 * c1))
@@ -265,6 +266,8 @@ def rank_program(g, core, T, topo):
         else:
             ts(out, V("sc", a + 15, b, 16), OFFC, ALU.add, float(extra), ALU.add)
 
+    bank = lambda k, w: V("bl", 512 * k, 512 * k + w)
+
     loads = []
     for k in range(8):
         o = V("nbe", 0, 48 - 2 * (k % 2), 1, 16 * k, 16 * k + 16)
@@ -276,6 +279,8 @@ def rank_program(g, core, T, topo):
     iota(V("iu"), [[1, 3], [0, 8]], 0, 0)
     iota(IP(0), [[0, 1]], 0, 1)
     iota(V("iw"), [[1, 32], [0, 2]], 0, 0)
+    iota(V("id16"), [[1, 16]], 128, -1)
+    iota(V("ri"), [[1, 32]], 0, 0)
     cp(V("cu"), V("iu"))
     ts(IP(4), IP(0), 4, ALU.logical_shift_right, 1, ALU.bitwise_and)
     ts(IP(1), IP(0), 15, ALU.bitwise_and)
@@ -284,6 +289,17 @@ def rank_program(g, core, T, topo):
     cp(V("cexp"), V("iw"))
     cp(CF(4), IP(4))
     cp(V("cf", 6, 9), V("ip", 1, 4))
+    ts(OFFC, SCOL, 15.0, ALU.is_lt, -2048.0, ALU.mult)
+    ts(V("id16"), V("id16"), 15, ALU.bitwise_and)
+    ts(V("iw"), V("iw"), 0.0, ALU.mult)
+    ts(OFFM, OFFC, float(-NM), ALU.add)
+    ts(V("d16"), V("id16"), 0.0, ALU.is_equal, -2048.0, ALU.mult)
+    ts(V("d17"), V("id16"), 1.0, ALU.is_equal, 2048.0, ALU.mult)
+    ts(V("crep"), V("iw"), SCOL, ALU.add)
+    tt(V("d16"), V("d16"), V("d17"), ALU.add)
+    cp(V("twice", 0, 2), V("crep", 0, 2))
+    ts(V("twice", 2, 4), V("crep", 0, 2), 16.0, ALU.add)
+    ts(V("d16", 0, 1), V("d16", 0, 1), -4096.0, ALU.add)
     o = 16 * rank
     for e in (0, 1):
         cp(V("nbl", o + e, o + 12, 2, 0, 64), V("nbe", e, 24, 4, 0, 64))
@@ -292,11 +308,14 @@ def rank_program(g, core, T, topo):
     spread(V("nbl", o, o + 16), "nbr")
     arrives("nbr", groups * len(others), [V("nbl", 16 * d, 16 * d + 16) for d in others])
     quant(V("qu"), V("su"), V("ut"))
-    pick(V("qr"), V("sr"), V("qu"), V("su"), V("cu"))
-    quant(V("qc0", 0, M), V("scp0", 0, M), V("xt"))
+    pick(V("qr", 0, 128), V("sr", 0, 128), V("qu"), V("su"), V("cu", 0, 8))
+    act(V("d0"), V("d16"), off=V("crep"))
+    act(V("wn", 0, NM), V("d0"), scale=0.0)
+    act(V("wn", NM, NM + 16), V("d0", 0, 16), scale=0.0)
+    act(V("one"), V("d0", 0, 512), AF.Identity, scale=0.0, bias=1.0)
 
-    def height(out, t, q, s, a):
-        mm(V(out, 0, M), V("qr", 128 * t, 128 * t + 128), V("sr", 128 * t, 128 * t + 128), V(q, a, a + M), V(s, a, a + M), True, True)
+    def height(k, t, q, s, a, n):
+        mm(bank(k, n), V("qr", 128 * t, 128 * t + 128), V("sr", 128 * t, 128 * t + 128), V(q, a, a + n), V(s, a, a + n), True, True)
 
     def share(t):
         spread(V("xh%d" % t, 8 * rank, 8 * rank + 8), "h%d" % t)
@@ -314,49 +333,55 @@ def rank_program(g, core, T, topo):
         for d in others:
             turn("fh", 8 * d, 8 * d + 8)
 
-    height("hp", 0, "qc0", "scp0", 0)
-    tr(V("ht"), V("hp", 0, M))
+    for h in (0, 1):
+        quant(V("qc0", H * h, H * h + H), V("scp0", H * h, H * h + H), V("xt", 4 * H * h, 4 * H * h + 4 * H))
+    for h in (0, 1):
+        height(h, 0, "qc0", "scp0", H * h, H)
+    for h in (0, 1):
+        tr(V("ht", H * h, H * h + H), bank(h, H))
     cp(V("xh0", 8 * rank, 8 * rank + 8), V("ht", 0, M, 32))
     share(0)
     dmas("dw", [("y", A(V("wt")), T.w[:], [V("wt")], [])])
 
-    iota(V("ri"), [[1, 32]], 0, 0)
-    iota(V("id16"), [[1, 16]], 128, -1)
-    iota(V("idf"), [[1, NM + 16]], 0, 0)
     iota(V("sn"), [[16, 16]], M * rank, 0)
     iota(V("ki"), [[16, 16]], 0, 0)
     iota(V("s80"), [[16, 8]], 0, 0)
+    iota(V("idf"), [[1, NM]], 0, 0)
     iota(V("io2"), [[1, M]], NM, 0)
     own_f(0)
     for k in range(J):
         for e in (0, 1):
             a = 32 * k + 8 * rank
             cp(V("lnb", a + e, a + 8, 2), V("nbe", 16 * k + e, 16 * k + 16, 4))
-    fill(V("one"), 1.0)
-    ts(OFFC, SCOL, 15.0, ALU.is_lt, -2048.0, ALU.mult)
-    ts(V("id16"), V("id16"), 15, ALU.bitwise_and)
-    ts(V("iw"), V("iw"), 0.0, ALU.mult)
-    ts(OFFM, OFFC, float(-NM), ALU.add)
-    ts(V("d16"), V("id16"), 0.0, ALU.is_equal, -2048.0, ALU.mult)
-    ts(V("d17"), V("id16"), 1.0, ALU.is_equal, 2048.0, ALU.mult)
-    ts(V("crep"), V("iw"), SCOL, ALU.add)
-    tt(V("d16"), V("d16"), V("d17"), ALU.add)
-    fill(V("one32"), 1.0)
-    ts(V("d16", 0, 1), V("d16", 0, 1), -4096.0, ALU.add)
-    act(V("wn"), V("idf"), scale=0.0)
     for b in range(4):
         blk = V("wn", p0=32 * b, p1=32 * b + 32)
         select(blk, blk, [[1, NM + 16]], ALU.not_equal, 1.0, -(8 * b + 8), -32)
         select(blk, blk, [[1, NM + 16]], ALU.not_equal, 2048.0, -(8 * b + 9), -32)
     for b in range(4):
         select(V("et", 512 * b, 512 * b + 512), V("one"), [[1, 512]], ALU.is_equal, 0.0, -b, -4)
-    ts(CF(11), LCOL, 32.0, ALU.mult)
-    ts(CF(10), LCOL, -1.0, ALU.mult, float(NM), ALU.add)
+    ts(BETA, LCOL, float(NTS), ALU.is_lt, NM / 2.0, ALU.mult)
+    fill(V("one32"), 1.0)
     ts(V("mlt"), V("ri"), LCOL, ALU.is_gt)
-    ts(CF(12), BCOL, 8.0, ALU.mult, CF(11), ALU.add)
+    ts(IP(6), IP(2), 7, ALU.bitwise_and)
+    ts(IP(7), IP(1), 3, ALU.logical_shift_right)
+    ts(IP(8), IP(1), 7, ALU.bitwise_and)
+    ts(V("alp"), V("one32"), BETA, ALU.mult, -1.0 / NM, ALU.mult)
+    ts(CF(9), IP(6), 32.0, ALU.mult, float(BIGR), ALU.add)
+    tt(IP(9), IP(3), IP(7), ALU.subtract)
+    cp(CF(20), IP(8))
+    ts(V("alp"), V("alp"), 1.0, ALU.add)
+    ts(V("rest"), V("ri"), CF(9), ALU.add)
+    ts(IP(10), IP(9), 4.0, ALU.add)
+    ts(IP(11), IP(9), 2.0, ALU.add)
+    ts(V("sn"), V("sn"), SCOL, ALU.add)
+    ts(V("ip", 12, 14), V("ip", 10, 12), 3, ALU.bitwise_and)
+    ts(V("ki"), V("ki"), SCOL, ALU.add)
+    cp(V("rest2"), V("rest"), V("twice"))
+    ts(V("rotl"), V("ip", 12, 14), 8.0, ALU.mult, CF(20), ALU.add)
+    ts(V("s80"), V("s80"), SCOL, ALU.add)
+    fill(V("ypd"), 0.0)
+    ts(CF(10), LCOL, -1.0, ALU.mult, float(NM), ALU.add)
     ts(V("cn", 96, 128), V("ri"), -32.0, ALU.mult, CF(10), ALU.add)
-    for k in (6, 7):
-        ts(CF(10 + k), CF(12), float(k), ALU.add)
 
     dmas("dswap", [("y", A(V("nbw", p0=0, p1=64)), A(V("nbl", p0=64, p1=128)), [V("nbw", p0=0, p1=64)], [V("nbl", p0=64, p1=128)]),
                    ("y", A(V("nbw", p0=64, p1=128)), A(V("nbl", p0=0, p1=64)), [V("nbw", p0=64, p1=128)], [V("nbl", p0=0, p1=64)])])
@@ -372,39 +397,16 @@ def rank_program(g, core, T, topo):
     others_f(0)
     lists("nbw", 64, 0)
 
-    def around(win, mid=None):
-        cuts = ((384, 1024), (1024, 1536))
+    cuts = ((384, 896), (896, 1280), (1280, 1536))
+
+    def around(win, mid):
         for a, b in cuts:
             act(V("ra", a, b), win, off=V("lnb", a // 16, b // 16))
         cp(V("ra", 0, 384), win, V("lnb", 0, 24))
-        tr(V("rb", 0, 384), V("ra", 0, 384))
-        tr(V("rb", 384, 1024), V("ra", 384, 1024))
-        if mid:
-            mid()
-        tr(V("rb", 1024, 1536), V("ra", 1024, 1536))
-
-    around(V("idf", 0, NM))
-    ts(V("cn", 0, 96), V("rb", 0, 1536, 16), -1.0, ALU.mult, float(NM), ALU.add)
-
-    def late():
-        ts(BETA, LCOL, float(NTS), ALU.is_lt, NM / 2.0, ALU.mult)
-        ts(IP(6), IP(2), 7, ALU.bitwise_and)
-        ts(IP(7), IP(1), 3, ALU.logical_shift_right)
-        ts(IP(8), IP(1), 7, ALU.bitwise_and)
-        ts(V("alp"), V("one32"), BETA, ALU.mult, -1.0 / NM, ALU.mult)
-        ts(CF(9), IP(6), 32.0, ALU.mult, float(BIGR), ALU.add)
-        tt(IP(9), IP(3), IP(7), ALU.subtract)
-        cp(CF(20), IP(8))
-        ts(V("alp"), V("alp"), 1.0, ALU.add)
-        ts(V("rest"), V("ri"), CF(9), ALU.add)
-        ts(IP(10), IP(9), 4.0, ALU.add)
-        ts(IP(11), IP(9), 2.0, ALU.add)
-        ts(V("sn"), V("sn"), SCOL, ALU.add)
-        ts(V("ip", 12, 14), V("ip", 10, 12), 3, ALU.bitwise_and)
-        ts(V("ki"), V("ki"), SCOL, ALU.add)
-        ts(V("rotl"), V("ip", 12, 14), 8.0, ALU.mult, CF(20), ALU.add)
-        ts(V("s80"), V("s80"), SCOL, ALU.add)
-        fill(V("ypd"), 0.0)
+        for a, b in ((0, 384),) + cuts[:2]:
+            tr(V("rb", a, b), V("ra", a, b))
+        mid()
+        tr(V("rb", *cuts[2]), V("ra", *cuts[2]))
 
     b1, b2 = CUT1, CUT2
     win3 = ["fa", "fb", "fc"]
@@ -425,51 +427,67 @@ def rank_program(g, core, T, topo):
 
         around(V("fh"), mid)
         if not t:
-            act(V("d0"), V("d16"), off=V("crep"))
+            for a, b in ((0, 512), (512, 1024), (1024, 1536)):
+                act(V("rc", a, b), V("idf"), off=V("lnb", a // 16, b // 16))
         tt(V("mm"), V("m1"), nbh[2], ALU.max)
         for k in range(J + 1):
             tt(V("eq4", 32 * k, 32 * k + 32), nbh[k], V("mm"), ALU.is_equal)
+        if not t:
+            for a, b in ((0, 512), (512, 1024), (1024, 1536)):
+                tr(V("rd", a, b), V("rc", a, b))
+            ts(V("cn", 0, 96), V("rd", 0, 1536, 16), -1.0, ALU.mult, float(NM), ALU.add)
         tt(V("b4"), V("eq4"), V("cn"), ALU.mult)
         tt(V("b2"), V("b4", 0, 64), V("b4", 64, 128), ALU.max)
         tt(V("b1"), V("b2", 0, 32), V("b2", 32, 64), ALU.max)
-        for a, b in ((0, 16), (16, 24), (24, 32)):
-            widen("b1", a, b, "s", -1.0, float(NM))
-        ts(V("nx"), V("b1"), -1.0, ALU.mult, float(NM), ALU.add)
-        tr(V("tn"), V("nx"))
-        for a in (0, 16, 32, 48):
-            cp(V("zz", a, a + 16), V("tn", a // 32 * 16, a // 32 * 16 + 16))
+        wide = lambda a, b: (V("xe", 32 * a, 32 * b), V("b1"), V("cexp", 2 * a, 2 * b))
+        for a, b in ((0, 12), (12, 20), (20, 26)):
+            out, win, off = wide(a, b)
+            act(out, win, AF.Identity, off=off, scale=-1.0, bias=float(NM))
+        tr(V("tn"), V("b1"))
+        out, win, off = wide(26, 32)
+        ts(out, win, -1.0, ALU.mult, float(NM), ALU.add, off)
+        cp(V("zz"), V("tn"), V("twice"))
+        turn("fa", 26, 32)
         tr(V("zt"), V("zz"))
+        turn("fa", 0, 12)
         for e in (0, 1):
-            cp(V("la", e, 64, 2), V("zt", 32 * e, 32 * e + 32))
-        for a, b in ((0, 16), (16, 24), (24, 32)):
-            turn("fa", a, b)
+            ts(V("la", e, 64, 2), V("zt", 32 * e, 32 * e + 32), -1.0, ALU.mult, float(NM), ALU.add)
+        turn("fa", 12, 20)
+        turn("fa", 20, 26)
         for k in range(10):
             fi, fo, li, lw = win3[k % 3], win3[(k + 1) % 3], lst3[k % 3], lst3[(k + 1) % 3]
-            act(V(fo, 0, b1), V(fi), off=V(li, 0, b1 // 16))
             act(V(fo, b1, b2), V(fi), off=V(li, b1 // 16, b2 // 16))
-            cp(V(fo, b2, NM), V(fi), V(li, b2 // 16, 64))
-            for a, b in ((0, b1), (b1, NM)):
-                lift(fo, a, b)
-                if k < 9:
-                    listed(V(lw, a // 16, b // 16), a, b)
-                else:
-                    listed(V("l0", a // 16, b // 16), a, b, 8)
-                    act(V("trs", 0, b - a), V("wn"), off=V("l0", a // 16, b // 16), accum=ACC(3 * (a > 0)))
+            cp(V(fo, 0, b1), V(fi), V(li, 0, b1 // 16))
+            if k:
+                listed(V(li, b2 // 16, 64), b2, NM)
+            act(V(fo, b2, NM), V(fi), off=V(li, b2 // 16, 64))
+            lift(fo, 0, b1)
+            lift(fo, b1, b2)
+            if k < 9:
+                listed(V(lw, 0, b2 // 16), 0, b2)
+            else:
+                listed(V("l0", 0, b2 // 16), 0, b2, 8)
+            lift(fo, b2, NM)
         ff = win3[10 % 3]
-        for j in (1, 2):
-            listed(V("l%d" % j), 0, NM, 8 - 2 * j)
-            act(V("trs"), V("wn"), off=V("l%d" % j), accum=ACC(j))
+        act(V("trs", 0, b2), V("wn"), off=V("l0", 0, b2 // 16), accum=ACC(0))
+        listed(V("l3"), 0, NM, 2)
+        listed(V("l0", b2 // 16, 64), b2, NM, 8)
+        act(V("trs", 0, NM - b2), V("wn"), off=V("l0", b2 // 16, 64), accum=ACC(4))
+        listed(V("l1"), 0, NM, 6)
+        act(V("trs"), V("wn"), off=V("l1"), accum=ACC(1))
+        listed(V("l2"), 0, NM, 4)
+        act(V("trs", 0, CUT3), V("wn"), off=V("l2", 0, CUT3 // 16), accum=ACC(2))
+        cp(V("dvs"), V("wn"), V("l3"))
+        cp(V("dvt"), V("wn"), V("l2", CUT3 // 16, 64))
+        red(ACC(3), V("dvs"), ALU.add)
+        red(ACC(6), V("dvt"), ALU.add)
         row = V(ff, lo, lo + M, 1, 0, 1)
         dmas("drt", [("y", T.rt[0:1, M * t:M * t + M], A(row), [], [row])])
-        ts(V("eqa"), V(ff), CF(16), ALU.is_equal)
-        ts(V("eqb"), V(ff), CF(17), ALU.is_equal)
-        red(V("sz8", 6, 7), V("eqa"), ALU.add)
-        tt(ACC(0), ACC(0), ACC(3), ALU.add)
-        red(V("sz8", 7, 8), V("eqb"), ALU.add)
-        ts(V("aci", 0, 3), V("acc", 0, 3), 1.0 / 2048.0, ALU.mult, -0.499, ALU.add)
-        for j in range(3):
-            ts(V("sz8", 2 * j, 2 * j + 1), V("aci", j, j + 1), -2048.0, ALU.mult, ACC(j), ALU.add)
-        cp(V("sz8", 1, 6, 2), V("aci", 0, 3))
+        tt(V("acc", 0, 4, 2), V("acc", 0, 4, 2), V("acc", 4, 8, 2), ALU.add)
+        ts(V("aci"), V("acc", 0, 4), 1.0 / 2048.0, ALU.mult, -0.499, ALU.add)
+        ts(V("t2", 0, 4), V("aci"), -2048.0, ALU.mult)
+        cp(V("sz8", 1, 8, 2), V("aci"))
+        tt(V("sz8", 0, 8, 2), V("t2", 0, 4), V("acc", 0, 4), ALU.add)
         moves = []
         for i in (1, 2, 3):
             c = 32 * i
@@ -478,8 +496,6 @@ def rank_program(g, core, T, topo):
                 moves.append((qn, A(o), A(s), [o], [s]))
         dmas("drot", moves)
         cp(V("rot", 0, 8), V("sz8"))
-        if not t:
-            late()
         listed(V("rho", 0, 16), lo, lo + M)
         listed(V("lro"), lo, lo + M)
         cp(V("rhi"), V("rho", 0, 16))
@@ -500,36 +516,28 @@ def rank_program(g, core, T, topo):
         red(COL(0), V("ytr"), ALU.add)
         ts(V("a1"), V("alp"), COL(0), ALU.mult, BETA, ALU.add)
         tr(V("cs"), V("a1"))
-        act(V("trs", 0, 32), V("cs"), AF.Sign, bias=0.5 - K, accum=ACC(4))
+        act(V("trs", 0, 32), V("cs"), AF.Sign, bias=0.5 - K, accum=V("thr", 0, 1))
         ts(V("f2"), V("cs"), float(K), ALU.is_ge, 2048.0, ALU.mult)
+        gt, eq, thr = V("ge", 0, 32), V("ge", 32, 64), V("thr", 0, 1)
+        ts(gt, V("szs"), thr, ALU.is_gt)
+        ts(eq, V("szs"), thr, ALU.is_equal)
         tt(V("g1"), V("cs"), V("f2"), ALU.subtract)
-        gt, eq = V("ge", 0, 32), V("ge", 32, 64)
-        ts(gt, V("szs"), ACC(4), ALU.is_gt)
-        ts(eq, V("szs"), ACC(4), ALU.is_equal)
-        red(COL(2), V("g1"), ALU.max)
         scan(V("inc", 0, 32), V("one32"), gt, ALU.mult, ALU.add)
         scan(V("inc", 32, 64), V("one32"), eq, ALU.mult, ALU.add)
-        tt(V("nr"), gt, eq, ALU.add)
+        red(COL(2), V("g1"), ALU.max)
         ts(V("a2", 0, 32), V("mlt"), V("inc", 31, 32), ALU.mult)
         ts(V("a2", 32, 64), V("mlt"), V("inc", 63, 64), ALU.mult)
-        ts(V("nr"), V("nr"), -1.0, ALU.mult, 1.0, ALU.add)
+        ts(V("hh"), V("ge"), -BIG - 1.0, ALU.mult, BIG, ALU.add)
         tr(V("a2t"), V("a2"))
-        tt(V("ie"), V("inc"), V("ge"), ALU.subtract)
-        ts(V("e4"), eq, -LOW, ALU.mult)
+        tt(V("je"), V("inc"), V("hh"), ALU.add)
         red(COL(3), V("a2t", 0, 32), ALU.add)
         red(COL(5), V("a2t", 32, 64), ALU.add)
-        tt(V("nr"), V("nr"), V("rest"), ALU.mult)
-        ts(V("ne"), eq, LOW, ALU.mult, -LOW, ALU.add)
-        tt(V("e4"), V("e4"), V("ie", 0, 32), ALU.add)
-        tt(V("je"), V("ne"), V("ie", 32, 64), ALU.add)
-        tt(V("jg"), V("e4"), V("nr"), ALU.add)
-        ts(V("ue"), V("je"), COL(5), ALU.add, COL(2), ALU.add)
-        ts(V("ug"), V("jg"), COL(3), ALU.add)
-        for a in (0, 16, 32, 48):
-            h = a // 32 * 16
-            tt(V("zz", a, a + 16), V("ug", h, h + 16), V("ue", h, h + 16), ALU.max)
+        ts(V("ug"), V("je", 0, 32), COL(3), ALU.add)
+        ts(V("ue"), V("je", 32, 64), COL(5), ALU.add, COL(2), ALU.add)
+        tt(V("um"), V("ug"), V("ue"), ALU.min)
+        tt(V("zz"), V("um"), V("rest2"), ALU.min, V("twice"))
         tr(V("zt"), V("zz"))
-        tt(V("slot"), V("ug"), V("ue"), ALU.max)
+        tt(V("slot"), V("um"), V("rest"), ALU.min)
         for e in (0, 1):
             cp(V("sll", e, 16, 2), V("zt", 32 * e + 8 * rank, 32 * e + 8 * rank + 8))
         tr(V("sx"), V("slot"))
@@ -563,46 +571,58 @@ def rank_program(g, core, T, topo):
         tt(V("rho", 48, 64), V("rho", 48, 64), V("ki"), ALU.add)
         cp(V("kl"), V("rho", 48, 64))
         if not t:
+            pick(V("qr", 128, 384), V("sr", 128, 384), V("qu"), V("su"), V("cu", 8, 24))
             quant(V("qe"), V("se"), V("et"))
             quant(V("qw"), V("sw"), V("wt"))
         if t + 1 < R:
-            height("yp", t + 1, qc, sp, 0)
-        for b in range(4):
-            mm(V("bl", 512 * b, 512 * b + M), V("qe", 128 * b, 128 * b + 128), V("se", 128 * b, 128 * b + 128), V(qc, 0, M), V(sp, 0, M), True, False)
-        if t + 1 < R:
-            tr(V("ho"), V("yp", 0, M))
+            height(7, t + 1, qc, sp, 0, M)
+            tr(V("ho"), bank(7, M))
             m0, m1 = V("rho", 16, 32, 2), V("rho", 17, 32, 2)
             tt(V("mx"), m1, m0, ALU.subtract)
             ts(V("mx"), V("mx"), HCOL, ALU.mult)
             tt(V("mx"), V("mx"), m0, ALU.add)
             ts(V("mx1"), V("mx"), -1.0, ALU.mult, 1.0, ALU.add)
             tt(V("xo"), V("ho", 0, M, 32), V("mx1"), ALU.mult)
-        pick(V("qp%d" % t), V("sp%d" % t), V(qb), V(sb), V("pl"))
-        for b in range(4):
-            mm(V("bl", 512 * b, 512 * b + M), V("qe", 128 * b, 128 * b + 128), V("se", 128 * b, 128 * b + 128), V("qp%d" % t), V("sp%d" % t), False, True)
-        for b in range(4):
-            src, out = V("bl", 512 * b, 512 * b + M), V("hb", b, 4 * M, 4)
-            if b % 2:
-                act(out, src, scale=0.5)
-            else:
-                ts(out, src, 0.5, ALU.mult)
-        quant(V(qc, M, 2 * M), V(sp, M, 2 * M), V("hb"))
+        unpack = [(V("qe", 128 * b, 128 * b + 128), V("se", 128 * b, 128 * b + 128)) for b in range(4)]
+        half = [(H * h, H * h + H) for h in (0, 1)]
+        qp, pp = "qp%d" % t, "sp%d" % t
+        for h in (0, 1):
+            for b in range(4):
+                mm(bank(4 * h + b, H), *unpack[b], V(qc, *half[h]), V(sp, *half[h]), True, False)
+        for h in (0, 1):
+            pick(V(qp, *half[h]), V(pp, *half[h]), V(qb), V(sb), V("pl", 8 * h, 8 * h + 8))
+        for h in (0, 1):
+            for b in range(4):
+                mm(bank(4 * h + b, H), *unpack[b], V(qp, *half[h]), V(pp, *half[h]), False, True)
+        for h in (0, 1):
+            for b in range(4):
+                src, out = bank(4 * h + b, H), V("hb", 4 * H * h + b, 4 * H * h + 4 * H, 4)
+                if b % 2:
+                    act(out, src, scale=0.5)
+                else:
+                    ts(out, src, 0.5, ALU.mult)
+            quant(V(qc, M + H * h, M + H * h + H), V(sp, M + H * h, M + H * h + H), V("hb", 4 * H * h, 4 * H * h + 4 * H))
+            if t + 1 < R:
+                height(h, t + 1, qc, sp, M + H * h, H)
+        nq, ns = "qc%d" % (t + 1), "scp%d" % (t + 1)
         if t + 1 < R:
-            height("hp", t + 1, qc, sp, M)
-            tr(V("ht"), V("hp", 0, M))
+            for h in (0, 1):
+                tr(V("ht", *half[h]), bank(h, H))
             tt(V("xm"), V("ht", 0, M, 32), V("mx"), ALU.mult)
             tt(V("xh%d" % (t + 1), 8 * rank, 8 * rank + 8), V("xm"), V("xo"), ALU.add)
             share(t + 1)
-        pick(V("qc%d" % (t + 1), 0, M), V("scp%d" % (t + 1), 0, M), V(qc), V(sp), V("kl"))
+            pick(V(nq, 0, M), V(ns, 0, M), V(qc), V(sp), V("kl"))
 
-    qc, sp = V("qc%d" % R), V("scp%d" % R)
-    mm(V("yp", 0, M), V("qw"), V("sw"), qc, sp, True, True)
-    outs = [("y", T.oc[:], A(qc).bitcast(dt.uint8), [], [qc])]
+    outs = []
+    for h in (0, 1):
+        pick(V(nq, *half[h]), V(ns, *half[h]), V(qc, 0, M + H * h + H), V(sp, 0, M + H * h + H), V("kl", 8 * h, 8 * h + 8))
+        mm(bank(h, H), V("qw"), V("sw"), V(nq, *half[h]), V(ns, *half[h]), True, True)
+        cp(V("ys", *half[h]), bank(h, H))
+        outs.append(("y", T.oc[:, 4 * H * h:4 * H * h + 4 * H], A(V(nq, *half[h])).bitcast(dt.uint8), [], [V(nq, *half[h])]))
+        outs.append(("s" if h else "y", T.y[:, H * h:H * h + H], A(V("ys", *half[h])), [], [V("ys", *half[h])]))
     for k in range(4):
-        o = V("scp%d" % R, 0, M, 1, 32 * k, 32 * k + 4)
+        o = V(ns, 0, M, 1, 32 * k, 32 * k + 4)
         outs.append(("y", T.osc[4 * k:4 * k + 4, 0:M], A(o), [], [o]))
-    cp(V("ys"), V("yp", 0, M))
-    outs.append(("s", T.y[:], A(V("ys")), [], [V("ys")]))
     dmas("dout", outs)
     for sem in sorted(cnt):
         g.sync.wait_ge(T.sem[sem], cnt[sem])

@@ -13,8 +13,14 @@ NTS = 8
 BIG = 4.0 * NM
 BIGR = NM + K
 WINV = BIGR + M + K
-CUT1, CUT2 = 160, 640
-CUT3 = 672
+RUNS = ((0, 128, 0, 4), (128, 256, 512, 2), (256, 768, 768, 1), (768, 896, 1280, 2), (896, 1024, 1536, 4))
+WS, MID = 2048, 1024.0
+TOP = 1100.0
+UP = float(2 ** 30)
+VPART = ((0, 128), (128, 256), (256, 288))
+SPART = ((288, 768), (768, 896), (896, 1024))
+SCUT = SPART[0][1]
+CUT3 = 512
 C8, U8, F32, B16, I32, U16 = "float8_e4m3fn_x4", "uint8", "float32", "bfloat16", "int32", "uint16"
 
 SCRATCH = {
@@ -22,32 +28,34 @@ SCRATCH = {
     "qu": ("sbuf", [128, 128], C8), "su": ("sbuf", [128, 128], U8),
     "qw": ("sbuf", [128, 128], C8), "sw": ("sbuf", [128, 128], U8),
     "qr": ("sbuf", [128, 384], C8), "sr": ("sbuf", [128, 384], U8),
-    "one": ("sbuf", [128, 512], B16), "et": ("sbuf", [128, 2048], B16),
+    "one": ("sbuf", [128, NM], B16), "et": ("sbuf", [128, 2048], B16),
     "qe": ("sbuf", [128, 512], C8), "se": ("sbuf", [128, 512], U8),
     "bl": ("psum", [128, 4096], F32),
-    "d0": ("sbuf", [128, NM], F32), "idf": ("sbuf", [128, NM], F32), "io2": ("sbuf", [128, M], F32),
-    "wn": ("sbuf", [128, NM + 16], F32),
-    "xe": ("sbuf", [128, NM], F32), "fh": ("sbuf", [128, NM], F32), "fs": ("sbuf", [128, NM], F32),
-    "fa": ("sbuf", [128, NM], F32), "fb": ("sbuf", [128, NM], F32), "fc": ("sbuf", [128, NM], F32),
-    "la": ("sbuf", [128, 64], U16), "lb": ("sbuf", [128, 64], U16), "lc": ("sbuf", [128, 64], U16),
-    "l0": ("sbuf", [128, 64], U16), "l1": ("sbuf", [128, 64], U16), "l2": ("sbuf", [128, 64], U16), "l3": ("sbuf", [128, 64], U16),
-    "sc": ("sbuf", [128, NM], F32), "ra": ("sbuf", [128, 1536], F32), "rb": ("sbuf", [128, 1536], F32),
-    "rc": ("sbuf", [128, 1536], F32), "rd": ("sbuf", [128, 1536], F32),
+    "d0": ("sbuf", [128, 512], B16), "io2": ("sbuf", [128, M], F32),
+    "dg": ("sbuf", [128, NM], B16), "dw": ("sbuf", [128, NM], B16), "wb": ("sbuf", [128, NM + 16], B16),
+    "w0": ("sbuf", [128, WS], B16), "w1": ("sbuf", [128, WS], B16), "w2": ("sbuf", [128, WS], B16), "w3": ("sbuf", [128, WS], B16),
+    "idn": ("sbuf", [128, WS], F32), "rtf": ("sbuf", [128, M], F32),
+    "xe": ("sbuf", [128, NM], F32), "xb": ("sbuf", [128, NM], B16), "fh": ("sbuf", [128, NM], F32), "fs": ("sbuf", [128, WS], B16),
+    "fa": ("sbuf", [128, WS], B16), "fb": ("sbuf", [128, WS], B16), "fc": ("sbuf", [128, WS], B16),
+    "la": ("sbuf", [128, 64], U16), "lb": ("sbuf", [128, 64], U16), "lc": ("sbuf", [128, 64], U16), "l0": ("sbuf", [128, 64], U16),
+    "sc": ("sbuf", [128, NM], B16), "scf": ("sbuf", [128, 128], F32), "ra": ("sbuf", [128, 1536], F32), "rb": ("sbuf", [128, 1536], F32),
     "trs": ("sbuf", [128, NM], F32), "dvs": ("sbuf", [128, NM], F32), "dvt": ("sbuf", [128, NM - CUT3], F32),
-    "ht": ("sbuf", [128, M], F32), "ho": ("sbuf", [128, M], F32), "rs": ("sbuf", [128, M], F32), "inv": ("sbuf", [128, WINV], F32),
+    "ht": ("sbuf", [128, M], F32), "ho": ("sbuf", [128, M], F32), "rs": ("sbuf", [128, M], B16), "inv": ("sbuf", [128, WINV], F32),
     "iw": ("sbuf", [128, 64], I32), "iu": ("sbuf", [128, 24], I32), "id16": ("sbuf", [128, 16], I32),
     "cm": ("sbuf", [128, 32 * NTH], F32),
     "nbe": ("sbuf", [128, 48], I32), "nbl": ("sbuf", [128, 64], U16), "nbw": ("sbuf", [128, 64], U16), "lnb": ("sbuf", [128, 96], U16),
+    "lnw": ("sbuf", [128, 96], U16),
     "sz8": ("sbuf", [128, 8], F32), "rot": ("sbuf", [128, 32], F32), "acc": ("sbuf", [128, 8], F32), "ypd": ("sbuf", [128, 32], F32),
     "szs": ("sbuf", [128, 32], F32), "hb": ("sbuf", [128, 4 * M], B16), "ys": ("sbuf", [128, M], F32),
 }
 SMALL = {
     "zf": (F32, {"d16": 16, "d17": 16, "cf": 32, "ri": 32, "mlt": 32, "rest": 32, "rest2": 64, "alp": 32, "one32": 32, "cn": 128, "sn": 16, "ki": 16, "s80": 8,
+                 "nn": 128, "nm": 96, "n1": 128, "n2": 128, "n3": 128, "n4": 128,
                  "m1": 32, "mm": 32, "eq4": 128, "b4": 128, "b2": 64, "b1": 32, "tn": 32, "zz": 64, "zt": 64, "thr": 8, "t2": 8,
                  "ytr": 32, "col": 8, "a1": 32, "cs": 32, "f2": 32, "g1": 32, "ge": 64, "inc": 64, "hh": 64, "je": 64, "a2": 64, "a2t": 64,
                  "ug": 32, "ue": 32, "um": 32, "slot": 32, "sx": 32,
                  "rho": 64, "j2f": 8, "mx": 8, "mx1": 8, "xo": 8, "xm": 8}),
-    "zi": (I32, {"ip": 16, "aci": 4, "rhi": 16}),
+    "zi": (I32, {"ip": 16, "aci": 4}),
     "zu": (U16, {"cexp": 64, "crep": 64, "cu": 24, "twice": 4, "rotl": 2, "lro": 16, "sll": 16, "j1": 6, "j2": 6, "pl": 16, "kl": 16}),
 }
 AT = {}
@@ -70,7 +78,14 @@ for _t in range(R + 1):
 
 SEMAPHORES = (["ev", "es", "et", "eg", "loc", "nbr"] + ["h%d" % t for t in range(R)]
               + ["%s%d" % (k, t) for t in range(R) for k in ("ac", "as", "bc", "bs")]
-              + ["dx", "du", "dw", "dnb", "dswap", "drot", "drt", "dout"])
+              + ["dx", "du", "dw", "dnb", "dswap", "dnum", "drot", "drt", "dout"])
+
+
+def place(n):
+    for n0, n1, c, s in RUNS:
+        if n0 <= n < n1:
+            return c + s * (n - n0)
+    return WS
 
 
 def rank_program(g, core, T, topo):
@@ -120,7 +135,8 @@ def rank_program(g, core, T, topo):
     def mark(sem, val, reads, writes):
         reads, writes = split(reads, writes)
         for r in writes:
-            hist[r[0]] = [h for h in hist.get(r[0], []) if not (r[3] == 1 and r[1] <= h[0][1] and h[0][2] <= r[2] and r[4] <= h[0][4] and h[0][5] <= r[5])]
+            hist[r[0]] = [h for h in hist.get(r[0], [])
+                          if not ((r[3] == 1 or h[0] == r) and r[1] <= h[0][1] and h[0][2] <= r[2] and r[4] <= h[0][4] and h[0][5] <= r[5])]
         for r, w in [(r, False) for r in reads] + [(r, True) for r in writes]:
             hist.setdefault(r[0], []).append((r, w, sem, val))
 
@@ -186,13 +202,17 @@ def rank_program(g, core, T, topo):
     def fill(out, c):
         emit("v", lambda: g.vector.memset(A(out), c), [out], [])
 
-    def act(out, in_, func=AF.Copy, off=None, accum=None, **kw):
+    def act(out, in_, func=AF.Copy, off=None, accum=None, scale=None, **kw):
         src = lambda: A(in_) if off is None else ind(in_, off)
+        cols = [scale] if isinstance(scale, tuple) else []
         def fn():
-            if accum is None:
-                return g.scalar.activation(A(out), src(), func, **kw)
-            return g.scalar.activation(A(out), src(), func, accum_out=A(accum), **kw)
-        emit("s", fn, [out] + ([accum] if accum else []), [in_] + ([off] if off else []))
+            k2 = dict(kw)
+            if scale is not None:
+                k2["scale"] = A(scale) if cols else scale
+            if accum is not None:
+                k2["accum_out"] = A(accum)
+            return g.scalar.activation(A(out), src(), func, **k2)
+        emit("s", fn, [out] + ([accum] if accum else []), [in_] + cols + ([off] if off else []))
 
     def iota(out, pattern, base, cm):
         if SCRATCH[out[0]][2] == I32:
@@ -244,8 +264,8 @@ def rank_program(g, core, T, topo):
         arrives(semc, n, [V(q, K, 2 * K)])
         arrives(sems, n, [V(s, K, 2 * K)])
 
-    def widen(x, c0, c1, on):
-        out, win, off = V("xe", 32 * c0, 32 * c1), V(x, c0, c1), V("cexp", 0, 2 * (c1 - c0))
+    def widen(x, c0, c1, on, to="xe"):
+        out, win, off = V(to, 32 * c0, 32 * c1), V(x, c0, c1), V("cexp", 0, 2 * (c1 - c0))
         if on == "v":
             cp(out, win, off)
         else:
@@ -254,17 +274,26 @@ def rank_program(g, core, T, topo):
     def turn(f, c0, c1):
         tr(V(f, 32 * c0, 32 * c1), V("xe", 32 * c0, 32 * c1))
 
+    def run(f, a, b):
+        n0, n1, c, s = [r for r in RUNS if r[0] <= a and b <= r[1]][0]
+        return V(f, c + s * (a - n0), c + s * (b - n0), s)
+
+    def runs(a, b):
+        return [(max(a, r[0]), min(b, r[1])) for r in RUNS if r[0] < b and a < r[1]]
+
+    def turn_s(f, c0, c1):
+        for a, b in runs(32 * c0, 32 * c1):
+            tr(run(f, a, b), V("xb", a, b))
+
     CF = lambda k: V("cf", k, k + 1)
-    OFFC, OFFM, SCOL, LCOL, BCOL, BETA, HCOL = [CF(k) for k in (0, 1, 6, 7, 8, 3, 4)]
+    SCL, HI, LO, SCOL, LCOL, BCOL, BETA, HCOL = [CF(k) for k in (0, 4, 11, 6, 7, 8, 3, 4)]
 
     def lift(f, a, b):
-        scan(V("sc", a, b), V("d0", 0, b - a), V(f, a, b), ALU.add, ALU.max)
+        for x, y in runs(a, b):
+            scan(V("sc", x, y), V("d0", 0, y - x), run(f, x, y), ALU.mult, ALU.add)
 
-    def listed(out, a, b, extra=None):
-        if extra is None:
-            ts(out, V("sc", a + 15, b, 16), OFFC, ALU.add)
-        else:
-            ts(out, V("sc", a + 15, b, 16), OFFC, ALU.add, float(extra), ALU.add)
+    def listed(out, a, b):
+        ts(out, V("sc", a + 15, b, 16), SCL, ALU.mult, MID, ALU.add)
 
     bank = lambda k, w: V("bl", 512 * k, 512 * k + w)
 
@@ -281,6 +310,7 @@ def rank_program(g, core, T, topo):
     iota(V("iw"), [[1, 32], [0, 2]], 0, 0)
     iota(V("id16"), [[1, 16]], 128, -1)
     iota(V("ri"), [[1, 32]], 0, 0)
+    fill(V("one"), 1.0)
     cp(V("cu"), V("iu"))
     ts(IP(4), IP(0), 4, ALU.logical_shift_right, 1, ALU.bitwise_and)
     ts(IP(1), IP(0), 15, ALU.bitwise_and)
@@ -289,17 +319,16 @@ def rank_program(g, core, T, topo):
     cp(V("cexp"), V("iw"))
     cp(CF(4), IP(4))
     cp(V("cf", 6, 9), V("ip", 1, 4))
-    ts(OFFC, SCOL, 15.0, ALU.is_lt, -2048.0, ALU.mult)
     ts(V("id16"), V("id16"), 15, ALU.bitwise_and)
     ts(V("iw"), V("iw"), 0.0, ALU.mult)
-    ts(OFFM, OFFC, float(-NM), ALU.add)
-    ts(V("d16"), V("id16"), 0.0, ALU.is_equal, -2048.0, ALU.mult)
-    ts(V("d17"), V("id16"), 1.0, ALU.is_equal, 2048.0, ALU.mult)
+    ts(SCL, SCOL, 15.0, ALU.is_equal, 1.0 - 1.0 / UP, ALU.mult)
+    ts(V("d16"), V("id16"), 1.0, ALU.is_equal, UP, ALU.mult)
+    ts(V("d17"), V("id16"), 0.0, ALU.is_gt)
     ts(V("crep"), V("iw"), SCOL, ALU.add)
+    ts(SCL, SCL, 1.0 / UP, ALU.max)
     tt(V("d16"), V("d16"), V("d17"), ALU.add)
     cp(V("twice", 0, 2), V("crep", 0, 2))
     ts(V("twice", 2, 4), V("crep", 0, 2), 16.0, ALU.add)
-    ts(V("d16", 0, 1), V("d16", 0, 1), -4096.0, ALU.add)
     o = 16 * rank
     for e in (0, 1):
         cp(V("nbl", o + e, o + 12, 2, 0, 64), V("nbe", e, 24, 4, 0, 64))
@@ -309,10 +338,7 @@ def rank_program(g, core, T, topo):
     arrives("nbr", groups * len(others), [V("nbl", 16 * d, 16 * d + 16) for d in others])
     quant(V("qu"), V("su"), V("ut"))
     pick(V("qr", 0, 128), V("sr", 0, 128), V("qu"), V("su"), V("cu", 0, 8))
-    act(V("d0"), V("d16"), off=V("crep"))
-    act(V("wn", 0, NM), V("d0"), scale=0.0)
-    act(V("wn", NM, NM + 16), V("d0", 0, 16), scale=0.0)
-    act(V("one"), V("d0", 0, 512), AF.Identity, scale=0.0, bias=1.0)
+    act(V("d0"), V("d16"), off=V("crep", 0, 32))
 
     def height(k, t, q, s, a, n):
         mm(bank(k, n), V("qr", 128 * t, 128 * t + 128), V("sr", 128 * t, 128 * t + 128), V(q, a, a + n), V(s, a, a + n), True, True)
@@ -346,22 +372,22 @@ def rank_program(g, core, T, topo):
     iota(V("sn"), [[16, 16]], M * rank, 0)
     iota(V("ki"), [[16, 16]], 0, 0)
     iota(V("s80"), [[16, 8]], 0, 0)
-    iota(V("idf"), [[1, NM]], 0, 0)
+    select(V("dg"), V("one"), [[1, 32], [-1, 32]], ALU.is_equal, 0.0, 0, 0)
     iota(V("io2"), [[1, M]], NM, 0)
+    for n0, n1, c, s in RUNS:
+        iota(V("idn", c, c + s * (n1 - n0), s), [[1, n1 - n0]], n0, 0)
+    ts(CF(12), BCOL, -8.0, ALU.mult, LCOL, ALU.add)
     own_f(0)
+    ts(CF(13), CF(12), 6.0, ALU.is_equal)
+    ts(CF(14), CF(12), 7.0, ALU.is_equal, 2048.0, ALU.mult)
     for k in range(J):
         for e in (0, 1):
             a = 32 * k + 8 * rank
             cp(V("lnb", a + e, a + 8, 2), V("nbe", 16 * k + e, 16 * k + 16, 4))
-    for b in range(4):
-        blk = V("wn", p0=32 * b, p1=32 * b + 32)
-        select(blk, blk, [[1, NM + 16]], ALU.not_equal, 1.0, -(8 * b + 8), -32)
-        select(blk, blk, [[1, NM + 16]], ALU.not_equal, 2048.0, -(8 * b + 9), -32)
-    for b in range(4):
-        select(V("et", 512 * b, 512 * b + 512), V("one"), [[1, 512]], ALU.is_equal, 0.0, -b, -4)
+    tt(CF(15), CF(13), CF(14), ALU.add)
     ts(BETA, LCOL, float(NTS), ALU.is_lt, NM / 2.0, ALU.mult)
     fill(V("one32"), 1.0)
-    ts(V("mlt"), V("ri"), LCOL, ALU.is_gt)
+    fill(V("wb", NM, NM + 16), 0.0)
     ts(IP(6), IP(2), 7, ALU.bitwise_and)
     ts(IP(7), IP(1), 3, ALU.logical_shift_right)
     ts(IP(8), IP(1), 7, ALU.bitwise_and)
@@ -370,18 +396,29 @@ def rank_program(g, core, T, topo):
     tt(IP(9), IP(3), IP(7), ALU.subtract)
     cp(CF(20), IP(8))
     ts(V("alp"), V("alp"), 1.0, ALU.add)
-    ts(V("rest"), V("ri"), CF(9), ALU.add)
     ts(IP(10), IP(9), 4.0, ALU.add)
     ts(IP(11), IP(9), 2.0, ALU.add)
     ts(V("sn"), V("sn"), SCOL, ALU.add)
     ts(V("ip", 12, 14), V("ip", 10, 12), 3, ALU.bitwise_and)
-    ts(V("ki"), V("ki"), SCOL, ALU.add)
-    cp(V("rest2"), V("rest"), V("twice"))
+    ts(LO, HI, -1.0, ALU.mult, 1.0, ALU.add)
     ts(V("rotl"), V("ip", 12, 14), 8.0, ALU.mult, CF(20), ALU.add)
-    ts(V("s80"), V("s80"), SCOL, ALU.add)
     fill(V("ypd"), 0.0)
-    ts(CF(10), LCOL, -1.0, ALU.mult, float(NM), ALU.add)
-    ts(V("cn", 96, 128), V("ri"), -32.0, ALU.mult, CF(10), ALU.add)
+    for h in (0, 1):
+        n0 = M * rank + H * h
+        step = place(n0 + 1) - place(n0)
+        ts(V("sn", 8 * h, 8 * h + 8), V("sn", 8 * h, 8 * h + 8), float(step), ALU.mult, float(place(n0) - step * n0), ALU.add)
+    ts(V("nn", 96, 128), V("ri"), 32.0, ALU.mult, LCOL, ALU.add)
+
+    def coded(a, b):
+        n1, n2, n3, n4, cn = [V(x, a, b) for x in ("n1", "n2", "n3", "n4", "cn")]
+        act(n3, V("nn", a, b), AF.Identity, scale=-4.0, bias=TOP + NM / 2)
+        ts(n1, V("nn", a, b), 896.0, ALU.min, 128.0, ALU.max)
+        ts(n2, V("nn", a, b), 768.0, ALU.min, 256.0, ALU.max)
+        act(n4, n1, scale=2.0)
+        tt(n2, n2, n3, ALU.add)
+        tt(cn, n2, n4, ALU.add)
+
+    coded(96, 128)
 
     dmas("dswap", [("y", A(V("nbw", p0=0, p1=64)), A(V("nbl", p0=64, p1=128)), [V("nbw", p0=0, p1=64)], [V("nbl", p0=64, p1=128)]),
                    ("y", A(V("nbw", p0=64, p1=128)), A(V("nbl", p0=0, p1=64)), [V("nbw", p0=64, p1=128)], [V("nbl", p0=0, p1=64)])])
@@ -396,6 +433,12 @@ def rank_program(g, core, T, topo):
     lists("nbl", 0, 64)
     others_f(0)
     lists("nbw", 64, 0)
+    swaps = []
+    for k in range(8):
+        i = k ^ 1
+        w, r = V("lnw", 0, 96, 1, 16 * k, 16 * k + 16), V("lnb", 0, 96, 1, 16 * i, 16 * i + 16)
+        swaps.append(("y", A(w), A(r), [w], [r]))
+    dmas("dnum", swaps)
 
     cuts = ((384, 896), (896, 1280), (1280, 1536))
 
@@ -408,7 +451,6 @@ def rank_program(g, core, T, topo):
         mid()
         tr(V("rb", *cuts[2]), V("ra", *cuts[2]))
 
-    b1, b2 = CUT1, CUT2
     win3 = ["fa", "fb", "fc"]
     lst3 = ["la", "lb", "lc"]
     lo = M * rank
@@ -427,62 +469,67 @@ def rank_program(g, core, T, topo):
 
         around(V("fh"), mid)
         if not t:
-            for a, b in ((0, 512), (512, 1024), (1024, 1536)):
-                act(V("rc", a, b), V("idf"), off=V("lnb", a // 16, b // 16))
+            act(V("dw"), V("dg"), scale=CF(15))
+            ts(V("nn", 0, 96, 2), V("lnb", 0, 96, 2), LO, ALU.mult)
+            ts(V("nn", 1, 96, 2), V("lnb", 1, 96, 2), HI, ALU.mult)
+            ts(V("nm", 0, 96, 2), V("lnw", 1, 96, 2), HI, ALU.mult)
+            ts(V("nm", 1, 96, 2), V("lnw", 0, 96, 2), LO, ALU.mult)
+            tt(V("nn", 0, 96), V("nn", 0, 96), V("nm"), ALU.add)
+            coded(0, 96)
         tt(V("mm"), V("m1"), nbh[2], ALU.max)
         for k in range(J + 1):
             tt(V("eq4", 32 * k, 32 * k + 32), nbh[k], V("mm"), ALU.is_equal)
-        if not t:
-            for a, b in ((0, 512), (512, 1024), (1024, 1536)):
-                tr(V("rd", a, b), V("rc", a, b))
-            ts(V("cn", 0, 96), V("rd", 0, 1536, 16), -1.0, ALU.mult, float(NM), ALU.add)
         tt(V("b4"), V("eq4"), V("cn"), ALU.mult)
         tt(V("b2"), V("b4", 0, 64), V("b4", 64, 128), ALU.max)
         tt(V("b1"), V("b2", 0, 32), V("b2", 32, 64), ALU.max)
-        wide = lambda a, b: (V("xe", 32 * a, 32 * b), V("b1"), V("cexp", 2 * a, 2 * b))
-        for a, b in ((0, 12), (12, 20), (20, 26)):
+        wide = lambda a, b: (V("xb", 32 * a, 32 * b), V("b1"), V("cexp", 2 * a, 2 * b))
+        for a, b in ((0, 8), (8, 16), (16, 24)):
             out, win, off = wide(a, b)
-            act(out, win, AF.Identity, off=off, scale=-1.0, bias=float(NM))
+            act(out, win, AF.Identity, off=off, scale=-1.0, bias=TOP)
         tr(V("tn"), V("b1"))
-        out, win, off = wide(26, 32)
-        ts(out, win, -1.0, ALU.mult, float(NM), ALU.add, off)
+        out, win, off = wide(24, 32)
+        ts(out, win, -1.0, ALU.mult, TOP, ALU.add, off)
         cp(V("zz"), V("tn"), V("twice"))
-        turn("fa", 26, 32)
+        turn_s("fa", 24, 32)
         tr(V("zt"), V("zz"))
-        turn("fa", 0, 12)
+        turn_s("fa", 0, 8)
         for e in (0, 1):
-            ts(V("la", e, 64, 2), V("zt", 32 * e, 32 * e + 32), -1.0, ALU.mult, float(NM), ALU.add)
-        turn("fa", 12, 20)
-        turn("fa", 20, 26)
+            ts(V("la", e, 64, 2), V("zt", 32 * e, 32 * e + 32), -1.0, ALU.mult, TOP + MID, ALU.add)
+        if not t:
+            tr(V("wb", 0, NM), V("dw"))
+        turn_s("fa", 8, 16)
+        turn_s("fa", 16, 24)
+        if not t:
+            for i in range(4):
+                for n0, n1, c, s in RUNS:
+                    select(V("w%d" % i, c, c + s * (n1 - n0), s), V("wb", n0 + 6 - 2 * i, n1 + 6 - 2 * i), [[0, n1 - n0]], ALU.is_gt, 0.0, 1, 0)
+            for b in range(4):
+                select(V("et", 512 * b, 512 * b + 512), V("one", 0, 512), [[1, 512]], ALU.is_equal, 0.0, -b, -4)
         for k in range(10):
-            fi, fo, li, lw = win3[k % 3], win3[(k + 1) % 3], lst3[k % 3], lst3[(k + 1) % 3]
-            act(V(fo, b1, b2), V(fi), off=V(li, b1 // 16, b2 // 16))
-            cp(V(fo, 0, b1), V(fi), V(li, 0, b1 // 16))
-            if k:
-                listed(V(li, b2 // 16, 64), b2, NM)
-            act(V(fo, b2, NM), V(fi), off=V(li, b2 // 16, 64))
-            lift(fo, 0, b1)
-            lift(fo, b1, b2)
-            if k < 9:
-                listed(V(lw, 0, b2 // 16), 0, b2)
-            else:
-                listed(V("l0", 0, b2 // 16), 0, b2, 8)
-            lift(fo, b2, NM)
-        ff = win3[10 % 3]
-        act(V("trs", 0, b2), V("wn"), off=V("l0", 0, b2 // 16), accum=ACC(0))
-        listed(V("l3"), 0, NM, 2)
-        listed(V("l0", b2 // 16, 64), b2, NM, 8)
-        act(V("trs", 0, NM - b2), V("wn"), off=V("l0", b2 // 16, 64), accum=ACC(4))
-        listed(V("l1"), 0, NM, 6)
-        act(V("trs"), V("wn"), off=V("l1"), accum=ACC(1))
-        listed(V("l2"), 0, NM, 4)
-        act(V("trs", 0, CUT3), V("wn"), off=V("l2", 0, CUT3 // 16), accum=ACC(2))
-        cp(V("dvs"), V("wn"), V("l3"))
-        cp(V("dvt"), V("wn"), V("l2", CUT3 // 16, 64))
+            fi, fo, li = win3[k % 3], win3[(k + 1) % 3], lst3[k % 3]
+            lw = lst3[(k + 1) % 3] if k < 9 else "l0"
+            a, b = SPART[0]
+            act(run(fo, a, b), V(fi), off=V(li, a // 16, b // 16))
+            for j, (a, b) in enumerate(VPART):
+                cp(run(fo, a, b), V(fi), V(li, a // 16, b // 16))
+                if k and not j:
+                    listed(V(li, SCUT // 16, 64), SCUT, NM)
+            for a, b in SPART[1:]:
+                act(run(fo, a, b), V(fi), off=V(li, a // 16, b // 16))
+            for a, b in VPART + SPART[:1]:
+                lift(fo, a, b)
+            listed(V(lw, 0, SCUT // 16), 0, SCUT)
+            for a, b in SPART[1:]:
+                lift(fo, a, b)
+        act(V("trs", 0, SCUT), V("w0"), off=V("l0", 0, SCUT // 16), accum=ACC(0))
+        listed(V("l0", SCUT // 16, 64), SCUT, NM)
+        act(V("trs", 0, NM - SCUT), V("w0"), off=V("l0", SCUT // 16, 64), accum=ACC(4))
+        act(V("trs"), V("w1"), off=V("l0"), accum=ACC(1))
+        act(V("trs", 0, CUT3), V("w2"), off=V("l0", 0, CUT3 // 16), accum=ACC(2))
+        cp(V("dvs"), V("w3"), V("l0"))
+        cp(V("dvt"), V("w2"), V("l0", CUT3 // 16, 64))
         red(ACC(3), V("dvs"), ALU.add)
         red(ACC(6), V("dvt"), ALU.add)
-        row = V(ff, lo, lo + M, 1, 0, 1)
-        dmas("drt", [("y", T.rt[0:1, M * t:M * t + M], A(row), [], [row])])
         tt(V("acc", 0, 4, 2), V("acc", 0, 4, 2), V("acc", 4, 8, 2), ALU.add)
         ts(V("aci"), V("acc", 0, 4), 1.0 / 2048.0, ALU.mult, -0.499, ALU.add)
         ts(V("t2", 0, 4), V("aci"), -2048.0, ALU.mult)
@@ -496,15 +543,27 @@ def rank_program(g, core, T, topo):
                 moves.append((qn, A(o), A(s), [o], [s]))
         dmas("drot", moves)
         cp(V("rot", 0, 8), V("sz8"))
-        listed(V("rho", 0, 16), lo, lo + M)
         listed(V("lro"), lo, lo + M)
-        cp(V("rhi"), V("rho", 0, 16))
+        listed(V("rho", 0, 16), lo, lo + M)
+        act(V("rtf"), V("idn"), off=V("lro"))
+        row = V("rtf", 0, M, 1, 0, 1)
+        dmas("drt", [("y", T.rt[0:1, M * t:M * t + M], A(row), [], [row])])
         tt(V("rho", 16, 32), V("rho", 0, 16), V("sn"), ALU.not_equal)
-        ts(V("rhi"), V("rhi"), 8, ALU.logical_shift_right)
         fill(V("inv", 0, 96), 0.0)
-        ts(V("rho", 32, 48), V("rhi"), float(pair2[0]), ALU.is_equal, float(K), ALU.mult)
-        ts(V("rho", 48, 64), V("rhi"), float(pair2[1]), ALU.is_equal, float(K), ALU.mult)
-        tt(V("rho", 32, 48), V("rho", 32, 48), V("rho", 48, 64), ALU.add)
+        far_in = [float(d in pair2) for d in range(N)]
+        terms = [(ALU.is_lt, M, far_in[0] * K)] + [(ALU.is_ge, M * d, (far_in[d] - (far_in[d - 1] if d > 1 else 0.0)) * K) for d in range(1, N)]
+        terms = [(op, float(place(n)), v) for op, n, v in terms if v]
+        parts = ("m1", "mm")
+        for j, (op, n, v) in enumerate(terms):
+            ts(V("rho", 32, 48) if not j else V(parts[j % 2], 0, 16), V("rho", 0, 16), n, op, v, ALU.mult)
+            if j:
+                tt(V("rho", 32, 48), V("rho", 32, 48), V(parts[j % 2], 0, 16), ALU.add)
+        if not t:
+            ts(V("rest"), V("ri"), CF(9), ALU.add)
+            ts(V("mlt"), V("ri"), LCOL, ALU.is_gt)
+            cp(V("rest2"), V("rest"), V("twice"))
+            ts(V("s80"), V("s80"), SCOL, ALU.add)
+            ts(V("ki"), V("ki"), SCOL, ALU.add)
         for j in range(NTS):
             act(V("trs", 32 * j, 32 * j + 32), V("rot"), AF.Sign, bias=-1.5 - j, accum=V("ypd", j, j + 1))
         act(V("szs"), V("rot"), AF.Identity, off=V("rotl"), scale=2.0, bias=-34.0)
@@ -542,25 +601,25 @@ def rank_program(g, core, T, topo):
             cp(V("sll", e, 16, 2), V("zt", 32 * e + 8 * rank, 32 * e + 8 * rank + 8))
         tr(V("sx"), V("slot"))
         emit("v", lambda: g.vector.tensor_copy(ind(V("inv"), V("sll")), A(V("io2"))), [V("inv")], [V("io2"), V("sll")])
-        widen("sx", 0, 16, "s")
-        lift("inv", 0, K)
-        k5 = V("sc", 15, K, 16)
-        ts(V("j1", 0, 5), k5, OFFM, ALU.add, 0.0, ALU.max)
+        widen("sx", 0, 16, "s", "xb")
+        scan(V("scf", 0, K), V("d0", 0, K), V("inv", 0, K), ALU.mult, ALU.add)
+        k5 = V("scf", 15, K, 16)
+        ts(V("j1", 0, 5), k5, SCL, ALU.mult, float(-NM), ALU.add)
         qa, sa, qb, sb = "qa%d" % t, "sa%d" % t, "qb%d" % t, "sb%d" % t
         pick(V(qa, 0, K), V(sa, 0, K), V(qc, 0, M), V(sp, 0, M), V("j1", 0, 5))
-        widen("sx", 16, 32, "s")
+        widen("sx", 16, 32, "s", "xb")
         swap(qa, sa, near, "ac%d" % t, "as%d" % t)
-        ts(V("j2f", 0, 5), k5, OFFC, ALU.add, float(NM), ALU.is_lt)
-        turn("fs", 0, 16)
+        ts(V("j2f", 0, 5), k5, SCL, ALU.mult, NM - 0.5, ALU.is_lt)
+        turn_s("fs", 0, 16)
         ts(V("j2f", 0, 5), V("j2f", 0, 5), float(K), ALU.mult)
         tt(V("j2f", 0, 5), V("j2f", 0, 5), V("s80", 0, 5), ALU.add)
-        turn("fs", 16, 32)
+        turn_s("fs", 16, 32)
         cp(V("j2", 0, 5), V("j2f", 0, 5))
         cp(V("rs"), V("fs"), V("lro"))
-        scan(V("sc", 0, M), V("d0", 0, M), V("rs"), ALU.add, ALU.max)
+        scan(V("sc", 0, M), V("d0", 0, M), V("rs"), ALU.mult, ALU.add)
         so, me = V("rho", 0, 16), V("rho", 16, 32)
-        listed(so, 0, M)
-        ts(V("rho", 48, 64), so, float(K), ALU.is_lt)
+        ts(so, V("sc", 15, M, 16), SCL, ALU.mult)
+        ts(V("rho", 48, 64), so, K - 0.5, ALU.is_lt)
         tt(me, me, V("rho", 48, 64), ALU.mult)
         tt(so, so, me, ALU.mult)
         tt(V("rho", 32, 48), V("rho", 32, 48), so, ALU.add)

import numpy as np
from concourse.bass import DstId, RemoteDMATransfer
from concourse.mybir import dt, AluOpType, AxisListType, ActivationFunctionType

ALU = AluOpType
AF = ActivationFunctionType
N, M, K, J, R = 4, 256, 80, 3, 3
NM = N * M
H = M // 2
SMAX = NM // K + 1
NTH = SMAX - 1
NTS = 8
BIG = 4.0 * NM
BIGR = NM + K
WINV = BIGR + M + K
RUNS = ((0, 128, 0, 4), (128, 256, 512, 2), (256, 768, 768, 1), (768, 896, 1280, 2), (896, 1024, 1536, 4))
WS, MID = 2048, 1024.0
TOP = 1100.0
UP = float(2 ** 30)
VPART = ((0, 128), (128, 256), (256, 288))
SPART = ((288, 768), (768, 896), (896, 1024))
SCUT = SPART[0][1]
CUT3 = 512
C8, U8, F32, B16, I32, U16 = "float8_e4m3fn_x4", "uint8", "float32", "bfloat16", "int32", "uint16"

SCRATCH = {
    "xt": ("sbuf", [128, 4 * M], B16), "ut": ("sbuf", [128, 512], B16), "wt": ("sbuf", [128, 512], B16),
    "qu": ("sbuf", [128, 128], C8), "su": ("sbuf", [128, 128], U8),
    "qw": ("sbuf", [128, 128], C8), "sw": ("sbuf", [128, 128], U8),
    "qr": ("sbuf", [128, 384], C8), "sr": ("sbuf", [128, 384], U8),
    "one": ("sbuf", [128, NM], B16), "et": ("sbuf", [128, 2048], B16),
    "qe": ("sbuf", [128, 512], C8), "se": ("sbuf", [128, 512], U8),
    "bl": ("psum", [128, 4096], F32),
    "d0": ("sbuf", [128, 512], B16), "io2": ("sbuf", [128, M], F32),
    "dg": ("sbuf", [128, NM], B16), "dw": ("sbuf", [128, NM], B16), "wb": ("sbuf", [128, NM + 16], B16),
    "w0": ("sbuf", [128, WS], B16), "w1": ("sbuf", [128, WS], B16), "w2": ("sbuf", [128, WS], B16), "w3": ("sbuf", [128, WS], B16),
    "idn": ("sbuf", [128, WS], F32), "rtf": ("sbuf", [128, M], F32),
    "xe": ("sbuf", [128, NM], F32), "xb": ("sbuf", [128, NM], B16), "fh": ("sbuf", [128, NM], F32), "fs": ("sbuf", [128, WS], B16),
    "fa": ("sbuf", [128, WS], B16), "fb": ("sbuf", [128, WS], B16), "fc": ("sbuf", [128, WS], B16),
    "la": ("sbuf", [128, 64], U16), "lb": ("sbuf", [128, 64], U16), "lc": ("sbuf", [128, 64], U16), "l0": ("sbuf", [128, 64], U16),
    "sc": ("sbuf", [128, NM], B16), "scf": ("sbuf", [128, 128], F32), "ra": ("sbuf", [128, 1536], F32), "rb": ("sbuf", [128, 1536], F32),
    "trs": ("sbuf", [128, NM], F32), "dvs": ("sbuf", [128, NM], F32), "dvt": ("sbuf", [128, NM - CUT3], F32),
    "ht": ("sbuf", [128, M], F32), "ho": ("sbuf", [128, M], F32), "rs": ("sbuf", [128, M], B16), "inv": ("sbuf", [128, WINV], F32),
    "iw": ("sbuf", [128, 64], I32), "iu": ("sbuf", [128, 24], I32), "id16": ("sbuf", [128, 16], I32),
    "cm": ("sbuf", [128, 32 * NTH], F32),
    "nbe": ("sbuf", [128, 48], I32), "nbl": ("sbuf", [128, 64], U16), "nbw": ("sbuf", [128, 64], U16), "lnb": ("sbuf", [128, 96], U16),
    "lnw": ("sbuf", [128, 96], U16),
    "sz8": ("sbuf", [128, 8], F32), "rot": ("sbuf", [128, 32], F32), "acc": ("sbuf", [128, 8], F32), "ypd": ("sbuf", [128, 32], F32),
    "szs": ("sbuf", [128, 32], F32), "hb": ("sbuf", [128, 4 * M], B16), "ys": ("sbuf", [128, M], F32),
}
SMALL = {
    "zf": (F32, {"d16": 16, "d17": 16, "cf": 32, "ri": 32, "mlt": 32, "rest": 32, "rest2": 64, "alp": 32, "one32": 32, "cn": 128, "sn": 16, "ki": 16, "s80": 8,
                 "nn": 128, "nm": 96, "n1": 128, "n2": 128, "n3": 128, "n4": 128,
                 "m1": 32, "mm": 32, "eq4": 128, "b4": 128, "b2": 64, "b1": 32, "tn": 32, "zz": 64, "zt": 64, "thr": 8, "t2": 8,
                 "ytr": 32, "col": 8, "a1": 32, "cs": 32, "f2": 32, "g1": 32, "ge": 64, "inc": 64, "hh": 64, "je": 64, "a2": 64, "a2t": 64,
                 "ug": 32, "ue": 32, "um": 32, "slot": 32, "sx": 32,
                 "rho": 64, "j2f": 8, "mx": 8, "mx1": 8, "xo": 8, "xm": 8}),
    "zi": (I32, {"ip": 16, "aci": 4}),
    "zu": (U16, {"cexp": 64, "crep": 64, "cu": 24, "twice": 4, "rotl": 2, "lro": 16, "sll": 16, "j1": 6, "j2": 6, "pl": 16, "kl": 16}),
}
AT = {}
for _b, (_d, _parts) in SMALL.items():
    _o = 0
    for _n, _w in _parts.items():
        AT[_n] = (_b, _o, _w)
        _o += -(-_w // 16) * 16
    SCRATCH[_b] = ("sbuf", [128, _o], _d)
for _t in range(R):
    SCRATCH["xh%d" % _t] = ("sbuf", [128, 32], F32)
    for _n in ("a", "b"):
        SCRATCH["q%s%d" % (_n, _t)] = ("sbuf", [128, 2 * K], C8)
        SCRATCH["s%s%d" % (_n, _t)] = ("sbuf", [128, 2 * K], U8)
    SCRATCH["qp%d" % _t] = ("sbuf", [128, M], C8)
    SCRATCH["sp%d" % _t] = ("sbuf", [128, M], U8)
for _t in range(R + 1):
    SCRATCH["qc%d" % _t] = ("sbuf", [128, 2 * M if _t < R else M], C8)
    SCRATCH["scp%d" % _t] = ("sbuf", [128, 2 * M if _t < R else M], U8)

SEMAPHORES = (["ev", "es", "et", "eg", "loc", "nbr"] + ["h%d" % t for t in range(R)]
              + ["%s%d" % (k, t) for t in range(R) for k in ("ac", "as", "bc", "bs")]
              + ["dx", "du", "dw", "dnb", "dswap", "dnum", "drot", "drt", "dout"])


def place(n):
    for n0, n1, c, s in RUNS:
        if n0 <= n < n1:
            return c + s * (n - n0)
    return WS


def rank_program(g, core, T, topo):
    rank = T.rank_of(core)
    if rank is None:
        return
    queue = {"v": g.vector, "s": g.scalar, "t": g.tensor, "g": g, "y": g.sync}
    esem = {"v": "ev", "s": "es", "t": "et", "g": "eg"}
    cnt, known, clock, hist = {}, {k: {} for k in queue}, {}, {}

    def V(name, a=0, b=None, step=1, p0=0, p1=128):
        buf, off, w = AT[name] if name in AT else (name, 0, SCRATCH[name][1][1])
        return (buf, off + a, off + (w if b is None else b), step, p0, p1)

    def A(r):
        return T[r[0]][r[4]:r[5], r[1]:r[2]] if r[3] == 1 else T[r[0]][r[4]:r[5], r[1]:r[2]:r[3]]

    def meets(a, b):
        if a[1] >= b[2] or b[1] >= a[2] or a[4] >= b[5] or b[4] >= a[5]:
            return False
        return not (a[3] == b[3] and a[3] > 1 and (a[1] - b[1]) % a[3])

    def grown(r):
        return (r[0], r[1] // 512 * 512, -(-r[2] // 512) * 512, 1, 0, 128)

    def split(reads, writes):
        ps = [r for r in list(reads) + list(writes) if SCRATCH[r[0]][0] == "psum"]
        return ([r for r in reads if SCRATCH[r[0]][0] != "psum"],
                [r for r in writes if SCRATCH[r[0]][0] != "psum"] + [grown(r) for r in ps])

    def use(qn, reads, writes):
        reads, writes = split(reads, writes)
        need = {}
        for r, w in [(r, False) for r in reads] + [(r, True) for r in writes]:
            for e, ew, sem, val in hist.get(r[0], []):
                if (w or ew) and meets(r, e) and known[qn].get(sem, 0) < val:
                    need[sem] = max(need.get(sem, 0), val)
        for sem in sorted(need):
            if any(o != sem and clock[(o, need[o])].get(sem, 0) >= need[sem] for o in need):
                continue
            queue[qn].wait_ge(T.sem[sem], need[sem])
        for sem in need:
            for s2, v2 in clock[(sem, need[sem])].items():
                known[qn][s2] = max(known[qn].get(s2, 0), v2)
            known[qn][sem] = max(known[qn].get(sem, 0), need[sem])

    def mark(sem, val, reads, writes):
        reads, writes = split(reads, writes)
        for r in writes:
            hist[r[0]] = [h for h in hist.get(r[0], [])
                          if not ((r[3] == 1 or h[0] == r) and r[1] <= h[0][1] and h[0][2] <= r[2] and r[4] <= h[0][4] and h[0][5] <= r[5])]
        for r, w in [(r, False) for r in reads] + [(r, True) for r in writes]:
            hist.setdefault(r[0], []).append((r, w, sem, val))

    def done(qn, inst, sem, n, reads, writes):
        cnt[sem] = cnt.get(sem, 0) + n
        inst.then_inc(T.sem[sem], n)
        clock[(sem, cnt[sem])] = dict(known[qn])
        mark(sem, cnt[sem], reads, writes)

    def emit(qn, fn, outs, ins):
        use(qn, ins, outs)
        if qn == "g" and known["g"].get("eg", 0) < cnt.get("eg", 0):
            g.wait_ge(T.sem.eg, cnt["eg"])
            known["g"]["eg"] = cnt["eg"]
        done(qn, fn(), esem[qn], 1, ins, outs)

    def dmas(sem, items):
        tot = cnt.get(sem, 0) + 16 * len(items)
        merged = {}
        for qn, out, in_, outs, ins in items:
            use(qn, ins, outs)
            queue[qn].dma_start(out, in_).then_inc(T.sem[sem], 16)
            for s, v in known[qn].items():
                merged[s] = max(merged.get(s, 0), v)
        cnt[sem] = tot
        clock[(sem, tot)] = merged
        for qn, out, in_, outs, ins in items:
            mark(sem, tot, ins, outs)

    def arrives(sem, n, writes):
        cnt[sem] = cnt.get(sem, 0) + n
        clock[(sem, cnt[sem])] = {}
        mark(sem, cnt[sem], [], writes)

    def ind(win, off):
        return A(win).indirect(A(off))

    def cp(out, in_, off=None):
        emit("v", lambda: g.vector.tensor_copy(A(out), A(in_) if off is None else ind(in_, off)), [out], [in_] + ([off] if off else []))

    def ts(out, in0, s1, op0, s2=None, op1=None, off=None):
        cols = [s for s in (s1, s2) if isinstance(s, tuple)]
        val = lambda s: A(s) if isinstance(s, tuple) else s
        src = lambda: A(in0) if off is None else ind(in0, off)
        if op1 is None:
            fn = lambda: g.vector.tensor_scalar(A(out), src(), val(s1), None, op0)
        else:
            fn = lambda: g.vector.tensor_scalar(A(out), src(), val(s1), val(s2), op0, op1)
        emit("v", fn, [out], [in0] + cols + ([off] if off else []))

    def tt(out, a, b, op, off=None):
        emit("v", lambda: g.vector.tensor_tensor(A(out), A(a) if off is None else ind(a, off), A(b), op), [out], [a, b] + ([off] if off else []))

    def red(out, in_, op):
        emit("v", lambda: g.vector.tensor_reduce(A(out), A(in_), AxisListType.X, op), [out], [in_])

    def scan(out, d0, d1, op0, op1):
        emit("v", lambda: g.vector.tensor_tensor_scan(A(out), A(d0), A(d1), 0.0, op0, op1), [out], [d0, d1])

    def tr(out, in_):
        emit("v", lambda: g.vector.transpose(A(out), A(in_)), [out], [in_])

    def fill(out, c):
        emit("v", lambda: g.vector.memset(A(out), c), [out], [])

    def act(out, in_, func=AF.Copy, off=None, accum=None, scale=None, **kw):
        src = lambda: A(in_) if off is None else ind(in_, off)
        cols = [scale] if isinstance(scale, tuple) else []
        def fn():
            k2 = dict(kw)
            if scale is not None:
                k2["scale"] = A(scale) if cols else scale
            if accum is not None:
                k2["accum_out"] = A(accum)
            return g.scalar.activation(A(out), src(), func, **k2)
        emit("s", fn, [out] + ([accum] if accum else []), [in_] + cols + ([off] if off else []))

    def iota(out, pattern, base, cm):
        if SCRATCH[out[0]][2] == I32:
            fn = lambda: g.iota(A(out), pattern, base, cm)
        else:
            fn = lambda: g.iota(A(out), pattern, base, cm, allow_small_or_imprecise_dtypes=True)
        emit("g", fn, [out], [])

    def select(out, in_, pattern, cmp, fillv, base, cm):
        emit("g", lambda: g.affine_select(A(out), A(in_), pattern, cmp, fillv, base, cm), [out], [in_])

    def quant(q, s, in_):
        emit("v", lambda: g.vector.quantize_mx(A(q), A(s), A(in_)), [q, s], [in_])

    def mm(out, lq, ls, rq, rs, start, stop):
        emit("t", lambda: g.tensor.matmul_mx(A(out), A(lq), A(ls), A(rq), A(rs), start, stop), [out], [lq, ls, rq, rs])

    def pick(qo, so, qi, si, off):
        emit("v", lambda: g.vector.tensor_copy(A(qo).bitcast(dt.uint32), A(qi).bitcast(dt.uint32).indirect(A(off))), [qo], [qi, off])
        act(so, si, off=off)

    others = [d for d in range(N) if d != rank]
    mask3 = 0xFFFF
    for d in others:
        mask3 &= topo.mask(core, T.cores[d])
    groups = bin(mask3).count("1")

    def spread(src, sem):
        use("g", [src], [])
        ids = [DstId(rid=topo.addr(T.cores[d])[0], pnc=topo.addr(T.cores[d])[1]) for d in others]
        g.remote_dma_fused([RemoteDMATransfer(dst_ids=ids, dma_engine_mask=mask3, remote_sem=T.sem[sem], srcs=[A(src)], dsts=[A(src) for d in others])],
                           local_sem=T.sem.loc)
        cnt["loc"] = cnt.get("loc", 0) + groups

    near = [d for d in others if topo.same_plane(topo.chip(core), topo.chip(T.cores[d]))][0]
    pair = sorted([rank, near])
    pair2 = [d for d in range(N) if d not in pair]
    far = pair2[pair.index(rank)]

    def swap(q, s, d, semc, sems):
        dst = T.cores[d]
        rid, pid = topo.addr(dst)[:2]
        mask, n = topo.mask(core, dst), len(topo.engines(core, dst))
        use("g", [V(q, 0, K)], [])
        g.remote_dma(A(V(q, K, 2 * K)).bitcast(dt.uint8), A(V(q, 0, K)).bitcast(dt.uint8), T.sem[semc], T.sem.loc, pid, rid, mask)
        use("g", [V(s, 0, K)], [])
        g.remote_dma(A(V(s, K, 2 * K)), A(V(s, 0, K)), T.sem[sems], T.sem.loc, pid, rid, mask)
        cnt["loc"] = cnt.get("loc", 0) + 2 * n
        arrives(semc, n, [V(q, K, 2 * K)])
        arrives(sems, n, [V(s, K, 2 * K)])

    def widen(x, c0, c1, on, to="xe"):
        out, win, off = V(to, 32 * c0, 32 * c1), V(x, c0, c1), V("cexp", 0, 2 * (c1 - c0))
        if on == "v":
            cp(out, win, off)
        else:
            act(out, win, off=off)

    def turn(f, c0, c1):
        tr(V(f, 32 * c0, 32 * c1), V("xe", 32 * c0, 32 * c1))

    def run(f, a, b):
        n0, n1, c, s = [r for r in RUNS if r[0] <= a and b <= r[1]][0]
        return V(f, c + s * (a - n0), c + s * (b - n0), s)

    def runs(a, b):
        return [(max(a, r[0]), min(b, r[1])) for r in RUNS if r[0] < b and a < r[1]]

    def turn_s(f, c0, c1):
        for a, b in runs(32 * c0, 32 * c1):
            tr(run(f, a, b), V("xb", a, b))

    CF = lambda k: V("cf", k, k + 1)
    SCL, HI, LO, SCOL, LCOL, BCOL, BETA, HCOL = [CF(k) for k in (0, 4, 11, 6, 7, 8, 3, 4)]

    def lift(f, a, b):
        for x, y in runs(a, b):
            scan(V("sc", x, y), V("d0", 0, y - x), run(f, x, y), ALU.mult, ALU.add)

    def listed(out, a, b):
        ts(out, V("sc", a + 15, b, 16), SCL, ALU.mult, MID, ALU.add)

    bank = lambda k, w: V("bl", 512 * k, 512 * k + w)

    loads = []
    for k in range(8):
        o = V("nbe", 0, 48 - 2 * (k % 2), 1, 16 * k, 16 * k + 16)
        loads.append(("ys"[k % 2], A(o), T.nb[:, 2 * (k % 2):48], [o], []))
    dmas("dnb", loads)
    dmas("dx", [("y", A(V("xt")), T.x[:], [V("xt")], [])])
    dmas("du", [("s", A(V("ut")), T.u[:], [V("ut")], [])])
    IP = lambda k: V("ip", k, k + 1)
    iota(V("iu"), [[1, 3], [0, 8]], 0, 0)
    iota(IP(0), [[0, 1]], 0, 1)
    iota(V("iw"), [[1, 32], [0, 2]], 0, 0)
    iota(V("id16"), [[1, 16]], 128, -1)
    iota(V("ri"), [[1, 32]], 0, 0)
    fill(V("one"), 1.0)
    cp(V("cu"), V("iu"))
    ts(IP(4), IP(0), 4, ALU.logical_shift_right, 1, ALU.bitwise_and)
    ts(IP(1), IP(0), 15, ALU.bitwise_and)
    ts(IP(2), IP(0), 31, ALU.bitwise_and)
    ts(IP(3), IP(0), 5, ALU.logical_shift_right)
    cp(V("cexp"), V("iw"))
    cp(CF(4), IP(4))
    cp(V("cf", 6, 9), V("ip", 1, 4))
    ts(V("id16"), V("id16"), 15, ALU.bitwise_and)
    ts(V("iw"), V("iw"), 0.0, ALU.mult)
    ts(SCL, SCOL, 15.0, ALU.is_equal, 1.0 - 1.0 / UP, ALU.mult)
    ts(V("d16"), V("id16"), 1.0, ALU.is_equal, UP, ALU.mult)
    ts(V("d17"), V("id16"), 0.0, ALU.is_gt)
    ts(V("crep"), V("iw"), SCOL, ALU.add)
    ts(SCL, SCL, 1.0 / UP, ALU.max)
    tt(V("d16"), V("d16"), V("d17"), ALU.add)
    cp(V("twice", 0, 2), V("crep", 0, 2))
    ts(V("twice", 2, 4), V("crep", 0, 2), 16.0, ALU.add)
    o = 16 * rank
    for e in (0, 1):
        cp(V("nbl", o + e, o + 12, 2, 0, 64), V("nbe", e, 24, 4, 0, 64))
        cp(V("nbl", o + e, o + 12, 2, 64, 128), V("nbe", 24 + e, 48, 4, 64, 128))
    cp(V("nbl", o + 12, o + 16), V("nbe", 0, 4))
    spread(V("nbl", o, o + 16), "nbr")
    arrives("nbr", groups * len(others), [V("nbl", 16 * d, 16 * d + 16) for d in others])
    quant(V("qu"), V("su"), V("ut"))
    pick(V("qr", 0, 128), V("sr", 0, 128), V("qu"), V("su"), V("cu", 0, 8))
    act(V("d0"), V("d16"), off=V("crep", 0, 32))

    def height(k, t, q, s, a, n):
        mm(bank(k, n), V("qr", 128 * t, 128 * t + 128), V("sr", 128 * t, 128 * t + 128), V(q, a, a + n), V(s, a, a + n), True, True)

    def share(t):
        spread(V("xh%d" % t, 8 * rank, 8 * rank + 8), "h%d" % t)
        arrives("h%d" % t, groups * len(others), [V("xh%d" % t, 8 * d, 8 * d + 8) for d in others])

    def own_f(t):
        widen("xh%d" % t, 8 * rank, 8 * rank + 8, "v")
        turn("fh", 8 * rank, 8 * rank + 8)

    def others_f(t):
        xh = "xh%d" % t
        widen(xh, 8 * others[1], 8 * others[1] + 8, "s")
        widen(xh, 8 * others[2], 8 * others[2] + 8, "s")
        widen(xh, 8 * others[0], 8 * others[0] + 8, "v")
        for d in others:
            turn("fh", 8 * d, 8 * d + 8)

    for h in (0, 1):
        quant(V("qc0", H * h, H * h + H), V("scp0", H * h, H * h + H), V("xt", 4 * H * h, 4 * H * h + 4 * H))
    for h in (0, 1):
        height(h, 0, "qc0", "scp0", H * h, H)
    for h in (0, 1):
        tr(V("ht", H * h, H * h + H), bank(h, H))
    cp(V("xh0", 8 * rank, 8 * rank + 8), V("ht", 0, M, 32))
    share(0)
    dmas("dw", [("y", A(V("wt")), T.w[:], [V("wt")], [])])

    iota(V("sn"), [[16, 16]], M * rank, 0)
    iota(V("ki"), [[16, 16]], 0, 0)
    iota(V("s80"), [[16, 8]], 0, 0)
    select(V("dg"), V("one"), [[1, 32], [-1, 32]], ALU.is_equal, 0.0, 0, 0)
    iota(V("io2"), [[1, M]], NM, 0)
    for n0, n1, c, s in RUNS:
        iota(V("idn", c, c + s * (n1 - n0), s), [[1, n1 - n0]], n0, 0)
    ts(CF(12), BCOL, -8.0, ALU.mult, LCOL, ALU.add)
    own_f(0)
    ts(CF(13), CF(12), 6.0, ALU.is_equal)
    ts(CF(14), CF(12), 7.0, ALU.is_equal, 2048.0, ALU.mult)
    for k in range(J):
        for e in (0, 1):
            a = 32 * k + 8 * rank
            cp(V("lnb", a + e, a + 8, 2), V("nbe", 16 * k + e, 16 * k + 16, 4))
    tt(CF(15), CF(13), CF(14), ALU.add)
    ts(BETA, LCOL, float(NTS), ALU.is_lt, NM / 2.0, ALU.mult)
    fill(V("one32"), 1.0)
    fill(V("wb", NM, NM + 16), 0.0)
    ts(IP(6), IP(2), 7, ALU.bitwise_and)
    ts(IP(7), IP(1), 3, ALU.logical_shift_right)
    ts(IP(8), IP(1), 7, ALU.bitwise_and)
    ts(V("alp"), V("one32"), BETA, ALU.mult, -1.0 / NM, ALU.mult)
    ts(CF(9), IP(6), 32.0, ALU.mult, float(BIGR), ALU.add)
    tt(IP(9), IP(3), IP(7), ALU.subtract)
    cp(CF(20), IP(8))
    ts(V("alp"), V("alp"), 1.0, ALU.add)
    ts(IP(10), IP(9), 4.0, ALU.add)
    ts(IP(11), IP(9), 2.0, ALU.add)
    ts(V("sn"), V("sn"), SCOL, ALU.add)
    ts(V("ip", 12, 14), V("ip", 10, 12), 3, ALU.bitwise_and)
    ts(LO, HI, -1.0, ALU.mult, 1.0, ALU.add)
    ts(V("rotl"), V("ip", 12, 14), 8.0, ALU.mult, CF(20), ALU.add)
    fill(V("ypd"), 0.0)
    for h in (0, 1):
        n0 = M * rank + H * h
        step = place(n0 + 1) - place(n0)
        ts(V("sn", 8 * h, 8 * h + 8), V("sn", 8 * h, 8 * h + 8), float(step), ALU.mult, float(place(n0) - step * n0), ALU.add)
    ts(V("nn", 96, 128), V("ri"), 32.0, ALU.mult, LCOL, ALU.add)

    def coded(a, b):
        n1, n2, n3, n4, cn = [V(x, a, b) for x in ("n1", "n2", "n3", "n4", "cn")]
        act(n3, V("nn", a, b), AF.Identity, scale=-4.0, bias=TOP + NM / 2)
        ts(n1, V("nn", a, b), 896.0, ALU.min, 128.0, ALU.max)
        ts(n2, V("nn", a, b), 768.0, ALU.min, 256.0, ALU.max)
        act(n4, n1, scale=2.0)
        tt(n2, n2, n3, ALU.add)
        tt(cn, n2, n4, ALU.add)

    coded(96, 128)

    dmas("dswap", [("y", A(V("nbw", p0=0, p1=64)), A(V("nbl", p0=64, p1=128)), [V("nbw", p0=0, p1=64)], [V("nbl", p0=64, p1=128)]),
                   ("y", A(V("nbw", p0=64, p1=128)), A(V("nbl", p0=0, p1=64)), [V("nbw", p0=64, p1=128)], [V("nbl", p0=0, p1=64)])])
    first, second = ((0, 0, 8), (32, 8, 4)), ((36, 0, 4), (64, 4, 8))

    def lists(src, a, b):
        for d in others:
            for p, parts in ((a, first), (b, second)):
                for to, at, n in parts:
                    cp(V("lnb", to + 8 * d, to + 8 * d + n, 1, p, p + 64), V(src, 16 * d + at, 16 * d + at + n, 1, p, p + 64))

    lists("nbl", 0, 64)
    others_f(0)
    lists("nbw", 64, 0)
    swaps = []
    for k in range(8):
        i = k ^ 1
        w, r = V("lnw", 0, 96, 1, 16 * k, 16 * k + 16), V("lnb", 0, 96, 1, 16 * i, 16 * i + 16)
        swaps.append(("y", A(w), A(r), [w], [r]))
    dmas("dnum", swaps)

    cuts = ((384, 896), (896, 1280), (1280, 1536))

    def around(win, mid):
        for a, b in cuts:
            act(V("ra", a, b), win, off=V("lnb", a // 16, b // 16))
        cp(V("ra", 0, 384), win, V("lnb", 0, 24))
        for a, b in ((0, 384),) + cuts[:2]:
            tr(V("rb", a, b), V("ra", a, b))
        mid()
        tr(V("rb", *cuts[2]), V("ra", *cuts[2]))

    win3 = ["fa", "fb", "fc"]
    lst3 = ["la", "lb", "lc"]
    lo = M * rank
    COL = lambda k: V("col", k, k + 1)
    ACC = lambda k: V("acc", k, k + 1)
    for t in range(R):
        xh, qc, sp = "xh%d" % t, "qc%d" % t, "scp%d" % t
        if t:
            own_f(t)
            others_f(t)
        nbh = [V("rb", 512 * k, 512 * k + 512, 16) for k in range(J)] + [V(xh)]

        def mid():
            tt(V("m1"), nbh[0], nbh[1], ALU.max)
            tt(V("m1"), V("m1"), nbh[3], ALU.max)

        around(V("fh"), mid)
        if not t:
            act(V("dw"), V("dg"), scale=CF(15))
            ts(V("nn", 0, 96, 2), V("lnb", 0, 96, 2), LO, ALU.mult)
            ts(V("nn", 1, 96, 2), V("lnb", 1, 96, 2), HI, ALU.mult)
            ts(V("nm", 0, 96, 2), V("lnw", 1, 96, 2), HI, ALU.mult)
            ts(V("nm", 1, 96, 2), V("lnw", 0, 96, 2), LO, ALU.mult)
            tt(V("nn", 0, 96), V("nn", 0, 96), V("nm"), ALU.add)
            coded(0, 96)
        tt(V("mm"), V("m1"), nbh[2], ALU.max)
        for k in range(J + 1):
            tt(V("eq4", 32 * k, 32 * k + 32), nbh[k], V("mm"), ALU.is_equal)
        tt(V("b4"), V("eq4"), V("cn"), ALU.mult)
        tt(V("b2"), V("b4", 0, 64), V("b4", 64, 128), ALU.max)
        tt(V("b1"), V("b2", 0, 32), V("b2", 32, 64), ALU.max)
        wide = lambda a, b: (V("xb", 32 * a, 32 * b), V("b1"), V("cexp", 2 * a, 2 * b))
        for a, b in ((0, 8), (8, 16), (16, 24)):
            out, win, off = wide(a, b)
            act(out, win, AF.Identity, off=off, scale=-1.0, bias=TOP)
        tr(V("tn"), V("b1"))
        out, win, off = wide(24, 32)
        ts(out, win, -1.0, ALU.mult, TOP, ALU.add, off)
        cp(V("zz"), V("tn"), V("twice"))
        turn_s("fa", 24, 32)
        tr(V("zt"), V("zz"))
        turn_s("fa", 0, 8)
        for e in (0, 1):
            ts(V("la", e, 64, 2), V("zt", 32 * e, 32 * e + 32), -1.0, ALU.mult, TOP + MID, ALU.add)
        if not t:
            tr(V("wb", 0, NM), V("dw"))
        turn_s("fa", 8, 16)
        turn_s("fa", 16, 24)
        if not t:
            for i in range(4):
                for n0, n1, c, s in RUNS:
                    select(V("w%d" % i, c, c + s * (n1 - n0), s), V("wb", n0 + 6 - 2 * i, n1 + 6 - 2 * i), [[0, n1 - n0]], ALU.is_gt, 0.0, 1, 0)
            for b in range(4):
                select(V("et", 512 * b, 512 * b + 512), V("one", 0, 512), [[1, 512]], ALU.is_equal, 0.0, -b, -4)
        for k in range(10):
            fi, fo, li = win3[k % 3], win3[(k + 1) % 3], lst3[k % 3]
            lw = lst3[(k + 1) % 3] if k < 9 else "l0"
            a, b = SPART[0]
            act(run(fo, a, b), V(fi), off=V(li, a // 16, b // 16))
            for j, (a, b) in enumerate(VPART):
                cp(run(fo, a, b), V(fi), V(li, a // 16, b // 16))
                if k and not j:
                    listed(V(li, SCUT // 16, 64), SCUT, NM)
            for a, b in SPART[1:]:
                act(run(fo, a, b), V(fi), off=V(li, a // 16, b // 16))
            for a, b in VPART + SPART[:1]:
                lift(fo, a, b)
            listed(V(lw, 0, SCUT // 16), 0, SCUT)
            for a, b in SPART[1:]:
                lift(fo, a, b)
        act(V("trs", 0, SCUT), V("w0"), off=V("l0", 0, SCUT // 16), accum=ACC(0))
        listed(V("l0", SCUT // 16, 64), SCUT, NM)
        act(V("trs", 0, NM - SCUT), V("w0"), off=V("l0", SCUT // 16, 64), accum=ACC(4))
        act(V("trs"), V("w1"), off=V("l0"), accum=ACC(1))
        act(V("trs", 0, CUT3), V("w2"), off=V("l0", 0, CUT3 // 16), accum=ACC(2))
        cp(V("dvs"), V("w3"), V("l0"))
        cp(V("dvt"), V("w2"), V("l0", CUT3 // 16, 64))
        red(ACC(3), V("dvs"), ALU.add)
        red(ACC(6), V("dvt"), ALU.add)
        tt(V("acc", 0, 4, 2), V("acc", 0, 4, 2), V("acc", 4, 8, 2), ALU.add)
        ts(V("aci"), V("acc", 0, 4), 1.0 / 2048.0, ALU.mult, -0.499, ALU.add)
        ts(V("t2", 0, 4), V("aci"), -2048.0, ALU.mult)
        cp(V("sz8", 1, 8, 2), V("aci"))
        tt(V("sz8", 0, 8, 2), V("t2", 0, 4), V("acc", 0, 4), ALU.add)
        moves = []
        for i in (1, 2, 3):
            c = 32 * i
            for qn, d0, d1, s0, s1 in (("y", c, 128, 0, 128 - c), ("s", 0, c, 128 - c, 128)):
                o, s = V("rot", 8 * i, 8 * i + 8, 1, d0, d1), V("sz8", 0, 8, 1, s0, s1)
                moves.append((qn, A(o), A(s), [o], [s]))
        dmas("drot", moves)
        cp(V("rot", 0, 8), V("sz8"))
        listed(V("lro"), lo, lo + M)
        listed(V("rho", 0, 16), lo, lo + M)
        act(V("rtf"), V("idn"), off=V("lro"))
        row = V("rtf", 0, M, 1, 0, 1)
        dmas("drt", [("y", T.rt[0:1, M * t:M * t + M], A(row), [], [row])])
        tt(V("rho", 16, 32), V("rho", 0, 16), V("sn"), ALU.not_equal)
        fill(V("inv", 0, 96), 0.0)
        far_in = [float(d in pair2) for d in range(N)]
        terms = [(ALU.is_lt, M, far_in[0] * K)] + [(ALU.is_ge, M * d, (far_in[d] - (far_in[d - 1] if d > 1 else 0.0)) * K) for d in range(1, N)]
        terms = [(op, float(place(n)), v) for op, n, v in terms if v]
        parts = ("m1", "mm")
        for j, (op, n, v) in enumerate(terms):
            ts(V("rho", 32, 48) if not j else V(parts[j % 2], 0, 16), V("rho", 0, 16), n, op, v, ALU.mult)
            if j:
                tt(V("rho", 32, 48), V("rho", 32, 48), V(parts[j % 2], 0, 16), ALU.add)
        if not t:
            ts(V("rest"), V("ri"), CF(9), ALU.add)
            ts(V("mlt"), V("ri"), LCOL, ALU.is_gt)
            cp(V("rest2"), V("rest"), V("twice"))
            ts(V("s80"), V("s80"), SCOL, ALU.add)
            ts(V("ki"), V("ki"), SCOL, ALU.add)
        for j in range(NTS):
            act(V("trs", 32 * j, 32 * j + 32), V("rot"), AF.Sign, bias=-1.5 - j, accum=V("ypd", j, j + 1))
        act(V("szs"), V("rot"), AF.Identity, off=V("rotl"), scale=2.0, bias=-34.0)
        for j in range(NTS, NTH):
            ts(V("cm", 32 * j, 32 * j + 32), V("rot"), float(j + 2), ALU.is_ge)
        for j in range(NTS, NTH):
            red(V("ypd", j, j + 1), V("cm", 32 * j, 32 * j + 32), ALU.add)
        tr(V("ytr"), V("ypd"))
        red(COL(0), V("ytr"), ALU.add)
        ts(V("a1"), V("alp"), COL(0), ALU.mult, BETA, ALU.add)
        tr(V("cs"), V("a1"))
        act(V("trs", 0, 32), V("cs"), AF.Sign, bias=0.5 - K, accum=V("thr", 0, 1))
        ts(V("f2"), V("cs"), float(K), ALU.is_ge, 2048.0, ALU.mult)
        gt, eq, thr = V("ge", 0, 32), V("ge", 32, 64), V("thr", 0, 1)
        ts(gt, V("szs"), thr, ALU.is_gt)
        ts(eq, V("szs"), thr, ALU.is_equal)
        tt(V("g1"), V("cs"), V("f2"), ALU.subtract)
        scan(V("inc", 0, 32), V("one32"), gt, ALU.mult, ALU.add)
        scan(V("inc", 32, 64), V("one32"), eq, ALU.mult, ALU.add)
        red(COL(2), V("g1"), ALU.max)
        ts(V("a2", 0, 32), V("mlt"), V("inc", 31, 32), ALU.mult)
        ts(V("a2", 32, 64), V("mlt"), V("inc", 63, 64), ALU.mult)
        ts(V("hh"), V("ge"), -BIG - 1.0, ALU.mult, BIG, ALU.add)
        tr(V("a2t"), V("a2"))
        tt(V("je"), V("inc"), V("hh"), ALU.add)
        red(COL(3), V("a2t", 0, 32), ALU.add)
        red(COL(5), V("a2t", 32, 64), ALU.add)
        ts(V("ug"), V("je", 0, 32), COL(3), ALU.add)
        ts(V("ue"), V("je", 32, 64), COL(5), ALU.add, COL(2), ALU.add)
        tt(V("um"), V("ug"), V("ue"), ALU.min)
        tt(V("zz"), V("um"), V("rest2"), ALU.min, V("twice"))
        tr(V("zt"), V("zz"))
        tt(V("slot"), V("um"), V("rest"), ALU.min)
        for e in (0, 1):
            cp(V("sll", e, 16, 2), V("zt", 32 * e + 8 * rank, 32 * e + 8 * rank + 8))
        tr(V("sx"), V("slot"))
        emit("v", lambda: g.vector.tensor_copy(ind(V("inv"), V("sll")), A(V("io2"))), [V("inv")], [V("io2"), V("sll")])
        widen("sx", 0, 16, "s", "xb")
        scan(V("scf", 0, K), V("d0", 0, K), V("inv", 0, K), ALU.mult, ALU.add)
        k5 = V("scf", 15, K, 16)
        ts(V("j1", 0, 5), k5, SCL, ALU.mult, float(-NM), ALU.add)
        qa, sa, qb, sb = "qa%d" % t, "sa%d" % t, "qb%d" % t, "sb%d" % t
        pick(V(qa, 0, K), V(sa, 0, K), V(qc, 0, M), V(sp, 0, M), V("j1", 0, 5))
        widen("sx", 16, 32, "s", "xb")
        swap(qa, sa, near, "ac%d" % t, "as%d" % t)
        ts(V("j2f", 0, 5), k5, SCL, ALU.mult, NM - 0.5, ALU.is_lt)
        turn_s("fs", 0, 16)
        ts(V("j2f", 0, 5), V("j2f", 0, 5), float(K), ALU.mult)
        tt(V("j2f", 0, 5), V("j2f", 0, 5), V("s80", 0, 5), ALU.add)
        turn_s("fs", 16, 32)
        cp(V("j2", 0, 5), V("j2f", 0, 5))
        cp(V("rs"), V("fs"), V("lro"))
        scan(V("sc", 0, M), V("d0", 0, M), V("rs"), ALU.mult, ALU.add)
        so, me = V("rho", 0, 16), V("rho", 16, 32)
        ts(so, V("sc", 15, M, 16), SCL, ALU.mult)
        ts(V("rho", 48, 64), so, K - 0.5, ALU.is_lt)
        tt(me, me, V("rho", 48, 64), ALU.mult)
        tt(so, so, me, ALU.mult)
        tt(V("rho", 32, 48), V("rho", 32, 48), so, ALU.add)
        cp(V("pl"), V("rho", 32, 48))
        pick(V(qb, 0, K), V(sb, 0, K), V(qa), V(sa), V("j2", 0, 5))
        swap(qb, sb, far, "bc%d" % t, "bs%d" % t)
        ts(V("rho", 48, 64), me, float(M), ALU.mult)
        tt(V("rho", 48, 64), V("rho", 48, 64), V("ki"), ALU.add)
        cp(V("kl"), V("rho", 48, 64))
        if not t:
            pick(V("qr", 128, 384), V("sr", 128, 384), V("qu"), V("su"), V("cu", 8, 24))
            quant(V("qe"), V("se"), V("et"))
            quant(V("qw"), V("sw"), V("wt"))
        if t + 1 < R:
            height(7, t + 1, qc, sp, 0, M)
            tr(V("ho"), bank(7, M))
            m0, m1 = V("rho", 16, 32, 2), V("rho", 17, 32, 2)
            tt(V("mx"), m1, m0, ALU.subtract)
            ts(V("mx"), V("mx"), HCOL, ALU.mult)
            tt(V("mx"), V("mx"), m0, ALU.add)
            ts(V("mx1"), V("mx"), -1.0, ALU.mult, 1.0, ALU.add)
            tt(V("xo"), V("ho", 0, M, 32), V("mx1"), ALU.mult)
        unpack = [(V("qe", 128 * b, 128 * b + 128), V("se", 128 * b, 128 * b + 128)) for b in range(4)]
        half = [(H * h, H * h + H) for h in (0, 1)]
        qp, pp = "qp%d" % t, "sp%d" % t
        for h in (0, 1):
            for b in range(4):
                mm(bank(4 * h + b, H), *unpack[b], V(qc, *half[h]), V(sp, *half[h]), True, False)
        for h in (0, 1):
            pick(V(qp, *half[h]), V(pp, *half[h]), V(qb), V(sb), V("pl", 8 * h, 8 * h + 8))
        for h in (0, 1):
            for b in range(4):
                mm(bank(4 * h + b, H), *unpack[b], V(qp, *half[h]), V(pp, *half[h]), False, True)
        for h in (0, 1):
            for b in range(4):
                src, out = bank(4 * h + b, H), V("hb", 4 * H * h + b, 4 * H * h + 4 * H, 4)
                if b % 2:
                    act(out, src, scale=0.5)
                else:
                    ts(out, src, 0.5, ALU.mult)
            quant(V(qc, M + H * h, M + H * h + H), V(sp, M + H * h, M + H * h + H), V("hb", 4 * H * h, 4 * H * h + 4 * H))
            if t + 1 < R:
                height(h, t + 1, qc, sp, M + H * h, H)
        nq, ns = "qc%d" % (t + 1), "scp%d" % (t + 1)
        if t + 1 < R:
            for h in (0, 1):
                tr(V("ht", *half[h]), bank(h, H))
            tt(V("xm"), V("ht", 0, M, 32), V("mx"), ALU.mult)
            tt(V("xh%d" % (t + 1), 8 * rank, 8 * rank + 8), V("xm"), V("xo"), ALU.add)
            share(t + 1)
            pick(V(nq, 0, M), V(ns, 0, M), V(qc), V(sp), V("kl"))

    outs = []
    for h in (0, 1):
        pick(V(nq, *half[h]), V(ns, *half[h]), V(qc, 0, M + H * h + H), V(sp, 0, M + H * h + H), V("kl", 8 * h, 8 * h + 8))
        mm(bank(h, H), V("qw"), V("sw"), V(nq, *half[h]), V(ns, *half[h]), True, True)
        cp(V("ys", *half[h]), bank(h, H))
        outs.append(("y", T.oc[:, 4 * H * h:4 * H * h + 4 * H], A(V(nq, *half[h])).bitcast(dt.uint8), [], [V(nq, *half[h])]))
        outs.append(("s" if h else "y", T.y[:, H * h:H * h + H], A(V("ys", *half[h])), [], [V("ys", *half[h])]))
    for k in range(4):
        o = V(ns, 0, M, 1, 32 * k, 32 * k + 4)
        outs.append(("y", T.osc[4 * k:4 * k + 4, 0:M], A(o), [], [o]))
    dmas("dout", outs)
    for sem in sorted(cnt):
        g.sync.wait_ge(T.sem[sem], cnt[sem])
